import numpy as np, ml_dtypes
CORES = [9,25,41,57]
N = 4
BF = ml_dtypes.bfloat16
L, W, RO, LX, M = 256, 4096, 4, 4, 16
KS = np.arange(16, dtype=np.int32)[:, None]
def places(c, u, a):
    return (((c * (2 * u + 1)) >> 5) + c + a) & (W - 1)
def pick(x, at):
    return np.take_along_axis(x, at.reshape(N, 8, 1, 16 * L), 3).reshape(N, 8, 16, 16, L)
def score(p):
    before = np.add.accumulate(p, axis=3) - p; e = np.add.reduce((16 - KS) * p, axis=3)
    return e, e[:, :, :, None] + KS * p - before
def plain(rng):
    return (rng.integers(0, 16, (N, 8, 16, W), dtype=np.int32), rng.integers(0, 4096, (N, 8, 16, L), dtype=np.int32), rng.integers(0, 64, (N, 8, 16, L), dtype=np.int32),
            rng.integers(0, 64, (N, 8, 16, 1), dtype=np.int32), rng.integers(45, 90, (N, 8, L), dtype=np.int32))
def stress(rng, mid):
    sh = (N, 8, 16, RO, L); kd = rng.integers(0, 3, (N, 8, 1, RO, L))
    near = mid + 18 * rng.standard_normal((N, 8, 1, RO, L)) + 12 * rng.standard_normal(sh)
    far = np.where(rng.random(sh) < 0.55, 200 + 56 * rng.random(sh), 40 * rng.random(sh))
    return np.clip(np.floor(np.where(kd == 0, near, np.where(kd == 1, 256 * rng.random(sh), far))), 0, 255).astype(np.int32)
def low(a):
    return np.asarray(a, np.float32).astype(BF)
def pack(x, c, s, y, wt, th):
    return {"x0": low(x.reshape(N, 128, W)), "c0": np.ascontiguousarray(c.reshape(N, 128, L)).astype(np.int32), "st": low(s.reshape(N, 128, RO * L)),
            "y0": low(y.reshape(N, 128, L)), "w": low(wt.reshape(N, 128, 1)), "th": low(th)}
def setup_inputs(rng):
    x, c, y, wt, th = plain(rng)
    return pack(x, c, stress(rng, 122), y, wt, th)
def setup_inputs_spread(rng):
    x, c, y, wt, th = plain(rng)
    x = np.minimum(np.floor(np.exp2(4 * rng.random((N, 8, 1, W), dtype=np.float32)) * rng.random((N, 8, 16, W), dtype=np.float32)), 15).astype(np.int32)
    c = np.floor(4096 * rng.random(c.shape) ** 3).astype(np.int32); y = np.floor(64 * rng.random(y.shape) ** 3).astype(np.int32)
    wt = np.floor(64 * rng.random(wt.shape) ** 2).astype(np.int32); th = np.floor(241 * rng.random(th.shape) ** 2).astype(np.int32)
    return pack(x, c, stress(rng, 15 + 40 * rng.random((N, 8, 1, 1, L))), y, wt, th)
def setup_inputs_ends(rng):
    sh = (N, 8, 16, RO, L); fz = (np.arange(N)[:, None] + np.arange(8)) & 1
    x = 15 * (rng.random((N, 8, 16, W), dtype=np.float32) < 0.5 * rng.integers(0, 3, (N, 8, 1, W))).astype(np.int32)
    c = 4095 * (rng.random((N, 8, 16, L)) < 0.5 * rng.integers(0, 3, (N, 8, 1, L))).astype(np.int32)
    y = 63 * (rng.random((N, 8, 16, L)) < 0.5 * rng.integers(0, 3, (N, 8, 1, L))).astype(np.int32)
    wt = 63 * (rng.random((N, 8, 16, 1)) < 0.6).astype(np.int32); wt[:, 7] = 63; wt[:, 0, 0] = 0; wt[:, :, 15] = 63
    th = 240 * rng.integers(0, 2, (N, 8, L))
    s = 255 * (rng.random(sh) < rng.choice(np.array([0.0, 0.45, 0.5, 0.55, 1.0]), (N, 8, 1, RO, L))).astype(np.int32)
    live = np.argsort(rng.random((N, 8, 1, L)), axis=-1) < 5 * L // 16; live[..., L - 4:] = False
    c = np.where(live, rng.integers(0, 4096, c.shape), c); s = np.where(live[:, :, :, None], stress(rng, 127), s)
    x[..., 0] = 15 * (1 - fz)[:, :, None]
    for u in (0, 1921): x[..., places(4095, u, 0)] = 15 * fz[:, :, None]
    x[..., 2:16] = 15; x[..., places(15, 1921, 0)] = 15
    full, none = 4095 * fz, 4095 * (1 - fz)
    y[..., L - 1] = 63; c[..., L - 1] = 0; s[:, :, :, 0, L - 1] = 255
    y[..., L - 4:L - 1] = 0; y[:, :, 15, L - 3] = 63
    for l in (L - 3, L - 2):
        c[..., l] = none[:, :, None]; c[:, :, 14, l] = full; c[:, :, 15, l] = 15; s[:, :, :, 0, l] = 30
    c[..., L - 4] = full[:, :, None]; c[:, :, 0, L - 4] = none; c[:, :, 2:, L - 4] = np.arange(2, 16); s[:, :, :, 0, L - 4] = 226
    return pack(x, c, s, y, wt, th)
def setup_inputs_corners(rng):
    x, c, y, wt, th = plain(rng); s = stress(rng, 150); n = np.arange(4096)
    typ = rng.integers(0, 4, (N, W)); p0 = int(places(4075, 2046, 0)); typ[:, p0] = 1; typ[:, (p0 + 1) & (W - 1)] = 0
    tb = typ[:, None, None, :]
    x = np.where(tb == 0, 0, np.where(tb == 1, 15, np.where(tb == 2, 13 + x % 3, x))).astype(np.int32)
    wt[:, :, 0] = 63; wt[:, :, 1] = 1; par = np.arange(L) & 1
    kd = np.stack([rng.permutation(L) % 8 for g in range(8)]); iu = rng.integers(0, 5, (8, L))
    top = (kd == 0) & (par == 1); fold = (kd == 0) & ((np.arange(L) & 3) == 0)
    iu = np.where(top, 3, np.where(fold, 2, iu)); ctl = (kd > 0) | top | fold
    y = np.where(ctl[:, None, :], 0, y); y[:, :, 0] = np.where(ctl, np.array([0, 0, 32, 32, 32])[iu], y[:, :, 0]); y[:, :, 1] = np.where(ctl, np.array([0, 1, 30, 31, 32])[iu], y[:, :, 1])
    c = np.where(top[:, None, :], 4095 - rng.integers(0, 3, c.shape), c)
    c = np.where(fold[:, None, :] & (rng.random(c.shape) < 0.5), 4075, c)
    th = rng.choice(np.array([0, 1, 60, 239, 240]), (N, 8, L)); th = np.where(kd == 7, rng.choice(np.array([0, 239]), (N, 8, L)), th)
    kb = kd[:, None, :]; a = rng.integers(8, 15, (8, 1, L)); b = np.minimum(15, a + 1 + rng.integers(0, 7, (8, 1, L))); z = np.zeros((8, 16, L), np.int64)
    want = np.select([kb == 1, (kb == 2) | (kb == 3), (kb == 4) | (kb == 7), kb == 5, kb == 6], [z + ((KS == a) | (KS == b)), z + (KS == b), z, z + 2, z + np.where(par == 1, KS > 0, True)], z - 1)
    eight = (7 * KS + np.arange(L)) % 16
    two = z + np.where((eight == 0) & (par == 1) & (b > a + 1), (225 + 15 * (16 - a)) >> 3, 30)
    s0 = np.select([kb == 1, kb == 2, kb == 3, kb == 4, kb == 5, kb == 6, kb == 7],
                   [two, z + 30 + (eight == 0) * par, z + 31, z + np.where(eight < 8 + par, 0, 255), 254 + rng.integers(0, 2, (8, 16, L)), z + np.where(par == 1, 226, 255), z + np.where(eight < 8, 0, 255)], z - 1)
    s[:, :, :, 0] = np.where(s0 < 0, s[:, :, :, 0], s0)
    us = np.array([0, 1, 2046, 2047, 0])
    for q in range(N):
        for i in range(5):
            kind = typ[q][places(n, us[i], 0)]
            for v in range(3):
                ix = np.flatnonzero(kind == v); ix = ix if len(ix) else n
                m = (iu == i)[:, None, :] & (want == v); c[q][m] = ix[rng.integers(0, len(ix), int(np.count_nonzero(m)))]
    for q in range(1, N, 2):
        s[q, :, :, 0] = np.where(kb == 7, 0, s[q, :, :, 0])
        for g, l in zip(*np.nonzero(kd == 7)):
            e = int(c[q - 1, g, 1, l]); kind = typ[q][(((n * e) >> 5) + n + 37 * e) & (W - 1)]; pos = (0, 14, 15, 16)[int(rng.integers(0, 4))]
            i0 = np.flatnonzero(kind == 0); i1 = np.flatnonzero(kind == 1); i0 = i0 if len(i0) else n; i1 = i1 if len(i1) else n
            zero = np.arange(16) >= pos; zero = zero & ((np.arange(16) == pos) | (rng.random(16) < 0.5))
            c[q, g, :, l] = np.where(zero, i0[rng.integers(0, len(i0), 16)], i1[rng.integers(0, len(i1), 16)])
    return pack(x, c, s, y, wt, th)
def setup_inputs_crowd(rng):
    x, c, y, wt, th = plain(rng); x = np.minimum(x, 14); s = stress(rng, 115)
    for q in range(N):
        for t in range(RO):
            kk = (q + t) % 4; g = (q + 3 * t + 7) % 8; l = (L - 1, 0)[t & 1]
            if kk < 2: s[q, :, :, t] = 255
            if kk == 1: s[q, g, :, t, l] = 0
            if kk == 3: s[q, :, :, t] = 0
            if kk == 3 and t != 1: s[q, g, :, t, l] = 255
    one = rng.integers(0, 4096, 8); one[2] = 4095; one[4] = 0
    for g in range(6):
        if g & 1: c[:, g, :, :L - 1] = one[g]
        else: c[:, g] = one[g]
    y[:, :4] = y[:, :4, :, :1].copy()
    th = np.where(rng.random(th.shape) < 0.5, th, 240 * rng.integers(0, 2, th.shape))
    return pack(x, c, s, y, wt, th)
def setup_inputs_ties(rng):
    x, c, y, wt, th = plain(rng); few = rng.integers(0, 16, (N, 8, 16, 40), dtype=np.int32); few[:, 1::2] = 8 * rng.integers(0, 2, (N, 4, 16, 40))
    x = np.ascontiguousarray(np.take_along_axis(few, rng.integers(0, 40, (N, 8, 1, W)), 3))
    c[:, 3] = rng.choice(np.array([0, 1, 2048, 4094, 4095]), (N, 16, L))
    u = np.add.reduce(wt * y, axis=2) & 2047; e, ek = score(pick(x, places(c, u[:, :, None], 0)))
    at = np.take_along_axis(ek, rng.integers(0, 16, (N, 8, 1, 1, L)), 3)[:, :, :, 0]
    s = stress(rng, 110); s[:, :, :, 0] = np.clip((at >> 3) + rng.integers(0, 2, (N, 8, 1, L)) * (rng.random(at.shape) < 0.4), 0, 255)
    th = rng.choice(np.array([0, 48, 56, 64]), (N, 8, L))
    return pack(x, c, s, y, wt, th)
def check_inputs(d):
    bad = []
    for k, hi in (("x0", 15), ("c0", 4095), ("st", 255), ("y0", 63), ("w", 63), ("th", 240)):
        v = np.asarray(d[k]).astype(np.float64)
        if not (np.min(v) >= 0 and np.max(v) <= hi): bad.append("range of " + k)
        elif np.any(v != np.floor(v)): bad.append("whole numbers in " + k)
    return bad
def reference(x0, c0, st, y0, w, th):
    x = x0.astype(np.int32).reshape(N, 8, 16, W); c = c0.astype(np.int32).reshape(N, 8, 16, L); y = y0.astype(np.int32).reshape(N, 8, 16, L)
    s = 8 * st.astype(np.int32).reshape(N, 8, 16, RO, L); wt = w.astype(np.int32).reshape(N, 8, 16, 1); bound = th.astype(np.int32)[:, :, None]
    a = np.zeros((N, 1, 1, 1), np.int64)
    for t in range(RO):
        u = (np.add.reduce(wt * y, axis=2) & 2047)[:, :, None]
        p = pick(x, places(c, u, a)); e, ek = score(p)
        g = np.add.reduce((ek >= s[:, :, :, t][:, :, :, None]).astype(np.int32), axis=2)
        best = 1 + np.argmax(g[:, :, 1:], axis=2)[:, :, None]
        g0 = g[:, :, :1]; gb = np.take_along_axis(g, best, 2)
        rest = g0 >= 9; move = ~rest & (gb > g0); go = ~rest & ~move
        name = np.take_along_axis(c, best, 2); v = np.take_along_axis(p, best[:, :, :, None], 3)[:, :, :, 0]
        fresh = (((name * u) >> 5) + u) & 4095
        down = np.concatenate([name, c[:, :, :15]], axis=2); up = np.concatenate([c[:, :, 1:], fresh], axis=2)
        c = np.where(move, np.where((KS <= best) | ((u & 1) == 1), down, c), np.where(go & (KS >= best), up, c))
        src = (np.arange(N) - 1 - t % (N - 1)) % N; ce, cv, come = name[src], v[src], go[src]
        h = (((c * ce) >> 5) + c + 37 * ce) & (W - 1)
        hit = np.add.reduce(np.abs(pick(x, h) - cv[:, :, :, None]), axis=2) <= bound
        pos = np.where(np.any(hit, axis=2), 1 + np.argmax(hit, axis=2), 0)[:, :, None]
        put = np.where(KS < pos, c, np.where(KS == pos, ce, np.concatenate([c[:, :, :1], c[:, :, :15]], axis=2)))
        c = np.where(come, put, c)
        y = e >> 5; a = np.add.reduce(go.reshape(N, -1).astype(np.int64), axis=1).reshape(N, 1, 1, 1)
        if t < LX:
            col = np.broadcast_to(M * np.arange(L) + (u & (M - 1)), (N, 8, 16, L))
            np.put_along_axis(x, col, ((np.take_along_axis(x, col, 3) + (e >> 7)) >> 1).astype(np.int32), 3)
    return {"yx": x.reshape(N, 128, W).astype(np.float32).astype(BF), "yc": c.reshape(N, 128, L).astype(np.float32), "yy": y.reshape(N, 128, L).astype(np.float32).astype(BF)}

@@ -1,0 +1,769 @@
+import math
+from concourse.mybir import AluOpType, ActivationFunctionType
+
+NR, RO = 4, 4
+BF, F16, F32, I32, U16 = "bfloat16", "float16", "float32", "int32", "uint16"
+MATS = ["dk", "BM", "Id", "nI", "I4", "Im2048", "Im32", "I64", "I2080", "I3232", "Lo", "Cm", "Mdl", "Md", "Mu", "Moh",
+        "Mst", "Sd", "SdI", "SuI", "R0", "R15", "Mco", "Wb", "tA", "tB", "tC", "tD", "tE", "tF", "c192", "I8", "nBM", "Mk", "nSdI"]
+SCRATCH = {m: ("sbuf", [128, 128], BF) for m in MATS}
+SCRATCH.update({
+    "Zs": ("sbuf", [128, 144], BF), "Sel": ("sbuf", [128, 2048], BF), "EX8": ("sbuf", [128, 128], BF),
+    "ImSd": ("sbuf", [128, 128], F32), "Rall": ("sbuf", [128, 128], F32), "c2050": ("sbuf", [128, 128], F16),
+    "cm192": ("sbuf", [128, 256], BF), "col": ("sbuf", [128, 32], F32), "coli": ("sbuf", [128, 8], I32),
+    "wcol": ("sbuf", [128, 8], BF), "basev": ("sbuf", [128, 8], BF), "basex": ("sbuf", [128, 16], F32),
+    "c0s": ("sbuf", [128, 256], I32), "y0s": ("sbuf", [128, 256], BF), "sts": ("sbuf", [128, 1024], BF),
+    "stT": ("sbuf", [128, 2048], BF), "ths": ("sbuf", [128, 256], BF),
+    "X0": ("sbuf", [128, 4096], BF), "X1": ("sbuf", [128, 4096], BF), "X2": ("sbuf", [128, 4096], BF),
+    "X3": ("sbuf", [128, 4096], BF), "X4": ("sbuf", [128, 4096], BF),
+    "B2": ("sbuf", [128, 8], BF), "vl": ("sbuf", [128, 128], U16), "xa": ("sbuf", [128, 4160], BF), "vg": ("sbuf", [128, 512], BF), "xT": ("sbuf", [128, 4096], BF),
+    "ind": ("sbuf", [128, 4096], BF), "xb": ("sbuf", [128, 4096], BF), "ad": ("sbuf", [128, 4096], BF),
+    "Cc": ("sbuf", [128, 256], F16), "C3": ("sbuf", [128, 256], F16), "Ct": ("sbuf", [128, 256], F16),
+    "yb": ("sbuf", [128, 256], BF), "hib": ("sbuf", [128, 256], BF), "mm": ("sbuf", [128, 256], F32),
+    "qq": ("sbuf", [128, 256], F32), "u16": ("sbuf", [128, 512], F16), "ob": ("sbuf", [128, 512], F16),
+    "pi": ("sbuf", [128, 256], I32), "pj": ("sbuf", [128, 256], I32), "pf": ("sbuf", [128, 256], F32),
+    "fi": ("sbuf", [128, 256], I32), "fj": ("sbuf", [128, 256], I32), "fr": ("sbuf", [128, 256], F16),
+    "off1": ("sbuf", [128, 256], U16), "off2": ("sbuf", [128, 256], U16), "offv": ("sbuf", [128, 16], U16),
+    "offx": ("sbuf", [128, 16], U16), "xi": ("sbuf", [128, 16], I32), "xj": ("sbuf", [128, 16], I32),
+    "xk": ("sbuf", [128, 16], F32), "Xo": ("sbuf", [128, 256], BF), "xn": ("sbuf", [128, 256], BF),
+    "km": ("sbuf", [128, 256], BF), "Za": ("sbuf", [128, 256], F16), "Zb": ("sbuf", [128, 256], F16), "lk": ("sbuf", [128, 256], BF), "ww": ("sbuf", [128, 256], BF), "ss": ("sbuf", [128, 256], BF),
+    "se": ("sbuf", [128, 256], F16), "dm": ("sbuf", [128, 256], BF), "hit": ("sbuf", [128, 256], BF),
+    "stay": ("sbuf", [128, 256], BF), "Z4": ("sbuf", [128, 256], F32), "acc": ("sbuf", [128, 16], F32),
+    "es": ("sbuf", [128, 1024], F16), "er": ("sbuf", [128, 1024], F16),
+    "vs": ("sbuf", [128, 3072], BF), "vr": ("sbuf", [128, 3072], BF),
+    "yco": ("sbuf", [128, 256], F32), "yyo": ("sbuf", [128, 256], BF),
+    "pT0": ("psum", [128, 1024], BF), "pT1": ("psum", [128, 1024], BF),
+    "pD0": ("psum", [128, 512], F32), "pD1": ("psum", [128, 512], F32),
+    "pa0": ("psum", [128, 512], F32), "pb0": ("psum", [128, 512], F32),
+    "pa1": ("psum", [128, 512], F32), "pb1": ("psum", [128, 512], F32),
+})
+DMAS = ["w", "y0", "c0", "x0", "st0", "st1", "th", "x1", "x2", "x3", "x4", "oyx", "oyc0", "oyc1", "oyc2", "oyc3", "oyy"]
+SEMAPHORES = (["qP", "qD", "qA", "qG", "sent"] + ["d" + n for n in DMAS]
+              + ["a%s%d%d" % (k, t, h) for k in "ev" for t in range(RO) for h in range(4)])
+
+OPT = {"kvm": True, "z16": True, "stag": 4000.0, "lam": 0.3, "lean": 100.0, "win": 120.0, "maxp": 0, "ns": 2, "lkg": True, "lkd": True, "tg": 1, "split": 2, "seeds": [],
+       "flex": True, "lag": 1, "each": False}
+NUDGES = [2008, 2012, 2013, 2017, 2018, 2020, 2040, 2048, 2066, 2070, 2082, 2109, 2113, 2141, 2146, 2147, 2212, 2223, 2227, 2235, 2366,
+          2378, 2454, 2670, 2704, 2797, 2895, 3011, 3096, 3197, 3340, 3345, 3389, 3497, 3528, 3533, 3570, 3610, 3639]
+WEIGH = [2.0, 1.0, 1.0, 0.5]
+PICK = {}
+COSTS = [(1.0, 0.5, 1.56, 3.8, 60.0, 90.0, 3000.0, 10.0), (0.85, 0.43, 1.1, 2.0, 40.0, 50.0, 2200.0, 0.0),
+         (1.2, 0.6, 2.0, 5.5, 70.0, 150.0, 4500.0, 10.0), (1.0, 0.85, 1.56, 3.8, 60.0, 90.0, 3000.0, 0.0)]
+MEMO = {}
+
+
+def build(g, T, topo, core, costs):
+    CY, PE, GA, SC, FIX, LAT, REM, MF = costs
+    NS, TG, SPL, LAG = OPT["ns"], OPT["tg"], OPT["split"], OPT["lag"]
+    H = 256 // NS
+    MAXP = [[OPT["maxp"] >> h & 1 for h in range(NS)] for t in range(RO)]
+    NP, XW = H // 32, 16 * H + 16
+    rank = T.rank_of(core)
+    A, AF = AluOpType, ActivationFunctionType
+    V, S, PEq, SY = g.vector, g.scalar, g.tensor, g.sync
+    ops, last_w, readers, cur = [], {}, {}, [0]
+
+    def add(eng, fns, cost, rd, wr, banks=(), sem=None, after=(), inc=1):
+        i = len(ops)
+        deps = set(after)
+        for k in rd:
+            if k in last_w:
+                deps.add(last_w[k])
+        for k in wr:
+            if k in last_w:
+                deps.add(last_w[k])
+            deps.update(readers.get(k, ()))
+        for k in rd:
+            readers.setdefault(k, []).append(i)
+        for k in wr:
+            last_w[k] = i
+            readers[k] = []
+        deps.discard(i)
+        ops.append({"alt": {eng: (fns, cost)}, "deps": deps, "banks": tuple(banks), "sem": sem, "inc": inc, "wr": wr, "half": cur[0]})
+        return i
+
+    def also(i, eng, fn, n, rate=1.0):
+        if OPT["flex"]:
+            ops[i]["alt"][eng] = ([fn], FIX + max(64, n * rate) * CY)
+        return i
+
+    def lin(out, in_, n, rd, wr, bias, scale):
+        i = act(out, in_, AF.Identity, n, rd, wr, bias, scale)
+        return also(i, "D", lambda: V.tensor_scalar(out, in_, scale, bias, A.mult, A.add), n)
+
+    def step(out, in_, n, rd, wr, bias, scale):
+        i = act(out, in_, AF.Sigmoid, n, rd, wr, bias, scale)
+        if isinstance(bias, float):
+            also(i, "D", lambda: V.tensor_scalar(out, in_, -bias / scale, None, A.is_gt if scale > 0 else A.is_lt), n)
+        return i
+
+    def bk(keys):
+        return sorted(set(k[0] for k in keys if k[0][0] == "p" and k[0][1] in "TDab" and len(k[0]) == 3))
+
+    def vec(fn, n, rd, wr, rate=1.0):
+        return add("D", [fn], FIX + max(64, n * rate) * CY, rd, wr, bk(rd + wr))
+
+    def act(out, in_, func, n, rd, wr, bias=0.0, scale=1.0, rate=1.0, acc=None):
+        return add("A", [lambda: S.activation(out, in_, func, bias=bias, scale=scale, accum_out=acc)],
+                   FIX + max(64, n * rate) * CY, rd, wr, bk(rd + wr))
+
+    def ts(out, in0, s1, s2, op0, op1, n, rd, wr, rate=1.0):
+        if s2 is None:
+            return vec(lambda: V.tensor_scalar(out, in0, s1, None, op0), n, rd, wr, rate)
+        return vec(lambda: V.tensor_scalar(out, in0, s1, s2, op0, op1), n, rd, wr, rate)
+
+    def tt(out, a, b, op, n, rd, wr, rate=1.0):
+        return vec(lambda: V.tensor_tensor(out, a, b, op), n, rd, wr, rate)
+
+    def cp(out, in_, n, rd, wr, rate=1.0):
+        return vec(lambda: V.tensor_copy(out, in_), n, rd, wr, rate)
+
+    def ms(ap, val, n, wr):
+        return vec(lambda: V.memset(ap, val), n, [], wr, 0.5)
+
+    def mmf(out, l, r, a, b):
+        return lambda: PEq.matmul(out, l, r, a, b)
+
+    def mm(items, rd, wr):
+        return add("P", [mmf(*it[:5]) for it in items], sum(it[5] * PE + MF for it in items) + 40, rd, wr, bk(rd + wr))
+
+    def grp(out, pairs, rd, wr, n=H):
+        k = len(pairs)
+        return mm([(out, p[0], p[1], i == 0, i == k - 1, max(64, n) * (p[2] if len(p) > 2 else 1))
+                   for i, p in enumerate(pairs)], rd, wr)
+
+    def dma(q, name, out, in_, cost, rd, wr, after=()):
+        qq = SY if q == "S" else S
+        return add(q, [lambda: qq.dma_start(out, in_)], cost, rd, wr, (), "d" + name, after, 16)
+
+    def gp(fn, n, rd, wr):
+        return add("G", [fn], 170 + 2 * n * CY, rd, wr)
+
+    def K(name, *a):
+        return (name,) + a
+
+    def M(name):
+        return T[name][:]
+
+    def col(j):
+        return T.col[:, j:j + 1]
+
+    XK = [[K("X%d" % t)] for t in range(5)]
+    i = dma("S", "w", T.wcol[:, 0:1], T.w[:], 2000, [], [K("wcol")])
+    dma("S", "y0", T.y0s[:], T.y0[:], 2200, [], [K("y0s")])
+    dma("S", "c0", T.c0s[:], T.c0[:], 2400, [], [K("c0s")])
+    i = dma("S", "x0", T.X0[:], T.x0[:], 6300, [], XK[0])
+    dma("S", "st0", T.sts[:, 0:256], T.st[:, 0:256], 6500, [], [K("sts", 0)])
+    dma("S", "st1", T.sts[:, 256:1024], T.st[:, 256:1024], 3000, [], [K("sts", 1)], [i])
+    dma("S", "th", T.ths[0:8, :], T.th[:], 2500, [], [K("ths")], [i])
+
+    gp(lambda: g.iota(T.coli[:, 0:1], [[0, 1]], 0, 1), 1, [], [K("coli", 0)])
+    gp(lambda: g.iota(M("tA"), [[1, 128]], 0, -1, allow_small_or_imprecise_dtypes=True), 128, [], [K("tA")])
+    gp(lambda: g.affine_select(M("tB"), M("tA"), [[-16, 8], [0, 16]], A.is_ge, -100.0, 0, 1), 128, [K("tA")], [K("tB")])
+    gp(lambda: g.affine_select(M("dk"), M("tB"), [[16, 8], [0, 16]], A.is_ge, -100.0, 15, -1), 128, [K("tB")], [K("dk")])
+    gp(lambda: g.iota(T.basex[:], [[256, 16]], 0, 0, allow_small_or_imprecise_dtypes=True), 16, [], [K("basex")])
+    ms(T.Sel[:], -8.0, 2048, [K("Sel")])
+    gp(lambda: g.affine_select(T.Sel[:], T.Sel[:], [[1, 128], [0, 16]], A.is_equal, 0.0, 0, -1), 2048, [K("Sel")], [K("Sel")])
+    ms(T.EX8[0:8, :], -1.0, 128, [K("EX8")])
+    gp(lambda: g.affine_select(T.EX8[0:8, :], T.EX8[0:8, :], [[1, 8], [0, 16]], A.is_equal, 0.0, 0, -1), 128, [K("EX8")], [K("EX8")])
+    ms(T.c192[:, 0:8], 192.0, 8, [K("c192")])
+    ms(T.cm192[:], -192.0, 256, [K("cm192")])
+    ms(T.Zs[:], 0.0, 144, [K("Zs")])
+    for h in range(NS):
+        ms(T.xa[:, h * XW + 16 * H:(h + 1) * XW], 0.0, 16, [K("xa", h, "pad")])
+    if H < 128:
+        ms(T.vg[:], 0.0, 512, [K("vg", h) for h in range(NS)])
+    ts(M("c2050"), T.cm192[:, 0:128], 0.0, 2050.0, A.mult, A.add, 128, [K("cm192")], [K("c2050")], 0.5)
+    KP, E0, E15, MID, C16, CD0, CT1, CV1, CT2, CV2, CM4, CM8, COH, CSG, CDM, CUM, CHT, CCO, C32, NG1, CQ, TM, TM2, B16, CH, CM, CU, CO, TM3 = range(29)
+    ts(T.coli[:, 2:3], T.coli[:, 0:1], 15, None, A.bitwise_and, None, 1, [K("coli", 0)], [K("coli", 2)])
+    cp(col(KP), T.coli[:, 2:3], 1, [K("coli", 2)], [K("col", KP)])
+
+    def c1(j, src, s1, s2, o0, o1, extra=()):
+        ts(col(j), col(src), s1, s2, o0, o1, 1, [K("col", src)] + [K("col", e) for e in extra], [K("col", j)])
+
+    def ca(j, src, scale, bias, func=None, extra=()):
+        lin(col(j), col(src), 1, [K("col", src)] + [K("col", e) for e in extra], [K("col", j)], bias, scale)
+
+    CE = math.log(32.0)
+    c1(E0, KP, 0.0, None, A.is_equal, None)
+    c1(E15, KP, 15.0, None, A.is_equal, None)
+    c1(TM, E0, col(E15), None, A.add, None, [E15])
+    ca(C16, KP, -1.0, 16.0)
+    ca(CD0, E0, -21.0, 1.0)
+    ca(NG1, E0, 1.0, -1.0)
+    ca(CT1, TM, -50.0, 0.0)
+    ca(CT2, TM, -50.0, -0.5)
+    ca(CM4, TM, -4096.0, 4096.0)
+    ca(CM8, TM, -8192.0, 8192.0)
+    ca(CV2, TM, -33.0, 1.0)
+    ca(CV1, E15, 64.0, col(CV2), None, [CV2])
+    ca(CSG, E15, -math.exp(CE * (8.5 - 16) - 10), 0.0)
+    ca(CHT, E15, 262144.0, 128.0 - 131072.0)
+    ca(CCO, E15, -512.0, 0.0)
+    ca(C32, E15, 32.0, 0.0)
+    ca(B16, KP, 16.0, 0.0)
+    c1(MID, KP, 14.0, -4096.0, A.min, A.mult)
+    c1(COH, E0, -8192.0, col(MID), A.mult, A.add, [MID])
+    c1(TM2, KP, 1.0, -128.0, A.max, A.mult)
+    ca(CDM, TM2, 1.0, -128.0 * (62 - 65600))
+    ca(TM3, KP, 128.0, -128.0 * 65)
+    ca(CUM, E15, 128.0, col(TM3), None, [TM3])
+    ms(col(CQ), -8388608.0, 1, [K("col", CQ)])
+    ts(T.basev[:], T.basex[:, 0:8], col(B16), 16.0, A.add, A.add, 8, [K("basex"), K("col", B16)], [K("basev")])
+    ts(T.basex[:], T.basex[:], col(B16), None, A.add, None, 16, [K("basex"), K("col", B16)], [K("basex")])
+
+    def mat(name, s1, o0, s2=1.0, cols=(), src="dk", o1=None):
+        ts(M(name), M(src), s1, s2, o0, o1 or A.mult, 128, [K(src)] + [K("col", c) for c in cols], [K(name)], 0.5)
+
+    def mat2(name, a, b, op):
+        tt(M(name), M(a), M(b), op, 128, [K(a), K(b)], [K(name)], 2.0)
+
+    mat("BM", -50.0, A.is_gt)
+    ts(M("Wb"), M("dk"), -50.0, T.wcol[:, 0:1], A.is_gt, A.mult, 128, [K("dk"), K("wcol")], [K("Wb")], 0.5)
+    pw, kw = T.pb1[:, 0:1], K("pb1", 0)
+    grp(pw, [(M("Wb"), T.c192[:, 0:1])], [K("Wb"), K("c192")], [kw], 1)
+    for j, sc, bi in ((CH, -1.0 / 2048, 191.5 + 2.0 ** -12), (CM, -2.0, 786465.0), (CU, -1.0, 393216.0), (CO, -0.5, 197632.75)):
+        lin(col(j), pw, 1, [kw], [K("col", j)], bi, sc)
+    for nm, v in (("Id", 1.0), ("Im2048", -2048.0), ("nI", -1.0), ("I4", 4.0), ("I8", 8.0), ("Im32", -32.0), ("I64", 64.0), ("I2080", 2080.0), ("I3232", 3232.0)):
+        mat(nm, 0.0, A.is_equal, v)
+    mat("Lo", 0.0, A.is_gt)
+    mat("tA", -50.0, A.is_gt, col(C16), [C16])
+    mat("tB", 0.0, A.is_equal, col(KP), [KP])
+    mat2("tA", "tA", "tB", A.add)
+    mat2("Cm", "tA", "Lo", A.subtract)
+    BO8 = T.BM[:, 0::16]
+    cp(T.Zs[:, 15:143:16], BO8, 8, [K("BM")], [K("Zs")])
+    mat("tC", -50.0, A.is_gt, col(NG1), [NG1])
+    mat("tD", 0.0, A.is_equal, 16.0)
+    mat2("Mdl", "tC", "tD", A.add)
+    ts(T.Mdl[:, 0::16], BO8, col(CD0), None, A.mult, None, 8, [K("BM"), K("col", CD0)], [K("Mdl")])
+    ts(T.Mdl[:, 15::16], BO8, col(E0), None, A.mult, None, 8, [K("BM"), K("col", E0)], [K("Mdl")])
+    mat("Md", col(CT1), A.is_gt, col(CV1), [CT1, CV1])
+    mat("Mu", col(CT2), A.is_gt, col(CV2), [CT2, CV2])
+    mat("tE", -0.5, A.is_gt, col(CM4), [CM4])
+    mat("tF", 0.0, A.is_gt, col(CM8), [CM8])
+    mat2("Moh", "tE", "tF", A.subtract)
+    if any(any(r) for r in MAXP):
+        mat("nBM", -50.0, A.is_gt, -1.0)
+        ts(T.B2[:], BO8, 2.0, None, A.mult, None, 8, [K("BM")], [K("B2")])
+        gp(lambda: g.iota(T.pj[:, 0:128], [[1, 128]], 0, 0), 128, [], [K("pj", 0)])
+        cp(T.vl[:], T.pj[:, 0:128], 128, [K("pj", 0)], [K("vl")])
+    if OPT["kvm"]:
+        gp(lambda: g.iota(M("Mk"), [[0, 8], [1, 16]], 0, 0, allow_small_or_imprecise_dtypes=True), 128, [], [K("Mk")])
+        mat("Mk", col(KP), A.is_equal, 1.0, [KP], "Mk")
+    mat("Sd", 1.0, A.is_equal)
+    mat2("SdI", "Sd", "Id", A.subtract)
+    mat("tA", -1.0, A.is_equal)
+    mat2("SuI", "tA", "Id", A.subtract)
+    mat("R0", 0.0, A.is_equal, col(E0), [E0])
+    mat("R15", 0.0, A.is_equal, col(E15), [E15])
+    mat("Rall", -200.0, A.is_gt, col(C32), [C32])
+    mat("tB", 0.0, A.is_gt, -17.0)
+    mat2("Mst", "tB", "BM", A.add)
+    mat("nSdI" if OPT["z16"] else "ImSd", -1.0, A.mult, 1.0, (), "SdI")
+    mat("Mco", -50.0, A.is_gt, col(CCO), [CCO])
+    ts(T.Mco[:, 15::16], T.Mco[:, 15::16], -1.0, None, A.mult, None, 8, [K("Mco")], [K("Mco")])
+
+    def OH(j):
+        return T.Zs[:, 15 - j:143 - j]
+
+    nT = [0]
+
+    def flip(srcs, dst, rows, rd, wr):
+        n = 128 * len(srcs)
+        kb = K("loan", len(ops))
+        p = add("P", [(lambda c: lambda: PEq.transpose(T[PICK[p]][0:rows, c * 128:(c + 1) * 128], srcs[c], M("Id")))(c) for c in range(len(srcs))],
+                len(srcs) * (128 * PE + MF) + 40, rd + [K("Id")], [kb])
+        i = vec(lambda: V.tensor_copy(dst, T[PICK[p]][0:rows, 0:n]), n, [kb], wr, 0.5)
+        also(i, "A", lambda: S.activation(dst, T[PICK[p]][0:rows, 0:n], AF.Copy), n)
+        ops[p]["take"], ops[i]["give"] = ("pT0", "pT1"), p
+
+    def wide(items, rd, out, func, bias, scale, wr):
+        kb = K("loan", len(ops))
+        p = add("P", [(lambda it: lambda: PEq.matmul(T[PICK[p]][:, it[0]:it[1]], *it[2:]))(it) for it in items],
+                sum((it[1] - it[0]) * PE + MF for it in items) + 40, rd, [kb])
+        i = add("A", [lambda: S.activation(out, T[PICK[p]][:, :], func, bias=bias, scale=scale)], FIX + 512 * CY, [kb], wr)
+        if func == AF.Sigmoid:
+            also(i, "D", lambda: V.tensor_scalar(out, T[PICK[p]][:, :], -bias / scale, None, A.is_gt), 512)
+        ops[p]["take"], ops[i]["give"] = ("pD0", "pD1"), p
+
+    def stflip(t):
+        flip([T.sts[:, t * 256 + h * H:t * 256 + (h + 1) * H] for h in range(NS)], T.stT[0:H, t * NS * 128:(t + 1) * NS * 128], H,
+             [K("sts", min(t, 1))], [K("stT", t)])
+
+    def hs(name, h, off=0):
+        return T[name][:, off + h * H:off + (h + 1) * H]
+
+    def slot(h, s, a=0, b=None, st=1):
+        nm = ["pa0", "pb0", "pa1", "pb1"][(h * 8 + s) * H // 512]
+        o = (h * 8 + s) * H % 512
+        return T[nm][:, o + a:o + (H if b is None else b):st], K(nm, o)
+
+    def uphase(t, h):
+        o = (t % 2) * 256
+        us, kus = slot(h, 5)
+        u, ku = slot(h, 6)
+        pr = [(M("Wb"), hs("yb", h))]
+        rd = [K("Wb"), K("yb", h)]
+        grp(us, pr, rd, [kus])
+        lin(hs("hib", h), us, H, [kus, K("col", CH)], [K("hib", h)], col(CH), 1.0 / 2048)
+        grp(u, pr + [(M("Im2048"), hs("hib", h))], rd + [K("Im2048"), K("hib", h)], [ku])
+        lin(hs("mm", h), u, H, [ku, K("col", CM)], [K("mm", h)], col(CM), 2.0)
+        ts(hs("u16", h, o), u, col(CU), None, A.add, None, H, [ku, K("col", CU)], [K("u16", t % 2, h)])
+        ts(hs("ob", h, o), u, 0.5, col(CO), A.mult, A.add, H, [ku, K("col", CO)], [K("ob", t % 2, h)])
+
+    def qphase(h):
+        lin(hs("qq", h), hs("mm", h), H, [K("mm", h), K("col", CQ)], [K("qq", h)], col(CQ), 2048.0)
+
+    def point(h, off):
+        ts(hs("pj", h), hs("pi", h), 5, 4095, A.arith_shift_right, A.bitwise_and, H, [K("pi", h)], [K("pj", h)])
+        cp(hs(off, h), hs("pj", h), H, [K("pj", h)], [K(off, h)])
+
+    def gather(out, win, offs, n, rd, wr):
+        i = vec(lambda: V.tensor_copy(out, win.indirect(offs)), n, rd, wr, GA)
+        return also(i, "A", lambda: S.activation(out, win.indirect(offs), AF.Copy), n, GA)
+
+    def reduce16(h, s, name, lk, extra, xrd):
+        out, ko = slot(h, s)
+        o = h * 16 * H
+        if not lk:
+            n = H // SPL
+            for b in range(SPL):
+                grp(slot(h, s, b * n, (b + 1) * n)[0],
+                    extra(b * n, (b + 1) * n) + [(OH(k), T[name][:, o + b * n * 16 + k:o + (b + 1) * n * 16:16]) for k in range(16)],
+                    [K(name, h, j) for j in range(b * NP // SPL, (b + 1) * NP // SPL)] + xrd + [K("Zs")], [ko], n)
+            return
+        mm([(slot(h, s, k, H, 16)[0], T[name][:, o + k:o + 16 * H:16], BO8, True, True, 64) for k in range(16)],
+           [K(name, h, j) for j in range(NP)] + [K("BM")], [ko])
+        lin(hs("lk", h), out, H, [ko], [K("lk", h)], 0.0, 1.0)
+        grp(out, extra(0, H) + [(hs("lk", h), M("Id"))], xrd + [K("lk", h), K("Id")], [ko])
+
+    def step12(t, h):
+        nn, kn = slot(h, 7)
+        E, kE = slot(h, 4)
+        tt(E, nn, hs("mm", h), A.mult, H, [kn, K("mm", h)], [kE])
+        tt(hs("pi", h), E, hs("qq", h), A.add, H, [kE, K("qq", h)], [K("pi", h)])
+        point(h, "off1")
+        xo = h * XW
+        X = T["X%d" % t]
+        for j in range(NP):
+            gather(T.xa[:, xo + j * 512:xo + (j + 1) * 512], X[:, 0:4096], T.off1[:, h * H + j * 32:h * H + (j + 1) * 32], 512,
+                   XK[t] + [K("off1", h)], [K("xa", h, j)])
+        so = (t * NS + h) * 128
+        for b in range(NP // TG):
+            o = h * 16 * H + b * TG * 512
+            flip([T.xa[:, xo + c * 128:xo + (c + 1) * 128] for c in range(4 * TG * b, 4 * TG * (b + 1))], T.xT[:, o:o + TG * 512], 128,
+                 [K("xa", h, j) for j in range(b * TG, (b + 1) * TG)], [K("xT", h, b)])
+            for j in range(b * TG, (b + 1) * TG):
+                o = h * 16 * H + j * 512
+                its = [(0, 512, T.stT[0:H, so:so + 128], T.Sel[0:H, j * 512:(j + 1) * 512], True, False)]
+                its += [(c * 128, (c + 1) * 128, T.xT[:, o + c * 128:o + (c + 1) * 128], M("Cm"), False, c == 3) for c in range(4)]
+                wide(its, [K("stT", t), K("Sel"), K("xT", h, b), K("Cm")], T.ind[:, o:o + 512], AF.Sigmoid, 128.0, 256.0, [K("ind", h, j)])
+        for b in range(NP // TG):
+            o = h * 16 * H
+            mm([(slot(h, 4, c * 8, c * 8 + 8)[0], T.xT[:, o + c * 128:o + (c + 1) * 128], T.Cm[:, 0::16], True, True, 64)
+                for c in range(4 * TG * b, 4 * TG * (b + 1))], [K("xT", h, b), K("Cm")], [kE])
+        reduce16(h, 0, "ind", OPT["lkg"], lambda a, b: [], [])
+        lin(hs("yb", h), E, H, [kE], [K("yb", h)], 191.5 + 1.0 / 64, 1.0 / 32)
+
+    def send(name, src, dst, ksrc, t, h):
+        to = T.cores[(rank + 1 + t % 3) % NR]
+        rid, pid = topo.addr(to)[:2]
+        mk = topo.mask(core, to)
+        n = len(topo.engines(core, to))
+        sem = "a%s%d%d" % (name, t, h)
+        i = add("G", [lambda: g.remote_dma(dst, src, T.sem[sem], T.sem.sent, pid, rid, mk)], 300, ksrc, [], (), "sent", (), n)
+        add("R", [], REM, [], [K(name + "r", t, h)], (), sem, [i], n)
+
+    def step3(t, h):
+        o = (t % 2) * 256
+        ku16, kob = K("u16", t % 2, h), K("ob", t % 2, h)
+        (a0, k0), (a1, k1), (a2, k2), (a3, k3) = [slot(h, s) for s in range(4)]
+        kC = K("Cc", h)
+        C = hs("Cc", h)
+        act(hs("ww", h), a0, AF.Sigmoid, H, [k0], [K("ww", h)], -16 * CE - 10, CE)
+        grp(a1, [(M("Mdl"), hs("ww", h))], [K("Mdl"), K("ww", h)], [k1])
+        act(hs("ss", h), a1, AF.Sign, H, [k1, K("col", CSG)], [K("ss", h)], col(CSG))
+        s, ks = hs("ss", h), K("ss", h)
+        grp(a0, [(M("Id"), C), (M("Moh"), s)], [K("Id"), kC, K("Moh"), ks], [k0])
+        ts(hs("se", h), a0, col(COH), -2048.0, A.add, A.max, H, [k0, K("col", COH)], [K("se", h)])
+        grp(a3, [(M("Mu"), s)], [K("Mu"), ks], [k3])
+        grp(a2, [(M("Im32"), hs("u16", h, o)), (M("I64"), hs("ob", h, o)), (M("Md"), s)], [K("Im32"), K("I64"), K("Md"), ku16, kob, ks], [k2])
+        grp(a1, [(M("BM"), T.c2050[:, 0:H]), (M("BM"), hs("se", h))], [K("BM"), K("c2050"), K("se", h)], [k1])
+        e, ke = hs("es", NS * t + h), K("es", t, h)
+        ts(e, a1, -2080.0, None, A.add, None, H, [k1], [ke])
+        send("e", e, hs("er", NS * t + h), [ke], t, h)
+        vo = (NS * t + h) * (128 + H)
+        um, kum = T.vs[:, vo + 128:vo + 128 + H], K("um", t, h)
+        act(um, a3, AF.Sigmoid, H, [k3, K("col", CUM)], [kum, K("acc", h)], col(CUM), 128.0, 1.0, T.acc[:, 4 * h:4 * h + 1])
+        act(hs("dm", h), a2, AF.Sigmoid, H, [k2, K("col", CDM)], [K("dm", h)], col(CDM), -128.0)
+        q = H // 16
+        kv = slot(h, 0, 0, q)[0]
+        if OPT["kvm"]:
+            grp(a0, [(um, M("BM"))], [kum, K("BM")], [k0])
+            tt(hs("km", h), a0, M("Mk"), A.mult, H, [k0, K("Mk")], [K("km", h)])
+            grp(kv, [(M("nI"), T.basev[:, 0:q]), (hs("km", h), BO8)], [K("nI"), K("basev"), K("km", h), K("BM")], [k0], q)
+        else:
+            grp(kv, [(M("nI"), T.basev[:, 0:q])] + [(OH(j), T.vs[:, vo + 128 + j:vo + 128 + H:16]) for j in range(16)],
+                [K("nI"), K("basev"), K("Zs"), kum], [k0], q)
+        ts(T.offv[:, q * h:q * h + q], kv, -1.0, None, A.mult, None, q, [k0], [K("offv", h)])
+        mx = MAXP[t][h]
+        gather(T.vs[:, vo:vo + H] if mx else T.vg[:, h * 128:h * 128 + H], T.xa[:, h * XW:(h + 1) * XW], T.offv[:, q * h:q * h + q], H,
+               [K("xa", h, j) for j in list(range(NP)) + ["pad"]] + [K("offv", h)], [K("v", t, h) if mx else K("vg", h)])
+        if not mx:
+            flip([T.vg[:, h * 128:(h + 1) * 128]], T.vs[:, vo:vo + 128], 128, [K("vg", h)], [K("v", t, h)])
+        send("v", T.vs[:, vo:vo + 128 + H], T.vr[:, vo:vo + 128 + H], [K("v", t, h), kum], t, h)
+        tt(hs("fi", h), a1, hs("u16", h, o), A.mult, H, [k1, ku16], [K("fi", h)])
+        ts(hs("fj", h), hs("fi", h), 5, 4095, A.arith_shift_right, A.bitwise_and, H, [K("fi", h)], [K("fj", h)])
+        ts(hs("fr", h), hs("fj", h), -2048.0, None, A.add, None, H, [K("fj", h)], [K("fr", h)])
+        grp(a2, [(M("SdI"), C), (M("R0"), e)], [K("SdI"), K("R0"), kC, ke], [k2])
+        tt(a2, a2, hs("dm", h), A.mult, H, [k2, K("dm", h)], [k2])
+        tt(hs("Ct", h), a2, C, A.add, H, [k2, kC], [K("Ct", h)])
+        grp(a3, [(M("SuI"), C), (M("R15"), hs("fr", h))], [K("SuI"), K("R15"), kC, K("fr", h)], [k3])
+        tt(a3, a3, um, A.mult, H, [k3, kum], [k3])
+        tt(hs("C3", h), a3, hs("Ct", h), A.add, H, [k3, K("Ct", h)], [K("C3", h)])
+
+    def xoffs(t):
+        o = (t % 2) * 256
+        r, kr = slot(0, 5, 0, 16)
+        grp(r, [(OH(j), T.u16[:, o + j:o + 256:16]) for j in range(16)], [K("Zs")] + [K("u16", t % 2, h) for h in range(NS)], [kr], 16)
+        cp(T.xi[:], r, 16, [kr], [K("xi")])
+        ts(T.xj[:], T.xi[:], 4, 15, A.arith_shift_right, A.bitwise_and, 16, [K("xi")], [K("xj")])
+        tt(T.xk[:], T.xj[:], T.basex[:], A.add, 16, [K("xj"), K("basex")], [K("xk")])
+        cp(T.offx[:], T.xk[:], 16, [K("xk")], [K("offx")])
+        gather(T.Xo[:], T["X%d" % t][:, 0:4096], T.offx[:], 256, XK[t] + [K("offx")], [K("Xo")])
+
+    def xnew(h):
+        r, kr = slot(h, 6)
+        grp(r, [(M("I4"), hs("Xo", h)), (M("Id"), hs("yb", h))], [K("I4"), K("Id"), K("Xo"), K("yb", h)], [kr])
+        lin(hs("xn", h), r, H, [kr], [K("xn", h)], 167.5 + 1.0 / 16, 1.0 / 8)
+
+    def xscatter(t):
+        return vec(lambda: V.tensor_tensor(T["X%d" % (t + 1)][:, 0:4096].indirect(T.offx[:]), T.xn[:], T.cm192[:], A.add), 256,
+                   [K("xn", h) for h in range(NS)] + [K("cm192"), K("offx")], XK[t + 1], SC)
+
+    def count():
+        r, kr = slot(NS - 1, 5, 0, 1)
+        grp(r, [(M("Rall"), T.acc[:, 4 * h:4 * h + 1], 4) for h in range(NS)], [K("Rall")] + [K("acc", h) for h in range(NS)], [kr], 1)
+        ts(col(CQ), r, 402653184.0, -402653184.0 - 8388608.0, A.add, A.add, 1, [kr], [K("col", CQ)])
+
+    def step4(t, h):
+        (a0, k0), (a1, k1), (a2, k2), (a3, k3) = [slot(h, s) for s in range(4)]
+        e, ke = hs("er", NS * t + h), K("er", t, h)
+        C, kC = hs("C3", h), K("C3", h)
+        vo = (NS * t + h) * (128 + H)
+        kv = K("vr", t, h)
+        grp(a0, [(M("Id"), e)], [K("Id"), ke], [k0])
+        grp(a1, [(M("I2080"), C), (M("I3232"), e)], [K("I2080"), K("I3232"), kC, ke], [k1])
+        tt(hs("pf", h), a0, C, A.mult, H, [k0, kC], [K("pf", h)])
+        tt(hs("pi", h), a1, hs("pf", h), A.add, H, [k1, K("pf", h)], [K("pi", h)])
+        point(h, "off2")
+        if not OPT["z16"]:
+            grp(a2, [(M("Id"), C), (M("nI"), e)], [K("Id"), K("nI"), kC, ke], [k2])
+        o = h * 16 * H
+        for j in range(NP):
+            gather(T.xb[:, o + j * 512:o + (j + 1) * 512], T["X%d" % t][:, 0:4096], T.off2[:, h * H + j * 32:h * H + (j + 1) * 32], 512,
+                   XK[t] + [K("off2", h)], [K("xb", h, j)])
+        def extra(a, b):
+            return [(T.EX8[0:8, :], T.ths[0:8, h * H + a:h * H + b]), (M("Mco"), T.vr[:, vo + 128 + a:vo + 128 + b])]
+
+        xrd = [K("EX8"), K("ths"), K("Mco"), kv]
+        if MAXP[t][h]:
+            v = T.vr[:, vo:vo + H]
+            for j in range(NP):
+                vec((lambda j: lambda: V.tensor_tensor(T.ad[:, o + j * 512:o + (j + 1) * 512], v.indirect(T.vl[:, j * 32:(j + 1) * 32]),
+                                                       T.xb[:, o + j * 512:o + (j + 1) * 512], A.max))(j), 512,
+                    [kv, K("vl"), K("xb", h, j)], [K("ad", h, j)], GA)
+            mm([(a0, v, M("nBM"), True, False, H)]
+               + [(slot(h, 0, k, H, 16)[0], T.xb[:, o + k:o + 16 * H:16], T.nBM[:, 0::16], False, False, 64) for k in range(16)],
+               [K("xb", h, j) for j in range(NP)] + [K("nBM"), kv, k2], [k0])
+            mm([(slot(h, 0, k, H, 16)[0], T.ad[:, o + k:o + 16 * H:16], T.B2[:, 0:8], False, k == 15, 64) for k in range(16)],
+               [K("ad", h, j) for j in range(NP)] + [K("B2")], [k0])
+            lin(hs("lk", h), a0, H, [k0], [K("lk", h)], 0.0, 1.0)
+            grp(a0, extra(0, H) + [(hs("lk", h), M("Id"))], xrd + [K("lk", h), K("Id")], [k0])
+        else:
+            for j in range(NP):
+                wide([(0, 512, T.vr[0:H, vo:vo + 128], T.Sel[0:H, j * 512:(j + 1) * 512], True, False),
+                      (0, 512, M("I8"), T.xb[:, o + j * 512:o + (j + 1) * 512], False, True)], [K("Sel"), K("I8"), kv, K("xb", h, j)],
+                     T.ad[:, o + j * 512:o + (j + 1) * 512], AF.Abs, 0.0, 0.125, [K("ad", h, j)])
+            reduce16(h, 0, "ad", OPT["lkd"], extra, xrd)
+        step(hs("hit", h), a0, H, [k0, K("col", CHT)], [K("hit", h)], col(CHT), -256.0)
+        grp(a3, [(M("Mst"), hs("hit", h))], [K("Mst"), K("hit", h)], [k3])
+        nn, kn = slot(h, 7)
+        if OPT["z16"]:
+            step(a2, a3, H, [k3], [k2], -128.0, 256.0)
+            tt(hs("Za", h), a2, C, A.mult, H, [k2, kC], [K("Za", h)])
+            tt(hs("Zb", h), a2, e, A.mult, H, [k2, ke], [K("Zb", h)])
+            grp(nn, [(M("Sd"), C), (M("R0"), e), (M("nSdI"), hs("Za", h)), (M("SdI"), hs("Zb", h))],
+                [K("Sd"), K("R0"), K("SdI"), K("nSdI"), kC, ke, K("Za", h), K("Zb", h)], [kn])
+        else:
+            step(hs("stay", h), a3, H, [k3], [K("stay", h)], -128.0, 256.0)
+            tt(hs("Z4", h), a2, hs("stay", h), A.mult, H, [k2, K("stay", h)], [K("Z4", h)])
+            grp(nn, [(M("Sd"), C), (M("R0"), e), (M("ImSd"), hs("Z4", h), 4)], [K("Sd"), K("R0"), K("ImSd"), kC, ke, K("Z4", h)], [kn])
+        if t < RO - 1:
+            cp(hs("Cc", h), nn, H, [kn], [K("Cc", h)])
+        else:
+            lin(hs("yco", h), nn, H, [kn], [K("yco", h)], 2048.0, 1.0)
+            dma("S", "oyc%d" % h, T.yc[:, h * H:(h + 1) * H], hs("yco", h), 2500, [K("yco", h)], [])
+
+    for h in range(NS):
+        ts(hs("yb", h), hs("y0s", h), 192.0, None, A.add, None, H, [K("y0s")], [K("yb", h)], 0.5)
+        ts(hs("Cc", h), hs("c0s", h), -2048.0, None, A.add, None, H, [K("c0s")], [K("Cc", h)])
+        nn, kn = slot(h, 7)
+        grp(nn, [(M("Id"), hs("Cc", h))], [K("Id"), K("Cc", h)], [kn])
+        uphase(0, h)
+        qphase(h)
+    dma("S", "x1", T.X1[:], T.x0[:], 6000, [], XK[1], [last_w[k] for k in XK[0]])
+    stflip(0)
+    for t in range(RO):
+        xoffs(t)
+        for h in range(NS):
+            cur[0] = h
+            step12(t, h)
+            step3(t, h)
+            xnew(h)
+            if t < RO - 1:
+                uphase(t + 1, h)
+        cur[0] = 0
+        if t < RO - 1:
+            stflip(t + 1)
+        xscatter(t)
+        if t < RO - 1:
+            count()
+            for h in range(NS):
+                qphase(h)
+        else:
+            dma("S", "oyx", T.yx[:], T.X4[:], 6000, XK[4], [])
+            ts(T.yyo[:], T.yb[:], -192.0, None, A.add, None, 256, [K("yb", h) for h in range(NS)], [K("yyo")], 0.5)
+            dma("S", "oyy", T.yy[:], T.yyo[:], 2500, [K("yyo")], [])
+        if t < RO - 1:
+            dma("S", "x%d" % (t + 2), T["X%d" % (t + 2)][:], T["X%d" % (t + 1)][:], 6000, XK[t + 1], XK[t + 2], [last_w[K("vr", t, NS - 1)]])
+        for h in range(NS):
+            cur[0] = h
+            step4(t, h)
+        cur[0] = 0
+    return ops
+
+
+def tight(ops, plan, lat):
+    _, st = replay(ops, plan, lat)
+    eng, deps, prev, last = {}, {}, {}, {}
+    for i, e, d, _ in plan:
+        eng[i], deps[i], prev[i], last[e] = e, d, last.get(e), i
+    fin = {i: st[i] + ops[i]["alt"][eng[i]][1] for i in st}
+    i, out = max(fin, key=fin.get), []
+    while i is not None:
+        p = None
+        for d in deps[i]:
+            if abs(fin[d] + (0.0 if eng[i] == "P" == eng[d] else lat) - st[i]) < 1:
+                p = d
+        if p is None and st[i] > 1:
+            p = prev[i]
+            out.append((i, p))
+        elif p is not None and p not in ops[i]["deps"]:
+            out.append((i, p))
+        i = p
+    return out
+
+
+def nudge(ops, adj, seed, path):
+    r = [seed * 7919 % 2147483648]
+
+    def rnd():
+        r[0] = (r[0] * 1103515245 + 12345) % 2147483648
+        return r[0] / 2147483648.0
+
+    rnd()
+    n = len(ops)
+    pr, le, win = list(adj[0]), list(adj[1]), list(adj[2])
+    kind = int(rnd() * 8)
+    a = int(rnd() * n)
+    if kind >= 4:
+        a, b = path[int(rnd() * len(path))]
+        d = 200.0 + 2500.0 * rnd() ** 2
+        if rnd() < 0.35 and b is not None:
+            if rnd() < 0.5:
+                pr[b] -= d
+            else:
+                le[b] += d * (1 if rnd() < 0.5 else -1)
+            return pr, le, win
+        who, edge = {a}, [a]
+        for _ in range(int(rnd() * 5)):
+            edge = [j for i in edge for j in ops[i]["deps"] if j not in who]
+            who.update(edge)
+        for i in who:
+            pr[i] += d
+        if rnd() < 0.3:
+            win[a] += 300.0 * rnd()
+        return pr, le, win
+    if kind % 4 == 0:
+        who = range(a, min(n, a + 1 + int(rnd() * 40)))
+    elif kind % 4 == 1:
+        who = [i for i in range(n) if ops[i]["wr"][:1] == ops[a]["wr"][:1]]
+    elif kind % 4 == 2:
+        who = [i for i in range(n) if ops[i]["wr"] and ops[a]["wr"] and ops[i]["wr"][0][0] == ops[a]["wr"][0][0]]
+    else:
+        who = [i for i in range(max(0, a - 60), min(n, a + 60)) if rnd() < 0.15]
+    d = rnd() - 0.5
+    what = rnd()
+    for i in who:
+        if what < 0.55:
+            pr[i] += 5000.0 * d
+        elif what < 0.8:
+            le[i] += 2000.0 * d
+        else:
+            win[i] = max(0.0, win[i] + 800.0 * d)
+    return pr, le, win
+
+
+def schedule(ops, lat, adj):
+    n = len(ops)
+    succ = [[] for _ in range(n)]
+    for i, o in enumerate(ops):
+        for d in o["deps"]:
+            succ[d].append(i)
+    pri = [0.0] * n
+    for i in range(n - 1, -1, -1):
+        pri[i] = min(a[1] for a in ops[i]["alt"].values()) + max([pri[j] + lat for j in succ[i]] + [0.0])
+    pri = [p + q for p, q in zip(pri, adj[0])]
+    lean, win = adj[1], adj[2]
+    left = [len(o["deps"]) for o in ops]
+    free = {e: 0.0 for e in "PDAGSR"}
+    fin, eng, plan = [0.0] * n, [None] * n, []
+    bank = {b: {} for b in ("pa0", "pb0", "pa1", "pb1")}
+    pool = {b: -1 for b in ("pT0", "pT1", "pD0", "pD1")}
+    held = {}
+
+    def enter(i):
+        o = ops[i]
+        return (i, [(e, a[1], max([fin[d] + (0.0 if e == "P" == eng[d] else lat) for d in o["deps"]] + [0.0])) for e, a in o["alt"].items()],
+                o["banks"], o.get("take"))
+
+    ready = [enter(i) for i in range(n) if left[i] == 0]
+    while ready:
+        st, t0 = [], 1e18
+        for x in ready:
+            i, al, bs, take = x
+            best = None
+            for e, c, s in al:
+                if free[e] > s:
+                    s = free[e]
+                for b in bs:
+                    for e2, f in bank[b].items():
+                        if e2 != e and fin[f] + lat > s:
+                            s = fin[f] + lat
+                v = s + c + (lean[i] if e == "D" else 0.0)
+                if best is None or v < best[0]:
+                    best = (v, s, e, c)
+            v, s, e, c = best
+            got = None
+            if take:
+                av = [(fin[pool[b]] + lat if pool[b] >= 0 else 0.0, b) for b in take if pool[b] is not None]
+                if not av:
+                    continue
+                f, got = min(av)
+                s = max(s, f)
+            st.append((s, x, e, c, got))
+            if s < t0:
+                t0 = s
+        s, x, e, c, got = max([y for y in st if y[0] <= t0 + win[y[1][0]]], key=lambda y: pri[y[1][0]])
+        i = x[0]
+        o = ops[i]
+        deps = set(o["deps"])
+        for b in x[2]:
+            deps.update(j for e2, j in bank[b].items() if e2 != e)
+            bank[b][e] = i
+        if got:
+            if pool[got] >= 0:
+                deps.add(pool[got])
+            pool[got] = None
+            held[i] = got
+        if "give" in o:
+            pool[held[o["give"]]] = i
+        fin[i] = s + c
+        eng[i] = e
+        if e != "R":
+            free[e] = s + 60.0 if e == "S" else fin[i]
+        plan.append((i, e, deps, got))
+        ready.remove(x)
+        for j in succ[i]:
+            left[j] -= 1
+            if left[j] == 0:
+                ready.append(enter(j))
+    return plan
+
+
+def replay(ops, plan, lat):
+    free, fin, eng, st = {}, {}, {}, {}
+    for i, e, deps, _ in plan:
+        s = max([free.get(e, 0.0)] + [fin[d] + (0.0 if e == "P" == eng[d] else lat) for d in deps])
+        st[i], fin[i], eng[i] = s, s + ops[i]["alt"][e][1], e
+        if e != "R":
+            free[e] = s + 60.0 if e == "S" else fin[i]
+    return max(fin.values()), st
+
+
+def choose(g, T, topo, core):
+    sets = [build(g, T, topo, core, c) for c in COSTS]
+    if "plan" not in MEMO:
+        ops = sets[0]
+        n = len(ops)
+        adj = ([-OPT["stag"] * o["half"] for o in ops], [OPT["lean"] + OPT["lam"] * o["alt"]["D"][1] if "D" in o["alt"] else 0.0 for o in ops], [OPT["win"]] * n)
+        best, kept, path = None, [], None
+        for s in [None] + NUDGES + list(OPT["seeds"]):
+            a = adj if s is None else nudge(ops, adj, s, path)
+            plan = schedule(ops, COSTS[0][5], a)
+            ts = [replay(o, plan, c[5])[0] for o, c in zip(sets, COSTS)]
+            v = sum(math.log(t) * w for t, w in zip(ts, WEIGH))
+            if best is None or v < best[0]:
+                best, adj, path = (v, plan, ts), a, tight(ops, plan, COSTS[0][5])
+                kept += [s] if s is not None else []
+        MEMO["plan"] = best + (kept,)
+    return sets[0], MEMO["plan"][1]
+
+
+def emit(g, T, ops, plan):
+    q = {"P": g.tensor, "D": g.vector, "A": g.scalar, "G": g, "S": g.sync}
+    total, known, mark, eng, pos = {}, {e: {} for e in q}, {}, {}, {}
+    for i, e, deps, got in plan:
+        o = ops[i]
+        PICK[i] = got
+        eng[i] = e
+        pos[i] = len(pos)
+        sem = o["sem"] or "q" + e
+        if e == "R":
+            total[sem] = o["inc"]
+            mark[i] = (sem, o["inc"], {})
+            continue
+        kn = known[e]
+        need = {}
+        for d in deps:
+            if e == "P" and eng[d] == "P":
+                continue
+            s, v, _ = mark[d]
+            if s != "sent" and kn.get(s, 0) < v and need.get(s, (0, 0))[0] < v:
+                need[s] = (v, d)
+        for s, (v, d) in sorted(need.items(), key=lambda x: -pos[x[1][1]]):
+            if kn.get(s, 0) < v:
+                q[e].wait_ge(T.sem[s], v)
+                kn[s] = v
+                for s2, v2 in mark[d][2].items():
+                    if kn.get(s2, 0) < v2:
+                        kn[s2] = v2
+        fns = o["alt"][e][0]
+        for f in fns:
+            ins = f()
+            if f is fns[-1] or OPT["each"]:
+                if sem != "sent":
+                    ins.then_inc(T.sem[sem], o["inc"])
+                total[sem] = total.get(sem, 0) + o["inc"]
+        mark[i] = (sem, total[sem], dict(kn))
+    for s in sorted(total):
+        if known["S"].get(s, 0) < total[s]:
+            g.sync.wait_ge(T.sem[s], total[s])
+
+
+def rank_program(g, core, T, topo):
+    if T.rank_of(core) is None:
+        return
+    ops, plan = choose(g, T, topo, core)
+    emit(g, T, ops, plan)

@@ -3,7 +3,7 @@ from concourse.mybir import AluOpType, ActivationFunctionType
 
 NR, RO = 4, 4
 BF, F16, F32, I32, U16 = "bfloat16", "float16", "float32", "int32", "uint16"
-MATS = ["dk", "BM", "Id", "nI", "I4", "Im2048", "Im32", "I64", "I2080", "I3232", "Lo", "Cm", "Mdl", "Md", "Mu", "Moh",
+MATS = ["dk", "BM", "Id", "nI", "I4", "Im2048", "Im32", "I64", "I2080", "B3232", "c1920", "R0a", "Lo", "Cm", "Mdl", "Md", "Mu", "Moh",
         "Mst", "Sd", "SdI", "SuI", "R0", "R15", "Mco", "Wb", "tA", "tB", "tC", "tD", "tE", "tF", "c192", "I8", "nBM", "Mk", "nSdI"]
 SCRATCH = {m: ("sbuf", [128, 128], BF) for m in MATS}
 SCRATCH.update({
@@ -40,19 +40,18 @@ DMAS = ["w", "y0", "c0", "x0", "st0", "st1", "th", "x1", "x2", "x3", "x4", "oyx"
 SEMAPHORES = (["qP", "qD", "qA", "qG", "sent"] + ["d" + n for n in DMAS]
               + ["a%s%d%d" % (k, t, h) for k in "ev" for t in range(RO) for h in range(4)])
 
-OPT = {"kvm": True, "z16": True, "stag": 4000.0, "lam": 0.3, "lean": 100.0, "win": 120.0, "maxp": 0, "ns": 2, "lkg": True, "lkd": True, "tg": 1, "split": 2, "seeds": [],
+OPT = {"kvm": True, "z16": True, "stag": 4000.0, "lam": 0.2, "lean": 50.0, "win": 150.0, "maxp": 0, "ns": 2, "lkg": False, "lkd": False, "tg": 2, "split": 2, "seeds": [],
        "flex": True, "lag": 1, "each": False}
-NUDGES = [2008, 2012, 2013, 2017, 2018, 2020, 2040, 2048, 2066, 2070, 2082, 2109, 2113, 2141, 2146, 2147, 2212, 2223, 2227, 2235, 2366,
-          2378, 2454, 2670, 2704, 2797, 2895, 3011, 3096, 3197, 3340, 3345, 3389, 3497, 3528, 3533, 3570, 3610, 3639]
-WEIGH = [2.0, 1.0, 1.0, 0.5]
+NUDGES = [4, 6, 12, 20, 26, 36, 54, 58, 63, 96, 106, 107, 133, 145, 150, 192, 195, 259, 269, 335, 336, 380, 414, 432, 469, 479, 517, 528, 631, 676, 684, 771, 826, 856, 873, 887, 950, 994, 1108, 1192, 1199, 1280, 1305, 1312, 1320, 1388, 1409, 1412, 1431, 1468, 1491]
+WEIGH = [1.0, 1.0, 1.0, 1.0, 1.0]
 PICK = {}
-COSTS = [(1.0, 0.5, 1.56, 3.8, 60.0, 90.0, 3000.0, 10.0), (0.85, 0.43, 1.1, 2.0, 40.0, 50.0, 2200.0, 0.0),
-         (1.2, 0.6, 2.0, 5.5, 70.0, 150.0, 4500.0, 10.0), (1.0, 0.85, 1.56, 3.8, 60.0, 90.0, 3000.0, 0.0)]
+COSTS = [(.88, .42, 1.4, 3.8, 40., 140., 3300., 5., 70.), (.83, .40, 1.56, 3.8, 30., 200., 2500., 0., 40.),
+         (.83, .40, 1.3, 3.8, 50., 50., 5000., 0., 130.), (1.04, .50, 1.3, 3.8, 50., 60., 2500., 0., 130.), (.83, .40, 1.3, 3.8, 0., 200., 2500., 28., 0.)]
 MEMO = {}
 
 
 def build(g, T, topo, core, costs):
-    CY, PE, GA, SC, FIX, LAT, REM, MF = costs
+    CY, PE, GA, SC, FIX, LAT, REM, MF, FA = costs
     NS, TG, SPL, LAG = OPT["ns"], OPT["tg"], OPT["split"], OPT["lag"]
     H = 256 // NS
     MAXP = [[OPT["maxp"] >> h & 1 for h in range(NS)] for t in range(RO)]
@@ -223,8 +222,12 @@ def build(g, T, topo, core, costs):
     grp(pw, [(M("Wb"), T.c192[:, 0:1])], [K("Wb"), K("c192")], [kw], 1)
     for j, sc, bi in ((CH, -1.0 / 2048, 191.5 + 2.0 ** -12), (CM, -2.0, 786465.0), (CU, -1.0, 393216.0), (CO, -0.5, 197632.75)):
         lin(col(j), pw, 1, [kw], [K("col", j)], bi, sc)
-    for nm, v in (("Id", 1.0), ("Im2048", -2048.0), ("nI", -1.0), ("I4", 4.0), ("I8", 8.0), ("Im32", -32.0), ("I64", 64.0), ("I2080", 2080.0), ("I3232", 3232.0)):
+    for nm, v in (("Id", 1.0), ("Im2048", -2048.0), ("nI", -1.0), ("I4", 4.0), ("I8", 8.0), ("Im32", -32.0), ("I64", 64.0), ("I2080", 2080.0)):
         mat(nm, 0.0, A.is_equal, v)
+    mat("B3232", -50.0, A.is_gt, 3232.0)
+    ms(M("c1920"), 1920.0, 128, [K("c1920")])
+    ms(M("R0a"), 0.0, 128, [K("R0a")])
+    cp(T.R0a[:, 0::16], T.BM[:, 0::16], 8, [K("BM")], [K("R0a")])
     mat("Lo", 0.0, A.is_gt)
     mat("tA", -50.0, A.is_gt, col(C16), [C16])
     mat("tB", 0.0, A.is_equal, col(KP), [KP])
@@ -385,13 +388,12 @@ def build(g, T, topo, core, costs):
         act(hs("ss", h), a1, AF.Sign, H, [k1, K("col", CSG)], [K("ss", h)], col(CSG))
         s, ks = hs("ss", h), K("ss", h)
         grp(a0, [(M("Id"), C), (M("Moh"), s)], [K("Id"), kC, K("Moh"), ks], [k0])
-        ts(hs("se", h), a0, col(COH), -2048.0, A.add, A.max, H, [k0, K("col", COH)], [K("se", h)])
+        e, ke = hs("es", NS * t + h), K("es", t, h)
+        ts(e, a0, col(COH), -2048.0, A.add, A.max, H, [k0, K("col", COH)], [ke])
+        send("e", e, hs("er", NS * t + h), [ke], t, h)
         grp(a3, [(M("Mu"), s)], [K("Mu"), ks], [k3])
         grp(a2, [(M("Im32"), hs("u16", h, o)), (M("I64"), hs("ob", h, o)), (M("Md"), s)], [K("Im32"), K("I64"), K("Md"), ku16, kob, ks], [k2])
-        grp(a1, [(M("BM"), T.c2050[:, 0:H]), (M("BM"), hs("se", h))], [K("BM"), K("c2050"), K("se", h)], [k1])
-        e, ke = hs("es", NS * t + h), K("es", t, h)
-        ts(e, a1, -2080.0, None, A.add, None, H, [k1], [ke])
-        send("e", e, hs("er", NS * t + h), [ke], t, h)
+        grp(a1, [(M("BM"), T.c2050[:, 0:H]), (M("BM"), e)], [K("BM"), K("c2050"), ke], [k1])
         vo = (NS * t + h) * (128 + H)
         um, kum = T.vs[:, vo + 128:vo + 128 + H], K("um", t, h)
         act(um, a3, AF.Sigmoid, H, [k3, K("col", CUM)], [kum, K("acc", h)], col(CUM), 128.0, 1.0, T.acc[:, 4 * h:4 * h + 1])
@@ -415,7 +417,7 @@ def build(g, T, topo, core, costs):
         tt(hs("fi", h), a1, hs("u16", h, o), A.mult, H, [k1, ku16], [K("fi", h)])
         ts(hs("fj", h), hs("fi", h), 5, 4095, A.arith_shift_right, A.bitwise_and, H, [K("fi", h)], [K("fj", h)])
         ts(hs("fr", h), hs("fj", h), -2048.0, None, A.add, None, H, [K("fj", h)], [K("fr", h)])
-        grp(a2, [(M("SdI"), C), (M("R0"), e)], [K("SdI"), K("R0"), kC, ke], [k2])
+        grp(a2, [(M("SdI"), C), (M("R0a"), T.c1920[:, 0:H]), (M("R0a"), e)], [K("SdI"), K("R0a"), K("c1920"), kC, ke], [k2])
         tt(a2, a2, hs("dm", h), A.mult, H, [k2, K("dm", h)], [k2])
         tt(hs("Ct", h), a2, C, A.add, H, [k2, kC], [K("Ct", h)])
         grp(a3, [(M("SuI"), C), (M("R15"), hs("fr", h))], [K("SuI"), K("R15"), kC, K("fr", h)], [k3])
@@ -452,11 +454,15 @@ def build(g, T, topo, core, costs):
         C, kC = hs("C3", h), K("C3", h)
         vo = (NS * t + h) * (128 + H)
         kv = K("vr", t, h)
-        grp(a0, [(M("Id"), e)], [K("Id"), ke], [k0])
-        grp(a1, [(M("I2080"), C), (M("I3232"), e)], [K("I2080"), K("I3232"), kC, ke], [k1])
+        c19 = T.c1920[:, 0:H]
+        mm([(a0, M("BM"), c19, True, False, H), (a0, M("BM"), e, False, True, H),
+            (a1, M("B3232"), c19, True, False, H), (a1, M("B3232"), e, False, False, H), (a1, M("I2080"), C, False, True, H)],
+           [K("BM"), K("c1920"), K("I2080"), K("B3232"), kC, ke], [k0, k1])
         tt(hs("pf", h), a0, C, A.mult, H, [k0, kC], [K("pf", h)])
         tt(hs("pi", h), a1, hs("pf", h), A.add, H, [k1, K("pf", h)], [K("pi", h)])
         point(h, "off2")
+        e, ke = hs("se", h), K("se", h)
+        cp(e, a0, H, [k0], [ke])
         if not OPT["z16"]:
             grp(a2, [(M("Id"), C), (M("nI"), e)], [K("Id"), K("nI"), kC, ke], [k2])
         o = h * 16 * H
@@ -541,6 +547,9 @@ def build(g, T, topo, core, costs):
             cur[0] = h
             step4(t, h)
         cur[0] = 0
+    for o in ops:
+        if "A" in o["alt"]:
+            o["alt"]["A"] = (o["alt"]["A"][0], o["alt"]["A"][1] + FA)
     return ops
 
 

@@ -1,67 +1,65 @@
 import math
 from concourse.mybir import AluOpType, ActivationFunctionType
 
-NR, RO = 4, 4
+NR, RO, NS, H = 4, 4, 2, 128
+OPT = {"R": 2, "tg": 2, "rl": 512, "both": False, "stag": 3000.0, "lam": 0.1, "lean": 100.0, "win": 0.0, "x0q": "A", "ua": 1, "pmax": 9999, "gs": 512}
+R = OPT["R"]
 BF, F16, F32, I32, U16 = "bfloat16", "float16", "float32", "int32", "uint16"
-MATS = ["dk", "BM", "Id", "nI", "I4", "Im2048", "Im32", "I64", "I2080", "B3232", "c1920", "R0a", "Lo", "Cm", "Mdl", "Md", "Mu", "Moh",
-        "Mst", "Sd", "SdI", "SuI", "R0", "R15", "Mco", "Wb", "tA", "tB", "tC", "tD", "tE", "tF", "c192", "I8", "nBM", "Mk", "nSdI"]
+MATS = ["val", "bq", "val1", "val2", "bq2", "dk", "B", "B2", "Id", "Ik1", "I1", "I4", "nI", "BMe", "nBMe", "B3232", "R0a", "Cm", "Mdl", "Md", "Mu", "Moh",
+        "Mst", "SdI", "SuI", "Mco", "R15", "Wb", "tA", "tB", "tC", "tD", "one", "c32", "cnt", "offt", "thT", "K16", "c192"]
 SCRATCH = {m: ("sbuf", [128, 128], BF) for m in MATS}
+XW = 2048 + 16
 SCRATCH.update({
-    "Zs": ("sbuf", [128, 144], BF), "Sel": ("sbuf", [128, 2048], BF), "EX8": ("sbuf", [128, 128], BF),
-    "ImSd": ("sbuf", [128, 128], F32), "Rall": ("sbuf", [128, 128], F32), "c2050": ("sbuf", [128, 128], F16),
-    "cm192": ("sbuf", [128, 256], BF), "col": ("sbuf", [128, 32], F32), "coli": ("sbuf", [128, 8], I32),
-    "wcol": ("sbuf", [128, 8], BF), "basev": ("sbuf", [128, 8], BF), "basex": ("sbuf", [128, 16], F32),
-    "c0s": ("sbuf", [128, 256], I32), "y0s": ("sbuf", [128, 256], BF), "sts": ("sbuf", [128, 1024], BF),
-    "stT": ("sbuf", [128, 2048], BF), "ths": ("sbuf", [128, 256], BF),
+    "Idf": ("sbuf", [128, 128], F32), "SdIf": ("sbuf", [128, 128], F32), "SdI1f": ("sbuf", [128, 128], F32),
+    "Sel": ("sbuf", [128, 2048], BF), "Rep": ("sbuf", [128, 256], BF), "RepN": ("sbuf", [128, 256], BF), "cst": ("sbuf", [128, 512], BF),
+    "RepP": ("sbuf", [128, 256], BF), "src": ("sbuf", [128, 1024], BF), "b8": ("sbuf", [128, 32], BF), "rows": ("sbuf", [128, 64], BF),
+    "cm192": ("sbuf", [128, 256], BF), "col": ("sbuf", [128, 48], F32), "coli": ("sbuf", [128, 8], I32), "wcol": ("sbuf", [128, 8], BF),
+    "c0s": ("sbuf", [128, 256], I32), "y0s": ("sbuf", [128, 256], BF), "sts": ("sbuf", [128, 1024], BF), "stT": ("sbuf", [128, 1024], BF),
     "X0": ("sbuf", [128, 4096], BF), "X1": ("sbuf", [128, 4096], BF), "X2": ("sbuf", [128, 4096], BF),
     "X3": ("sbuf", [128, 4096], BF), "X4": ("sbuf", [128, 4096], BF),
-    "B2": ("sbuf", [128, 8], BF), "vl": ("sbuf", [128, 128], U16), "xa": ("sbuf", [128, 4160], BF), "vg": ("sbuf", [128, 512], BF), "xT": ("sbuf", [128, 4096], BF),
-    "ind": ("sbuf", [128, 4096], BF), "xb": ("sbuf", [128, 4096], BF), "ad": ("sbuf", [128, 4096], BF),
-    "Cc": ("sbuf", [128, 256], F16), "C3": ("sbuf", [128, 256], F16), "Ct": ("sbuf", [128, 256], F16),
-    "yb": ("sbuf", [128, 256], BF), "hib": ("sbuf", [128, 256], BF), "mm": ("sbuf", [128, 256], F32),
-    "qq": ("sbuf", [128, 256], F32), "u16": ("sbuf", [128, 512], F16), "ob": ("sbuf", [128, 512], F16),
-    "pi": ("sbuf", [128, 256], I32), "pj": ("sbuf", [128, 256], I32), "pf": ("sbuf", [128, 256], F32),
-    "fi": ("sbuf", [128, 256], I32), "fj": ("sbuf", [128, 256], I32), "fr": ("sbuf", [128, 256], F16),
-    "off1": ("sbuf", [128, 256], U16), "off2": ("sbuf", [128, 256], U16), "offv": ("sbuf", [128, 16], U16),
-    "offx": ("sbuf", [128, 16], U16), "xi": ("sbuf", [128, 16], I32), "xj": ("sbuf", [128, 16], I32),
-    "xk": ("sbuf", [128, 16], F32), "Xo": ("sbuf", [128, 256], BF), "xn": ("sbuf", [128, 256], BF),
-    "km": ("sbuf", [128, 256], BF), "Za": ("sbuf", [128, 256], F16), "Zb": ("sbuf", [128, 256], F16), "lk": ("sbuf", [128, 256], BF), "ww": ("sbuf", [128, 256], BF), "ss": ("sbuf", [128, 256], BF),
-    "se": ("sbuf", [128, 256], F16), "dm": ("sbuf", [128, 256], BF), "hit": ("sbuf", [128, 256], BF),
-    "stay": ("sbuf", [128, 256], BF), "Z4": ("sbuf", [128, 256], F32), "acc": ("sbuf", [128, 16], F32),
-    "es": ("sbuf", [128, 1024], F16), "er": ("sbuf", [128, 1024], F16),
-    "vs": ("sbuf", [128, 3072], BF), "vr": ("sbuf", [128, 3072], BF),
+    "xa": ("sbuf", [128, 2 * XW], BF), "xT": ("sbuf", [128, 4096], BF), "ind": ("sbuf", [128, 4096], BF),
+    "dd": ("sbuf", [128, 4096], BF), "rl": ("sbuf", [128, 4096], BF),
+    "Cc": ("sbuf", [128, 256], F16), "C3": ("sbuf", [128, 512], F16), "fr": ("sbuf", [128, 256], F16),
+    "yb": ("sbuf", [128, 256], BF), "mm": ("sbuf", [128, 256], F32), "ur": ("sbuf", [128, 128], F32), "rem": ("sbuf", [128, 128], F16),
+    "uc": ("sbuf", [128, 16], F32), "pf": ("sbuf", [128, 256], F32), "pi": ("sbuf", [128, 256], I32), "pj": ("sbuf", [128, 256], I32),
+    "fi": ("sbuf", [128, 16], I32), "fj": ("sbuf", [128, 16], I32),
+    "off1": ("sbuf", [128, 256], U16), "off2": ("sbuf", [128, 256], U16), "offv": ("sbuf", [128, 64], U16), "offx": ("sbuf", [128, 16], U16),
+    "Xo": ("sbuf", [128, 256], BF), "xn": ("sbuf", [128, 256], BF), "ww": ("sbuf", [128, 256], BF), "ss": ("sbuf", [128, 256], BF),
+    "du": ("sbuf", [128, 512], BF), "Z3": ("sbuf", [128, 512], F32), "hit": ("sbuf", [128, 256], BF), "mv": ("sbuf", [128, 256], BF),
+    "Z4": ("sbuf", [128, 256], F32), "es": ("sbuf", [128, 1024], F16), "er": ("sbuf", [128, 1024], F16),
+    "vs": ("sbuf", [128, 1024 * R], BF), "vr": ("sbuf", [128, 1024 * R], BF),
     "yco": ("sbuf", [128, 256], F32), "yyo": ("sbuf", [128, 256], BF),
     "pT0": ("psum", [128, 1024], BF), "pT1": ("psum", [128, 1024], BF),
     "pD0": ("psum", [128, 512], F32), "pD1": ("psum", [128, 512], F32),
     "pa0": ("psum", [128, 512], F32), "pb0": ("psum", [128, 512], F32),
     "pa1": ("psum", [128, 512], F32), "pb1": ("psum", [128, 512], F32),
 })
-DMAS = ["w", "y0", "c0", "x0", "st0", "st1", "th", "x1", "x2", "x3", "x4", "oyx", "oyc0", "oyc1", "oyc2", "oyc3", "oyy"]
+DMAS = ["w", "y0", "c00", "c01", "x0", "st0", "st1", "th", "x1", "x2", "x3", "x4", "oyx", "oyc00", "oyc01", "oyc10", "oyc11", "oyy"]
 SEMAPHORES = (["qP", "qD", "qA", "qG", "sent"] + ["d" + n for n in DMAS]
-              + ["a%s%d%d" % (k, t, h) for k in "ev" for t in range(RO) for h in range(4)])
+              + ["a%s%d%d" % (k, t, h) for k in "ev" for t in range(RO) for h in range(NS)])
 
-OPT = {"kvm": True, "z16": True, "stag": 4000.0, "lam": 0.2, "lean": 50.0, "win": 150.0, "maxp": 0, "ns": 2, "lkg": False, "lkd": False, "tg": 2, "split": 2, "seeds": [],
-       "flex": True, "lag": 1, "each": False}
-NUDGES = [4, 6, 12, 20, 26, 36, 54, 58, 63, 96, 106, 107, 133, 145, 150, 192, 195, 259, 269, 335, 336, 380, 414, 432, 469, 479, 517, 528, 631, 676, 684, 771, 826, 856, 873, 887, 950, 994, 1108, 1192, 1199, 1280, 1305, 1312, 1320, 1388, 1409, 1412, 1431, 1468, 1491]
-WEIGH = [1.0, 1.0, 1.0, 1.0, 1.0]
+AHEAD = {'Pind01': 12000, 'Pind12': -7000, 'Prem': 9800, 'XD': 1000, 'Xo': 5300, 'cnt': -7300, 'col29': -5900, 'dd12': 6300, 'dd13': 3300, 'dd14': 6600, 'dm1': -300, 'fr0': 21000, 'ind00': 17000, 'ind02': 600, 'mm': -7700, 'off21': -5300, 'offv0': 1700, 'pa00BMe': 8700, 'pa00Z3': -23400, 'pa00hit': -13900, 'pa00ss': 300, 'pa01K16': 6000, 'pa02Z4': 3000, 'pa03Cm': -27700, 'pa10BMe': -5100, 'pa10ss': 9000, 'pb00ss': 1700, 'pb02er': -3700, 'pb03cnt': 1600, 'pb10ww': -26000, 'pb11Z4': -11700, 'pb11fr': 20600, 'pb13cnt': 16300, 'pf0': 3000, 'pf1': 9000, 'rem': 300, 'rl11536': 12400, 'sender1': -41300, 'tA': 15700, 'xT12': 7600, 'xa00': 9700, 'xa02': 9300, 'xa10': 9700, 'xa12': -6400, 'xb11536': 26300, 'xn': -9600}
+LEAN = {'Cc1': 2600, 'Xo': -1700, 'cnt': -5000, 'dm0': 5300, 'dm1': -500, 'hit1': -200, 'ind01': 8400, 'ind10': 2200, 'mm': -600, 'mv1': -300, 'v0': 7600, 'xa01': -2100, 'xa02': 1200, 'xa10': 1500, 'yb1': -200}
+WAIT = {'L31': 400, 'Pind00': 150, 'Prem': 150, 'PstT': 700, 'Z30': 700, 'Z40': 150, 'Z41': 150, 'es0': 250, 'ind01': 700, 'pa00b8': 400, 'pa10BMe': 1350, 'pa10Z3': 100, 'pa10b8': 150, 'pa12Z4': 950, 'pb13cnt': 550, 'rl01536': 150, 'ss0': 1000, 'ww0': 400, 'xa10': 150}
+AHEAD = {'Pcnt': -4000, 'Pind01': 400, 'Pind02': 3600, 'Pind03': 4000, 'PstT': -6000, 'XD': -3700, 'Z31': -6900, '_SdI1f': -700, '_Wb': 1300, '_c32': -7000, '_cm192': -300, '_cnt': 4700, '_col0': 1000, '_col14': -700, '_col15': -4000, '_col17': -5000, '_col29': -1000, '_col31': -1000, '_col5': 1300, '_coli2': 1700, '_coli4': 2000, '_cst0': 4000, '_cst3': 2000, '_nI': -1000, '_offtb': -4000, '_rem': -5700, '_tB': -3000, '_tC': -2400, '_tD': 1000, '_val': 2000, 'dd00': 3600, 'dd02': -2700, 'dd03': -1300, 'dd04': -1400, 'dd10': 7600, 'dd11': 3600, 'dd12': 7200, 'dd14': 6700, 'dd15': 8700, 'dm0': -4300, 'fi0': -300, 'fi1': 7000, 'pa00BMe': -4700, 'pa13Cmb': 3600, 'pb10es': -7000, 'pb13cnt': 3900, 'pf0': 6000, 'rl11536': -3000, 'ww1': -700, 'xT12': 2000, 'xa01': 5000, 'xa10': -3000, 'xb11536': 4300}
+LEAN = {'hit1': -500, 'ind00': -500, 'ind13': -3000, 'mv1': -500, 'rl01024': 500, 'rl10': -3000, 'uc': -500, 'xa03': 3000}
+WAIT = {'Pind10': 300, 'Pind11': 150, 'Z40': 700, '_b80': 150, '_col22': 150, '_dk': 400, '_offtd': 150, '_tCc': 400, 'dd11': 1100, 'dd12': 750, 'dd14': 700, 'dm0': 300, 'fr0': 150, 'ind10': 300, 'pa00hit': 300, 'pa01K16': 300, 'pa10BMe': 600, 'pa10ss': 300, 'pb01ss': 600, 'pb10b8': 150, 'pb10ss': 300, 'pb11fr': 150, 'pf0': 150, 'pi1': 150, 'v0': 150, 'ww0': 600, 'ww1': 600}
+WHEN, PERIOD = {}, 23500
 PICK = {}
-COSTS = [(.88, .42, 1.4, 3.8, 40., 140., 3300., 5., 70.), (.83, .40, 1.56, 3.8, 30., 200., 2500., 0., 40.),
+COSTS = [(.88, .42, 1.5, 3.8, 40., 140., 3300., 5., 40.), (.83, .40, 1.56, 3.8, 30., 200., 2500., 0., 40.),
          (.83, .40, 1.3, 3.8, 50., 50., 5000., 0., 130.), (1.04, .50, 1.3, 3.8, 50., 60., 2500., 0., 130.), (.83, .40, 1.3, 3.8, 0., 200., 2500., 28., 0.)]
 MEMO = {}
 
 
 def build(g, T, topo, core, costs):
     CY, PE, GA, SC, FIX, LAT, REM, MF, FA = costs
-    NS, TG, SPL, LAG = OPT["ns"], OPT["tg"], OPT["split"], OPT["lag"]
-    H = 256 // NS
-    MAXP = [[OPT["maxp"] >> h & 1 for h in range(NS)] for t in range(RO)]
-    NP, XW = H // 32, 16 * H + 16
+    TG, RL = OPT["tg"], OPT["rl"]
     rank = T.rank_of(core)
     A, AF = AluOpType, ActivationFunctionType
     V, S, PEq, SY = g.vector, g.scalar, g.tensor, g.sync
-    ops, last_w, readers, cur = [], {}, {}, [0]
+    ops, last_w, readers, cur = [], {}, {}, [0, -1]
 
-    def add(eng, fns, cost, rd, wr, banks=(), sem=None, after=(), inc=1):
+    def add(eng, fns, cost, rd, wr, banks=(), sem=None, after=(), inc=1, occ=None):
         i = len(ops)
         deps = set(after)
         for k in rd:
@@ -77,41 +75,43 @@ def build(g, T, topo, core, costs):
             last_w[k] = i
             readers[k] = []
         deps.discard(i)
-        ops.append({"alt": {eng: (fns, cost)}, "deps": deps, "banks": tuple(banks), "sem": sem, "inc": inc, "wr": wr, "half": cur[0]})
+        if eng == "A" and occ is None:
+            cost += FA
+        ops.append({"alt": {eng: (fns, cost)}, "deps": deps, "banks": tuple(banks), "sem": sem, "inc": inc, "wr": wr, "half": cur[0], "occ": occ,
+                    "tag": rd[-1][0] if rd else "", "t": cur[1]})
         return i
 
     def also(i, eng, fn, n, rate=1.0):
-        if OPT["flex"]:
-            ops[i]["alt"][eng] = ([fn], FIX + max(64, n * rate) * CY)
+        ops[i]["alt"][eng] = ([fn], FIX + max(64, n * rate) * CY + (FA if eng == "A" else 0.0))
         return i
 
-    def lin(out, in_, n, rd, wr, bias, scale):
-        i = act(out, in_, AF.Identity, n, rd, wr, bias, scale)
-        return also(i, "D", lambda: V.tensor_scalar(out, in_, scale, bias, A.mult, A.add), n)
-
-    def step(out, in_, n, rd, wr, bias, scale):
-        i = act(out, in_, AF.Sigmoid, n, rd, wr, bias, scale)
-        if isinstance(bias, float):
-            also(i, "D", lambda: V.tensor_scalar(out, in_, -bias / scale, None, A.is_gt if scale > 0 else A.is_lt), n)
-        return i
+    def at(x):
+        return x[0]() if isinstance(x, list) else x
 
     def bk(keys):
-        return sorted(set(k[0] for k in keys if k[0][0] == "p" and k[0][1] in "TDab" and len(k[0]) == 3))
+        return sorted(set(k[0] for k in keys if k[0] in ("pa0", "pb0", "pa1", "pb1")))
 
     def vec(fn, n, rd, wr, rate=1.0):
         return add("D", [fn], FIX + max(64, n * rate) * CY, rd, wr, bk(rd + wr))
 
-    def act(out, in_, func, n, rd, wr, bias=0.0, scale=1.0, rate=1.0, acc=None):
-        return add("A", [lambda: S.activation(out, in_, func, bias=bias, scale=scale, accum_out=acc)],
-                   FIX + max(64, n * rate) * CY, rd, wr, bk(rd + wr))
+    def act(out, in_, func, n, rd, wr, bias=0.0, scale=1.0):
+        return add("A", [lambda: S.activation(out, at(in_), func, bias=bias, scale=scale)], FIX + max(64, n) * CY, rd, wr, bk(rd + wr))
+
+    def lin(out, in_, n, rd, wr, bias, scale, rate=1.0):
+        i = act(out, in_, AF.Identity, n, rd, wr, bias, scale)
+        return also(i, "D", lambda: V.tensor_scalar(out, at(in_), scale, bias, A.mult, A.add), n, rate)
+
+    def step(out, in_, n, rd, wr, up, thr, bias):
+        i = act(out, in_, AF.Sigmoid, n, rd, wr, bias, 256.0 if up else -256.0)
+        return also(i, "D", lambda: V.tensor_scalar(out, at(in_), thr, None, A.is_gt if up else A.is_lt), n)
 
     def ts(out, in0, s1, s2, op0, op1, n, rd, wr, rate=1.0):
         if s2 is None:
-            return vec(lambda: V.tensor_scalar(out, in0, s1, None, op0), n, rd, wr, rate)
-        return vec(lambda: V.tensor_scalar(out, in0, s1, s2, op0, op1), n, rd, wr, rate)
+            return vec(lambda: V.tensor_scalar(out, at(in0), s1, None, op0), n, rd, wr, rate)
+        return vec(lambda: V.tensor_scalar(out, at(in0), s1, s2, op0, op1), n, rd, wr, rate)
 
     def tt(out, a, b, op, n, rd, wr, rate=1.0):
-        return vec(lambda: V.tensor_tensor(out, a, b, op), n, rd, wr, rate)
+        return vec(lambda: V.tensor_tensor(out, at(a), b, op), n, rd, wr, rate)
 
     def cp(out, in_, n, rd, wr, rate=1.0):
         return vec(lambda: V.tensor_copy(out, in_), n, rd, wr, rate)
@@ -119,20 +119,34 @@ def build(g, T, topo, core, costs):
     def ms(ap, val, n, wr):
         return vec(lambda: V.memset(ap, val), n, [], wr, 0.5)
 
-    def mmf(out, l, r, a, b):
-        return lambda: PEq.matmul(out, l, r, a, b)
+    def mm(items, rd, wr, rds=None):
+        k = len(items)
+        flags = [it[4] if len(it) > 4 else (j == 0, j == k - 1) for j, it in enumerate(items)]
 
-    def mm(items, rd, wr):
-        return add("P", [mmf(*it[:5]) for it in items], sum(it[5] * PE + MF for it in items) + 40, rd, wr, bk(rd + wr))
+        def one(j):
+            it = items[j]
+            if it[2] is None:
+                return lambda: PEq.transpose(at(it[0]), it[1], M("Id"))
+            return lambda: PEq.matmul(at(it[0]), it[1], it[2], *flags[j])
+        parts, n = [[]], 0
+        for j, it in enumerate(items):
+            if parts[-1] and n + it[3] > OPT["pmax"]:
+                parts.append([])
+                n = 0
+            parts[-1].append(j)
+            n += it[3]
+        for p in parts:
+            c = sum(items[j][3] * PE + MF for j in p)
+            i = add("P", [one(j) for j in p], c + 40, sum((rds[j] for j in p), []) + rd if rds else rd, wr, bk(wr), occ=c)
+            ops[i]["in"], ops[i]["open"] = not flags[p[0]][0], not flags[p[-1]][1]
+        return i
 
     def grp(out, pairs, rd, wr, n=H):
-        k = len(pairs)
-        return mm([(out, p[0], p[1], i == 0, i == k - 1, max(64, n) * (p[2] if len(p) > 2 else 1))
-                   for i, p in enumerate(pairs)], rd, wr)
+        return mm([(out, p[0], p[1], n * (p[2] if len(p) > 2 else 1)) for p in pairs], rd, wr)
 
-    def dma(q, name, out, in_, cost, rd, wr, after=()):
+    def dma(q, name, pairs, cost, rd, wr, after=()):
         qq = SY if q == "S" else S
-        return add(q, [lambda: qq.dma_start(out, in_)], cost, rd, wr, (), "d" + name, after, 16)
+        return add(q, [(lambda p: lambda: qq.dma_start(p[0], p[1]))(p) for p in pairs], cost, rd, wr, (), "d" + name, after, 16, 60.0 * len(pairs))
 
     def gp(fn, n, rd, wr):
         return add("G", [fn], 170 + 2 * n * CY, rd, wr)
@@ -146,227 +160,252 @@ def build(g, T, topo, core, costs):
     def col(j):
         return T.col[:, j:j + 1]
 
+    def loan(kind):
+        p = len(ops)
+        return p, K("loan", p), lambda a, b, r=128, s=1, r0=0: [lambda: T[PICK[p]][r0:r, a:b:s]]
+
+    def give(p, kind, i):
+        ops[p]["take"], ops[i]["give"] = (kind + "0", kind + "1"), p
+
     XK = [[K("X%d" % t)] for t in range(5)]
-    i = dma("S", "w", T.wcol[:, 0:1], T.w[:], 2000, [], [K("wcol")])
-    dma("S", "y0", T.y0s[:], T.y0[:], 2200, [], [K("y0s")])
-    dma("S", "c0", T.c0s[:], T.c0[:], 2400, [], [K("c0s")])
-    i = dma("S", "x0", T.X0[:], T.x0[:], 6300, [], XK[0])
-    dma("S", "st0", T.sts[:, 0:256], T.st[:, 0:256], 6500, [], [K("sts", 0)])
-    dma("S", "st1", T.sts[:, 256:1024], T.st[:, 256:1024], 3000, [], [K("sts", 1)], [i])
-    dma("S", "th", T.ths[0:8, :], T.th[:], 2500, [], [K("ths")], [i])
+    for h in range(NS):
+        i = dma("S", "c0%d" % h, [(T.c0s[:, h * H + 16 * q:h * H + 16 * q + 16], T.c0[16 * q:16 * q + 16, h * H:(h + 1) * H]) for q in range(8)],
+                3000, [], [K("c0s", h)])
+        if h == 0:
+            dma("S", "y0", [(T.y0s[:], T.y0[:])], 2400, [], [K("y0s")])
+            dma("S", "w", [(T.wcol[:, 0:1], T.w[:])], 2400, [], [K("wcol")])
+            ix = dma(OPT["x0q"], "x0", [(T.X0[:], T.x0[:])], 6500, [], XK[0])
+    dma("S", "st0", [(T.sts[:, 0:256], T.st[:, 0:256])], 6000, [], [K("sts", 0)])
+    dma("S", "th", [(T.thT[0:16, 16 * q:16 * q + 16], T.th[q:q + 1, :]) for q in range(8)], 3000, [], [K("thT")], [ix])
+    dma("S", "st1", [(T.sts[:, 256:1024], T.st[:, 256:1024])], 3000, [], [K("sts", 1)], [ix])
+
+    def iota(name, pattern, cm, n=128, base=0, ap=None):
+        gp(lambda: g.iota(ap or M(name), pattern, base, cm, allow_small_or_imprecise_dtypes=True), n, [], [K(name)])
 
     gp(lambda: g.iota(T.coli[:, 0:1], [[0, 1]], 0, 1), 1, [], [K("coli", 0)])
-    gp(lambda: g.iota(M("tA"), [[1, 128]], 0, -1, allow_small_or_imprecise_dtypes=True), 128, [], [K("tA")])
-    gp(lambda: g.affine_select(M("tB"), M("tA"), [[-16, 8], [0, 16]], A.is_ge, -100.0, 0, 1), 128, [K("tA")], [K("tB")])
-    gp(lambda: g.affine_select(M("dk"), M("tB"), [[16, 8], [0, 16]], A.is_ge, -100.0, 15, -1), 128, [K("tB")], [K("dk")])
-    gp(lambda: g.iota(T.basex[:], [[256, 16]], 0, 0, allow_small_or_imprecise_dtypes=True), 16, [], [K("basex")])
-    ms(T.Sel[:], -8.0, 2048, [K("Sel")])
-    gp(lambda: g.affine_select(T.Sel[:], T.Sel[:], [[1, 128], [0, 16]], A.is_equal, 0.0, 0, -1), 2048, [K("Sel")], [K("Sel")])
-    ms(T.EX8[0:8, :], -1.0, 128, [K("EX8")])
-    gp(lambda: g.affine_select(T.EX8[0:8, :], T.EX8[0:8, :], [[1, 8], [0, 16]], A.is_equal, 0.0, 0, -1), 128, [K("EX8")], [K("EX8")])
-    ms(T.c192[:, 0:8], 192.0, 8, [K("c192")])
-    ms(T.cm192[:], -192.0, 256, [K("cm192")])
-    ms(T.Zs[:], 0.0, 144, [K("Zs")])
+    iota("val1", [[1, 4], [4, 2], [8, 16]], -1)
+    iota("bq2", [[1, 8], [0, 16]], 0)
+    iota("val", [[1, 128]], -1)
+    iota("bq", [[0, 16], [1, 8]], 0)
+    iota("val2", [[1, 8], [8, 16]], -1)
+    iota("rowx", [[256, 16]], 0, 16, 0, T.rows[:, 0:16])
+    iota("rowv", [[0, R], [256, 2], [512, 4]], 0, 8 * R, 256, T.rows[:, 16:16 + 8 * R])
+    ms(T.src[:, 0:128], 4096.0, 128, [K("src", 0)])
+    ms(T.src[:, 256:512], -8.0, 256, [K("src", 1)])
+    ms(T.src[0:32, 512:768], -1.0, 256, [K("src", 2)])
+    ms(T.src[0:80, 768:1024], -32.0, 256, [K("src", 3)])
+
+    def sel(out, in_, pattern, base, n, rd, wr):
+        gp(lambda: g.affine_select(out, in_, pattern, A.is_equal, 0.0, base, -1), n, rd, wr)
+
     for h in range(NS):
-        ms(T.xa[:, h * XW + 16 * H:(h + 1) * XW], 0.0, 16, [K("xa", h, "pad")])
-    if H < 128:
-        ms(T.vg[:], 0.0, 512, [K("vg", h) for h in range(NS)])
-    ts(M("c2050"), T.cm192[:, 0:128], 0.0, 2050.0, A.mult, A.add, 128, [K("cm192")], [K("c2050")], 0.5)
-    KP, E0, E15, MID, C16, CD0, CT1, CV1, CT2, CV2, CM4, CM8, COH, CSG, CDM, CUM, CHT, CCO, C32, NG1, CQ, TM, TM2, B16, CH, CM, CU, CO, TM3 = range(29)
-    ts(T.coli[:, 2:3], T.coli[:, 0:1], 15, None, A.bitwise_and, None, 1, [K("coli", 0)], [K("coli", 2)])
-    cp(col(KP), T.coli[:, 2:3], 1, [K("coli", 2)], [K("col", KP)])
+        sel(T.Rep[0:16, h * H:(h + 1) * H], T.src[0:16, 0:128], [[1, 4], [4, 2], [0, 16]], 8 * h, 128, [K("src", 0)], [K("Rep", h)])
+    for c in range(4):
+        for r in range(2):
+            o = 512 * c + 256 * r
+            sel(T.Sel[:, o:o + 256], T.src[:, 256:512], [[2, 8], [0, 16], [64, 2]], 16 * c + r, 256, [K("src", 1)], [K("Sel", c, r)])
+    sel(T.RepP[0:80, :], T.src[0:80, 768:1024], [[8, 2], [0, 16], [1, 8]], 64, 256, [K("src", 3)], [K("RepP")])
+    sel(T.RepN[0:16, :], T.src[0:16, 512:768], [[8, 2], [0, 16], [1, 8]], 0, 256, [K("src", 2)], [K("RepN")])
+    ms(M("one"), 1.0, 128, [K("one")])
+    ms(M("c32"), 32.0, 128, [K("c32")])
+    ms(M("cnt"), 16.0, 128, [K("cnt")])
+    ms(T.c192[:, 0:80], -192.0, 80, [K("c192")])
+    ms(T.offt[0:23, 0:80], 0.0, 80, [K("offt")])
+    for rows, a, b, v in ((23, 0, 32, -44.5), (1, 32, 64, -7.5), (1, 64, 80, -0.5)):
+        ms(T.offt[0:rows, a:b], v, 32, [K("offt")])
+    ms(T.cst[0:32, 0:128], 992.0, 128, [K("cst", 0)])
+    ms(T.cst[0:32, 128:256], 87.0 * 2 ** 20, 128, [K("cst", 1)])
+    ms(T.cst[0:32, 256:384], -28672.0, 128, [K("cst", 2)])
+    ms(T.cst[0:32, 384:512], 0.0, 128, [K("cst", 3)])
+    ms(T.cst[0:32, 384:392], 28672.0, 8, [K("cst", 3)])
+    ms(T.cm192[:], -192.0, 256, [K("cm192")])
+    for h in range(NS):
+        ms(T.xa[:, h * XW + 2048:(h + 1) * XW], 0.0, 16, [K("xa", h, "pad")])
+    ts(T.fr[:], T.cm192[:], 0.0, None, A.mult, None, 256, [K("cm192")], [K("fr", h) for h in range(NS)], 0.5)
+
+    (KP, BP, IP, GP, E0, E15, TM, C16, CD0, NG1, PG1, CT1, CT2, CV1, CV2, CM4, CM8, CMF, COH, CSG, TD, BD, TU, BU, TH, BH,
+     C32, CCO, CX, MAG, T1, T2) = range(32)
+    for j, (c, s, op) in enumerate(((BP, 7, A.bitwise_and), (GP, 4, A.arith_shift_right), (KP, 3, A.arith_shift_right), (IP, 15, A.bitwise_and))):
+        ts(T.coli[:, 2 + j:3 + j], T.coli[:, 0:1], s, None, op, None, 1, [K("coli", 0)], [K("coli", 2 + j)])
+        lin(col(c), T.coli[:, 2 + j:3 + j], 1, [K("coli", 2 + j)], [K("col", c)], 0.0, 1.0)
+        ops[-1]["alt"].pop("A")
 
     def c1(j, src, s1, s2, o0, o1, extra=()):
         ts(col(j), col(src), s1, s2, o0, o1, 1, [K("col", src)] + [K("col", e) for e in extra], [K("col", j)])
 
-    def ca(j, src, scale, bias, func=None, extra=()):
+    def ca(j, src, scale, bias, extra=()):
         lin(col(j), col(src), 1, [K("col", src)] + [K("col", e) for e in extra], [K("col", j)], bias, scale)
 
     CE = math.log(32.0)
+    for j, (a, v) in enumerate(((0, 34), (32, 27), (64, 24))):
+        ms(T.col[a:a + 32, MAG:MAG + 1], 1.5 * 2 ** v, 1, [K("col", MAG)])
     c1(E0, KP, 0.0, None, A.is_equal, None)
     c1(E15, KP, 15.0, None, A.is_equal, None)
     c1(TM, E0, col(E15), None, A.add, None, [E15])
     ca(C16, KP, -1.0, 16.0)
     ca(CD0, E0, -21.0, 1.0)
     ca(NG1, E0, 1.0, -1.0)
-    ca(CT1, TM, -50.0, 0.0)
-    ca(CT2, TM, -50.0, -0.5)
+    ca(PG1, E0, -1.0, 1.0)
+    ca(CT1, TM, -50.0, 100.0)
+    ca(CT2, TM, -50.0, 99.5)
     ca(CM4, TM, -4096.0, 4096.0)
     ca(CM8, TM, -8192.0, 8192.0)
+    ca(CMF, TM, -1024.0, 0.0)
     ca(CV2, TM, -33.0, 1.0)
-    ca(CV1, E15, 64.0, col(CV2), None, [CV2])
+    ca(CV1, E15, 64.0, col(CV2), [CV2])
     ca(CSG, E15, -math.exp(CE * (8.5 - 16) - 10), 0.0)
-    ca(CHT, E15, 262144.0, 128.0 - 131072.0)
-    ca(CCO, E15, -512.0, 0.0)
-    ca(C32, E15, 32.0, 0.0)
-    ca(B16, KP, 16.0, 0.0)
-    c1(MID, KP, 14.0, -4096.0, A.min, A.mult)
-    c1(COH, E0, -8192.0, col(MID), A.mult, A.add, [MID])
-    c1(TM2, KP, 1.0, -128.0, A.max, A.mult)
-    ca(CDM, TM2, 1.0, -128.0 * (62 - 65600))
-    ca(TM3, KP, 128.0, -128.0 * 65)
-    ca(CUM, E15, 128.0, col(TM3), None, [TM3])
-    ms(col(CQ), -8388608.0, 1, [K("col", CQ)])
-    ts(T.basev[:], T.basex[:, 0:8], col(B16), 16.0, A.add, A.add, 8, [K("basex"), K("col", B16)], [K("basev")])
-    ts(T.basex[:], T.basex[:], col(B16), None, A.add, None, 16, [K("basex"), K("col", B16)], [K("basex")])
+    c1(T1, KP, 14.0, -4096.0, A.min, A.mult)
+    ca(COH, E0, -3072.0, col(T1), [T1])
+    c1(T2, KP, 1.0, 46.0, A.max, A.add)
+    ca(TD, T2, -1.0, 0.0)
+    ca(BD, T2, -256.0, 0.0)
+    c1(TU, C16, 49.0, col(E15), A.add, A.subtract, [E15])
+    ca(BU, TU, -256.0, 0.0)
+    ca(TH, E15, -1024.0, 512.5)
+    ca(BH, TH, 256.0, 0.0)
+    ca(C32, E0, -3232.0, 3232.0)
+    ca(CCO, E0, -0.5, 0.0)
+    ca(CX, IP, 16.0, 7.5)
 
-    def mat(name, s1, o0, s2=1.0, cols=(), src="dk", o1=None):
-        ts(M(name), M(src), s1, s2, o0, o1 or A.mult, 128, [K(src)] + [K("col", c) for c in cols], [K(name)], 0.5)
+    def mat(name, src, s1, o0, s2=1.0, cols=(), o1=None, a=0, b=128, out=None):
+        ts(out or M(name), T[src][:, a:b], s1, s2, o0, o1 or A.mult, b - a, [K(src)] + [K("col", c) for c in cols], [K(name)], 0.5)
 
     def mat2(name, a, b, op):
         tt(M(name), M(a), M(b), op, 128, [K(a), K(b)], [K(name)], 2.0)
 
-    mat("BM", -50.0, A.is_gt)
-    ts(M("Wb"), M("dk"), -50.0, T.wcol[:, 0:1], A.is_gt, A.mult, 128, [K("dk"), K("wcol")], [K("Wb")], 0.5)
-    pw, kw = T.pb1[:, 0:1], K("pb1", 0)
-    grp(pw, [(M("Wb"), T.c192[:, 0:1])], [K("Wb"), K("c192")], [kw], 1)
-    for j, sc, bi in ((CH, -1.0 / 2048, 191.5 + 2.0 ** -12), (CM, -2.0, 786465.0), (CU, -1.0, 393216.0), (CO, -0.5, 197632.75)):
-        lin(col(j), pw, 1, [kw], [K("col", j)], bi, sc)
-    for nm, v in (("Id", 1.0), ("Im2048", -2048.0), ("nI", -1.0), ("I4", 4.0), ("I8", 8.0), ("Im32", -32.0), ("I64", 64.0), ("I2080", 2080.0)):
-        mat(nm, 0.0, A.is_equal, v)
-    mat("B3232", -50.0, A.is_gt, 3232.0)
-    ms(M("c1920"), 1920.0, 128, [K("c1920")])
+    mat("I1", "val1", 0.0, A.is_equal)
+    mat("tC", "bq2", col(GP), A.is_equal, 1.0, [GP])
+    ts(M("Wb"), M("tC"), T.wcol[:, 0:1], None, A.mult, None, 128, [K("tC"), K("wcol")], [K("Wb")], 0.5)
+    for j, v in enumerate((1.0, 2.0, -1.0)):
+        ts(T.b8[:, 8 * j:8 * j + 8], T.bq2[:, 0::16], col(GP), v, A.is_equal, A.mult, 8, [K("bq2"), K("col", GP)], [K("b8", j)])
+    BO8, BO2, BOn = T.b8[:, 0:8], T.b8[:, 8:16], T.b8[:, 16:24]
+    mat("Id", "val", 0.0, A.is_equal)
+    mat("I4", "val", 0.0, A.is_equal, 4.0)
+    mat("nI", "val", 0.0, A.is_equal, -1.0)
+    mat("Idf", "val", 0.0, A.is_equal)
+    mat("Ik1", "val", 0.0, A.is_equal, col(PG1), [PG1])
+    mat("B2", "bq2", col(BP), A.is_equal, 1.0, [BP])
+    mat("tA", "val2", 0.0, A.is_gt, col(C16), [C16], A.subtract)
+    mat2("tA", "tA", "B2", A.mult)
+    mat("tB", "val2", 0.0, A.is_equal, col(KP), [KP])
+    mat2("Cm", "tB", "tA", A.subtract)
+    mat("B", "bq", col(BP), A.is_equal, 1.0, [BP])
+    mat("dk", "val", 0.125, A.mult, 100.0, (), A.add)
+    mat2("dk", "dk", "B", A.mult)
+    mat("nBMe", "bq", col(BP), A.is_equal, col(NG1), [BP, NG1])
+    mat("BMe", "bq", col(BP), A.is_equal, col(PG1), [BP, PG1])
+    mat("B3232", "bq", col(BP), A.is_equal, col(C32), [BP, C32])
+    mat("K16", "bq", col(BP), A.is_equal, -16.0, [BP])
+    mat("tD", "val", 0.0, A.is_equal, 16.0)
+    mat2("Mdl", "nBMe", "tD", A.add)
+    mat("Mdl", "bq", col(BP), A.is_equal, col(CD0), [BP, CD0], None, 0, 8, T.Mdl[:, 0:8])
+    mat("Mdl", "bq", col(BP), A.is_equal, col(E0), [BP, E0], None, 0, 8, T.Mdl[:, 120:128])
+    mat("Md", "dk", col(CT1), A.is_gt, col(CV1), [CT1, CV1])
+    mat("Mu", "dk", col(CT2), A.is_gt, col(CV2), [CT2, CV2])
+    mat("tC", "dk", 99.5, A.is_gt, col(CM4), [CM4])
+    mat("tD", "dk", 100.0, A.is_gt, col(CM8), [CM8])
+    mat2("Moh", "tC", "tD", A.subtract)
+    mat("Moh", "bq", col(BP), A.is_equal, col(CMF), [BP, CMF], None, 0, 8, T.Moh[:, 0:8])
     ms(M("R0a"), 0.0, 128, [K("R0a")])
-    cp(T.R0a[:, 0::16], T.BM[:, 0::16], 8, [K("BM")], [K("R0a")])
-    mat("Lo", 0.0, A.is_gt)
-    mat("tA", -50.0, A.is_gt, col(C16), [C16])
-    mat("tB", 0.0, A.is_equal, col(KP), [KP])
-    mat2("tA", "tA", "tB", A.add)
-    mat2("Cm", "tA", "Lo", A.subtract)
-    BO8 = T.BM[:, 0::16]
-    cp(T.Zs[:, 15:143:16], BO8, 8, [K("BM")], [K("Zs")])
-    mat("tC", -50.0, A.is_gt, col(NG1), [NG1])
-    mat("tD", 0.0, A.is_equal, 16.0)
-    mat2("Mdl", "tC", "tD", A.add)
-    ts(T.Mdl[:, 0::16], BO8, col(CD0), None, A.mult, None, 8, [K("BM"), K("col", CD0)], [K("Mdl")])
-    ts(T.Mdl[:, 15::16], BO8, col(E0), None, A.mult, None, 8, [K("BM"), K("col", E0)], [K("Mdl")])
-    mat("Md", col(CT1), A.is_gt, col(CV1), [CT1, CV1])
-    mat("Mu", col(CT2), A.is_gt, col(CV2), [CT2, CV2])
-    mat("tE", -0.5, A.is_gt, col(CM4), [CM4])
-    mat("tF", 0.0, A.is_gt, col(CM8), [CM8])
-    mat2("Moh", "tE", "tF", A.subtract)
-    if any(any(r) for r in MAXP):
-        mat("nBM", -50.0, A.is_gt, -1.0)
-        ts(T.B2[:], BO8, 2.0, None, A.mult, None, 8, [K("BM")], [K("B2")])
-        gp(lambda: g.iota(T.pj[:, 0:128], [[1, 128]], 0, 0), 128, [], [K("pj", 0)])
-        cp(T.vl[:], T.pj[:, 0:128], 128, [K("pj", 0)], [K("vl")])
-    if OPT["kvm"]:
-        gp(lambda: g.iota(M("Mk"), [[0, 8], [1, 16]], 0, 0, allow_small_or_imprecise_dtypes=True), 128, [], [K("Mk")])
-        mat("Mk", col(KP), A.is_equal, 1.0, [KP], "Mk")
-    mat("Sd", 1.0, A.is_equal)
-    mat2("SdI", "Sd", "Id", A.subtract)
-    mat("tA", -1.0, A.is_equal)
-    mat2("SuI", "tA", "Id", A.subtract)
-    mat("R0", 0.0, A.is_equal, col(E0), [E0])
-    mat("R15", 0.0, A.is_equal, col(E15), [E15])
-    mat("Rall", -200.0, A.is_gt, col(C32), [C32])
-    mat("tB", 0.0, A.is_gt, -17.0)
-    mat2("Mst", "tB", "BM", A.add)
-    mat("nSdI" if OPT["z16"] else "ImSd", -1.0, A.mult, 1.0, (), "SdI")
-    mat("Mco", -50.0, A.is_gt, col(CCO), [CCO])
-    ts(T.Mco[:, 15::16], T.Mco[:, 15::16], -1.0, None, A.mult, None, 8, [K("Mco")], [K("Mco")])
+    mat("R0a", "bq", col(BP), A.is_equal, col(PG1), [BP, PG1], None, 0, 8, T.R0a[:, 0:8])
+    mat("tA", "val", 8.0, A.is_equal)
+    mat2("SdI", "tA", "Id", A.subtract)
+    mat2("SdIf", "tA", "Id", A.subtract)
+    mat("tB", "val", -8.0, A.is_equal)
+    mat2("SuI", "tB", "Id", A.subtract)
+    mat("tC", "val1", 8.0, A.is_equal)
+    mat2("SdI1f", "tC", "I1", A.subtract)
+    mat("tD", "dk", 100.0, A.is_gt, -17.0)
+    mat2("Mst", "tD", "B", A.add)
+    mat("R15", "bq", -1.0, A.is_gt, col(E15), [E15])
+    mat("Mco", "bq", col(BP), A.is_equal, col(CCO), [BP, CCO])
+    mat("Mco", "Mco", -1.0, A.mult, 1.0, (), None, 120, 128, T.Mco[:, 120:128])
 
-    def OH(j):
-        return T.Zs[:, 15 - j:143 - j]
-
-    nT = [0]
-
-    def flip(srcs, dst, rows, rd, wr):
+    def flip(srcs, dst, rd, wr):
         n = 128 * len(srcs)
-        kb = K("loan", len(ops))
-        p = add("P", [(lambda c: lambda: PEq.transpose(T[PICK[p]][0:rows, c * 128:(c + 1) * 128], srcs[c], M("Id")))(c) for c in range(len(srcs))],
-                len(srcs) * (128 * PE + MF) + 40, rd + [K("Id")], [kb])
-        i = vec(lambda: V.tensor_copy(dst, T[PICK[p]][0:rows, 0:n]), n, [kb], wr, 0.5)
-        also(i, "A", lambda: S.activation(dst, T[PICK[p]][0:rows, 0:n], AF.Copy), n)
-        ops[p]["take"], ops[i]["give"] = ("pT0", "pT1"), p
-
-    def wide(items, rd, out, func, bias, scale, wr):
-        kb = K("loan", len(ops))
-        p = add("P", [(lambda it: lambda: PEq.matmul(T[PICK[p]][:, it[0]:it[1]], *it[2:]))(it) for it in items],
-                sum((it[1] - it[0]) * PE + MF for it in items) + 40, rd, [kb])
-        i = add("A", [lambda: S.activation(out, T[PICK[p]][:, :], func, bias=bias, scale=scale)], FIX + 512 * CY, [kb], wr)
-        if func == AF.Sigmoid:
-            also(i, "D", lambda: V.tensor_scalar(out, T[PICK[p]][:, :], -bias / scale, None, A.is_gt), 512)
-        ops[p]["take"], ops[i]["give"] = ("pD0", "pD1"), p
+        p, kb, B = loan("pT")
+        mm([(B(c * 128, (c + 1) * 128), s, None, 128, (True, True)) for c, s in enumerate(srcs)], [K("Id")], [kb], rd)
+        i = vec(lambda: V.tensor_copy(dst, at(B(0, n))), n, [kb], wr, 0.5)
+        also(i, "A", lambda: S.activation(dst, at(B(0, n)), AF.Copy), n)
+        give(p, "pT", i)
 
     def stflip(t):
-        flip([T.sts[:, t * 256 + h * H:t * 256 + (h + 1) * H] for h in range(NS)], T.stT[0:H, t * NS * 128:(t + 1) * NS * 128], H,
-             [K("sts", min(t, 1))], [K("stT", t)])
+        flip([T.sts[:, t * 256 + h * H:t * 256 + (h + 1) * H] for h in range(NS)], T.stT[:, t * 256:(t + 1) * 256], [[K("sts", min(t, 1))]] * NS, [K("stT", t)])
 
-    def hs(name, h, off=0):
-        return T[name][:, off + h * H:off + (h + 1) * H]
+    def hs(name, h, w=H):
+        return T[name][:, h * w:(h + 1) * w]
 
-    def slot(h, s, a=0, b=None, st=1):
-        nm = ["pa0", "pb0", "pa1", "pb1"][(h * 8 + s) * H // 512]
-        o = (h * 8 + s) * H % 512
-        return T[nm][:, o + a:o + (H if b is None else b):st], K(nm, o)
-
-    def uphase(t, h):
-        o = (t % 2) * 256
-        us, kus = slot(h, 5)
-        u, ku = slot(h, 6)
-        pr = [(M("Wb"), hs("yb", h))]
-        rd = [K("Wb"), K("yb", h)]
-        grp(us, pr, rd, [kus])
-        lin(hs("hib", h), us, H, [kus, K("col", CH)], [K("hib", h)], col(CH), 1.0 / 2048)
-        grp(u, pr + [(M("Im2048"), hs("hib", h))], rd + [K("Im2048"), K("hib", h)], [ku])
-        lin(hs("mm", h), u, H, [ku, K("col", CM)], [K("mm", h)], col(CM), 2.0)
-        ts(hs("u16", h, o), u, col(CU), None, A.add, None, H, [ku, K("col", CU)], [K("u16", t % 2, h)])
-        ts(hs("ob", h, o), u, 0.5, col(CO), A.mult, A.add, H, [ku, K("col", CO)], [K("ob", t % 2, h)])
-
-    def qphase(h):
-        lin(hs("qq", h), hs("mm", h), H, [K("mm", h), K("col", CQ)], [K("qq", h)], col(CQ), 2048.0)
-
-    def point(h, off):
-        ts(hs("pj", h), hs("pi", h), 5, 4095, A.arith_shift_right, A.bitwise_and, H, [K("pi", h)], [K("pj", h)])
-        cp(hs(off, h), hs("pj", h), H, [K("pj", h)], [K(off, h)])
+    def slot(b, h, s, a=0, e=H, st=1):
+        nm = "p%s%d" % (b, h)
+        return T[nm][:, s * H + a:s * H + e:st], K(nm, s)
 
     def gather(out, win, offs, n, rd, wr):
         i = vec(lambda: V.tensor_copy(out, win.indirect(offs)), n, rd, wr, GA)
         return also(i, "A", lambda: S.activation(out, win.indirect(offs), AF.Copy), n, GA)
 
-    def reduce16(h, s, name, lk, extra, xrd):
-        out, ko = slot(h, s)
-        o = h * 16 * H
-        if not lk:
-            n = H // SPL
-            for b in range(SPL):
-                grp(slot(h, s, b * n, (b + 1) * n)[0],
-                    extra(b * n, (b + 1) * n) + [(OH(k), T[name][:, o + b * n * 16 + k:o + (b + 1) * n * 16:16]) for k in range(16)],
-                    [K(name, h, j) for j in range(b * NP // SPL, (b + 1) * NP // SPL)] + xrd + [K("Zs")], [ko], n)
-            return
-        mm([(slot(h, s, k, H, 16)[0], T[name][:, o + k:o + 16 * H:16], BO8, True, True, 64) for k in range(16)],
-           [K(name, h, j) for j in range(NP)] + [K("BM")], [ko])
-        lin(hs("lk", h), out, H, [ko], [K("lk", h)], 0.0, 1.0)
-        grp(out, extra(0, H) + [(hs("lk", h), M("Id"))], xrd + [K("lk", h), K("Id")], [ko])
+    def uphase(t):
+        kyb = [K("yb", h) for h in range(NS)]
+        p, kb, B = loan("pD")
+        mm([(B(0, 128, 80), T.c192[:, 0:80], M("Wb"), 128)]
+           + [(B(i, 128, 32 * a + 16, 16, 32 * a), T.yb[:, i::16], T.Wb[:, 0::16], 16) for a in range(3) for i in range(16)]
+           + [(B(0, 128, 80), T.offt[0:23, 0:80], T.one[0:23, :], 128)],
+           kyb + [K("c192"), K("Wb"), K("offt"), K("one")], [kb])
+        mg = T.col[0:80, MAG:MAG + 1]
+        ts(T.ur[0:80, :], B(0, 128, 80), mg, mg, A.add, A.subtract, 128, [K("col", MAG)], [kb, K("ur")])
+        give(p, "pD", tt(T.rem[0:80, :], B(0, 128, 80), T.ur[0:80, :], A.subtract, 128, [K("ur")], [kb, K("rem")]))
+        p, kb, B = loan("pD")
+        mm([(B(0, 256), T.rem[0:16, :], T.Rep[0:16, :], 256, (True, True)), (B(256, 272), T.rem[0:16, :], T.Id[0:16, 0:16], 64, (True, True)),
+            (B(272, 288), T.one[0:1, :], T.rows[0:1, 0:16], 64, (True, False)), (B(272, 288), T.rem[0:48, :], T.Id[0:48, 32:48], 64, (False, True))],
+           [K("rem"), K("Rep", 0), K("Rep", 1), K("Id"), K("one"), K("rowx")], [kb])
+        lin(T.mm[:], B(0, 256), 256, [], [kb, K("mm")], 2080.0, 1.0 / 2048)
+        ts(T.offx[:], B(272, 288), col(CX), None, A.add, None, 16, [K("col", CX)], [kb, K("offx")])
+        give(p, "pD", lin(T.uc[:], B(256, 272), 16, [], [kb, K("uc")], 1023.5, 1.0))
+        gather(T.Xo[:], T["X%d" % t][:, 0:4096], T.offx[:], 256, XK[t] + [K("offx")], [K("Xo")])
+
+    def qphase(h):
+        q, kq = slot("b", h, 3)
+        grp(q, [(T.rem[0:16, :], T.Rep[0:16, h * H:(h + 1) * H]), (M("c32"), M("cnt"))], [K("rem"), K("Rep", h), K("c32"), K("cnt")], [kq])
+
+    def point(h, a, b, c, rd1, rd2, off):
+        tt(hs("pf", h), a, b, A.mult, H, rd1, [K("pf", h)])
+        tt(hs("pi", h), c, hs("pf", h), A.add, H, rd2 + [K("pf", h)], [K("pi", h)])
+        ts(hs("pj", h), hs("pi", h), 5, 4095, A.arith_shift_right, A.bitwise_and, H, [K("pi", h)], [K("pj", h)])
+        cp(hs(off, h), hs("pj", h), H, [K("pj", h)], [K(off, h)])
+
+    def fold(out, name, h, lo, rhs, a, b):
+        return [(out(i), lo(i), rhs, 64, (a, b(i))) for i in range(16)]
 
     def step12(t, h):
-        nn, kn = slot(h, 7)
-        E, kE = slot(h, 4)
-        tt(E, nn, hs("mm", h), A.mult, H, [kn, K("mm", h)], [kE])
-        tt(hs("pi", h), E, hs("qq", h), A.add, H, [kE, K("qq", h)], [K("pi", h)])
-        point(h, "off1")
-        xo = h * XW
-        X = T["X%d" % t]
-        for j in range(NP):
-            gather(T.xa[:, xo + j * 512:xo + (j + 1) * 512], X[:, 0:4096], T.off1[:, h * H + j * 32:h * H + (j + 1) * 32], 512,
-                   XK[t] + [K("off1", h)], [K("xa", h, j)])
-        so = (t * NS + h) * 128
-        for b in range(NP // TG):
-            o = h * 16 * H + b * TG * 512
-            flip([T.xa[:, xo + c * 128:xo + (c + 1) * 128] for c in range(4 * TG * b, 4 * TG * (b + 1))], T.xT[:, o:o + TG * 512], 128,
-                 [K("xa", h, j) for j in range(b * TG, (b + 1) * TG)], [K("xT", h, b)])
-            for j in range(b * TG, (b + 1) * TG):
-                o = h * 16 * H + j * 512
-                its = [(0, 512, T.stT[0:H, so:so + 128], T.Sel[0:H, j * 512:(j + 1) * 512], True, False)]
-                its += [(c * 128, (c + 1) * 128, T.xT[:, o + c * 128:o + (c + 1) * 128], M("Cm"), False, c == 3) for c in range(4)]
-                wide(its, [K("stT", t), K("Sel"), K("xT", h, b), K("Cm")], T.ind[:, o:o + 512], AF.Sigmoid, 128.0, 256.0, [K("ind", h, j)])
-        for b in range(NP // TG):
-            o = h * 16 * H
-            mm([(slot(h, 4, c * 8, c * 8 + 8)[0], T.xT[:, o + c * 128:o + (c + 1) * 128], T.Cm[:, 0::16], True, True, 64)
-                for c in range(4 * TG * b, 4 * TG * (b + 1))], [K("xT", h, b), K("Cm")], [kE])
-        reduce16(h, 0, "ind", OPT["lkg"], lambda a, b: [], [])
-        lin(hs("yb", h), E, H, [kE], [K("yb", h)], 191.5 + 1.0 / 64, 1.0 / 32)
+        nn, kn = slot("a", h, 2)
+        q, kq = slot("b", h, 3)
+        point(h, nn, hs("mm", h), q, [kn, K("mm")], [kq], "off1")
+        xo, o = h * XW, h * 2048
+        GS = OPT["gs"]
+        for c in range(2048 // GS):
+            gather(T.xa[:, xo + c * GS:xo + (c + 1) * GS], T["X%d" % t][:, 0:4096], T.off1[:, h * H + c * GS // 16:h * H + (c + 1) * GS // 16], GS,
+                   XK[t] + [K("off1", h)], [K("xa", h, c)])
+        so = t * 256 + h * H
+        kE = K("pa%d" % h, 3)
+        for c0 in range(0, 4, TG):
+            cs = range(c0, c0 + TG)
+            blocks = [(c, bh, r) for c in cs for bh in range(2) for r in range(2)]
+            flip([T.xa[:, xo + 512 * c + 256 * bh + r:xo + 512 * c + 256 * (bh + 1):2] for c, bh, r in blocks],
+                 T.xT[:, o + c0 * 512:o + (c0 + TG) * 512], [[K("xa", h, (512 * c + 256 * bh) // GS)] for c, bh, r in blocks], [K("xT", h, c0)])
+
+            def xT(c, bh, r):
+                a = o + 512 * c + 256 * bh + 128 * r
+                return T.xT[:, a:a + 128]
+            for c in cs:
+                p, kb, B = loan("pD")
+                mm([(B(0, 512), T.stT[:, so:so + 128], T.Sel[:, 512 * c:512 * (c + 1)], 512)]
+                   + [(B(256 * r + bh, 256 * (r + 1), 128, 2), xT(c, bh, r), M("Cm"), 128) for bh in range(2) for r in range(2)],
+                   [], [kb], [[K("stT", t), K("Sel", c, 0), K("Sel", c, 1), K("xa", h, 512 * c0 // GS)]] + [[K("xT", h, c0), K("Cm")]] * 4)
+                give(p, "pD", step(T.ind[:, o + c:o + 2048:4], B(0, 512), 512, [kb], [K("ind", h, c)], True, -0.5, 128.0))
+            mm([(slot("a", h, 3, 16 * (c + 4 * bh) + r, 16 * (c + 4 * bh) + 16, 2)[0], xT(c, bh, r), T.Cm[:, 0::16], 64, (True, True))
+                for c, bh, r in blocks], [K("xT", h, c0), K("Cm")], [kE])
+        mm([(slot("a", h, 0, i, H, 16)[0], T.ind[:, o + 128 * (8 * (i & 1) + i // 2):o + 128 * (8 * (i & 1) + i // 2 + 1)], BO8, 64, (True, True))
+            for i in range(16)], [K("ind", h, c) for c in range(4)] + [K("b8", 0)], [K("pa%d" % h, 0)])
+        lin(hs("yb", h), slot("a", h, 3)[0], H, [kE], [K("yb", h)], 191.5 + 1.0 / 64, 1.0 / 32)
 
     def send(name, src, dst, ksrc, t, h):
         to = T.cores[(rank + 1 + t % 3) % NR]
@@ -378,250 +417,149 @@ def build(g, T, topo, core, costs):
         add("R", [], REM, [], [K(name + "r", t, h)], (), sem, [i], n)
 
     def step3(t, h):
-        o = (t % 2) * 256
-        ku16, kob = K("u16", t % 2, h), K("ob", t % 2, h)
-        (a0, k0), (a1, k1), (a2, k2), (a3, k3) = [slot(h, s) for s in range(4)]
-        kC = K("Cc", h)
-        C = hs("Cc", h)
+        (a0, k0), (a1, k1) = slot("a", h, 0), slot("a", h, 1)
+        (b0, j0), (b1, j1), (b2, j2) = [slot("b", h, s) for s in range(3)]
+        C, kC = hs("Cc", h), K("Cc", h)
         act(hs("ww", h), a0, AF.Sigmoid, H, [k0], [K("ww", h)], -16 * CE - 10, CE)
-        grp(a1, [(M("Mdl"), hs("ww", h))], [K("Mdl"), K("ww", h)], [k1])
-        act(hs("ss", h), a1, AF.Sign, H, [k1, K("col", CSG)], [K("ss", h)], col(CSG))
+        grp(b0, [(M("Mdl"), hs("ww", h))], [K("Mdl"), K("ww", h)], [j0])
+        act(hs("ss", h), b0, AF.Sign, H, [j0, K("col", CSG)], [K("ss", h)], col(CSG))
         s, ks = hs("ss", h), K("ss", h)
-        grp(a0, [(M("Id"), C), (M("Moh"), s)], [K("Id"), kC, K("Moh"), ks], [k0])
+        grp(a0, [(M("Ik1"), C), (M("Moh"), s)], [K("Ik1"), kC, K("Moh"), ks], [k0])
         e, ke = hs("es", NS * t + h), K("es", t, h)
         ts(e, a0, col(COH), -2048.0, A.add, A.max, H, [k0, K("col", COH)], [ke])
         send("e", e, hs("er", NS * t + h), [ke], t, h)
-        grp(a3, [(M("Mu"), s)], [K("Mu"), ks], [k3])
-        grp(a2, [(M("Im32"), hs("u16", h, o)), (M("I64"), hs("ob", h, o)), (M("Md"), s)], [K("Im32"), K("I64"), K("Md"), ku16, kob, ks], [k2])
-        grp(a1, [(M("BM"), T.c2050[:, 0:H]), (M("BM"), e)], [K("BM"), K("c2050"), ke], [k1])
-        vo = (NS * t + h) * (128 + H)
-        um, kum = T.vs[:, vo + 128:vo + 128 + H], K("um", t, h)
-        act(um, a3, AF.Sigmoid, H, [k3, K("col", CUM)], [kum, K("acc", h)], col(CUM), 128.0, 1.0, T.acc[:, 4 * h:4 * h + 1])
-        act(hs("dm", h), a2, AF.Sigmoid, H, [k2, K("col", CDM)], [K("dm", h)], col(CDM), -128.0)
-        q = H // 16
-        kv = slot(h, 0, 0, q)[0]
-        if OPT["kvm"]:
-            grp(a0, [(um, M("BM"))], [kum, K("BM")], [k0])
-            tt(hs("km", h), a0, M("Mk"), A.mult, H, [k0, K("Mk")], [K("km", h)])
-            grp(kv, [(M("nI"), T.basev[:, 0:q]), (hs("km", h), BO8)], [K("nI"), K("basev"), K("km", h), K("BM")], [k0], q)
+        dm, um = T.du[:, 256 * h:256 * h + H], T.du[:, 256 * h + H:256 * (h + 1)]
+        grp(b0, [(M("Mu"), s)], [K("Mu"), ks], [j0])
+        step(um, b0, H, [j0, K("col", TU), K("col", BU)], [K("um", h)], True, col(TU), col(BU))
+        grp(b1, [(T.RepP[0:80, h * H:(h + 1) * H], T.rem[0:80, :]), (M("Md"), s)], [K("RepP"), K("rem"), K("Md"), ks], [j1])
+        step(dm, b1, H, [j1, K("col", TD), K("col", BD)], [K("dm", h)], False, col(TD), col(BD))
+        n = 8 * R
+        kv = slot("a", h, 1, 0, n)[0]
+        grp(kv, [(T.one[0:1, :], T.rows[0:1, 16:16 + n]), (um, T.K16[:, 0:n])], [K("one"), K("rowv"), K("um", h), K("K16")], [k1], 64)
+        ts(hs("offv", h, n), kv, col(IP), None, A.add, None, n, [k1, K("col", IP)], [K("offv", h)])
+        v = hs("vs", NS * t + h, H * R)
+        gather(v, T.xa[:, h * XW:(h + 1) * XW], hs("offv", h, n), H * R,
+               [K("xa", h, c) for c in list(range(2048 // OPT["gs"])) + ["pad"]] + [K("offv", h)], [K("v", t, h)])
+        send("v", v, hs("vr", NS * t + h, H * R), [K("v", t, h)], t, h)
+        ec = slot("a", h, 0, 0, 8)[0]
+        grp(ec, [(T.one[0:31, :], T.cst[0:31, 0:8]), (e, T.BMe[:, 0:8])], [K("one"), K("cst", 0), ke, K("BMe")], [k0], 64)
+        tt(hs("fi", h, 8), ec, hs("uc", h, 8), A.mult, 8, [k0, K("uc")], [K("fi", h)])
+        ts(hs("fj", h, 8), hs("fi", h, 8), 5, 4095, A.arith_shift_right, A.bitwise_and, 8, [K("fi", h)], [K("fj", h)])
+        ts(T.fr[:, h * H + 120:(h + 1) * H], hs("fj", h, 8), -2048.0, None, A.add, None, 8, [K("fj", h)], [K("fr", h)])
+        grp(b0, [(T.cst[0:1, 384:512], T.one[0:1, :]), (M("SdI"), C), (M("R0a"), e)], [K("cst", 3), K("one"), K("SdI"), K("R0a"), kC, ke], [j0])
+        grp(b1, [(M("SuI"), C), (hs("fr", h), M("Id"))], [K("SuI"), K("Id"), kC, K("fr", h)], [j1])
+        tt(hs("Z3", h, 256), slot("b", h, 0, 0, 256)[0], hs("du", h, 256), A.mult, 256, [j0, j1, K("dm", h), K("um", h)], [K("Z3", h)])
+        zd, zu = T.Z3[:, 256 * h:256 * h + H], T.Z3[:, 256 * h + H:256 * (h + 1)]
+        N3, L3 = T.C3[:, 256 * h:256 * h + H], T.C3[:, 256 * h + H:256 * (h + 1)]
+        rd = [K("Id"), K("Idf"), kC, K("Z3", h)]
+        if OPT["both"]:
+            grp(a1, [(C, M("Id")), (zd, M("Idf"), 4), (zu, M("Idf"), 4)], rd, [k1])
+            grp(a0, [(M("Id"), C), (M("Idf"), zd, 4), (M("Idf"), zu, 4)], rd, [k0])
+            lin(hs("C3", h, 256), slot("a", h, 0, 0, 256)[0], 256, [k0, k1], [K("C3", h), K("L3", h)], 0.0, 1.0)
         else:
-            grp(kv, [(M("nI"), T.basev[:, 0:q])] + [(OH(j), T.vs[:, vo + 128 + j:vo + 128 + H:16]) for j in range(16)],
-                [K("nI"), K("basev"), K("Zs"), kum], [k0], q)
-        ts(T.offv[:, q * h:q * h + q], kv, -1.0, None, A.mult, None, q, [k0], [K("offv", h)])
-        mx = MAXP[t][h]
-        gather(T.vs[:, vo:vo + H] if mx else T.vg[:, h * 128:h * 128 + H], T.xa[:, h * XW:(h + 1) * XW], T.offv[:, q * h:q * h + q], H,
-               [K("xa", h, j) for j in list(range(NP)) + ["pad"]] + [K("offv", h)], [K("v", t, h) if mx else K("vg", h)])
-        if not mx:
-            flip([T.vg[:, h * 128:(h + 1) * 128]], T.vs[:, vo:vo + 128], 128, [K("vg", h)], [K("v", t, h)])
-        send("v", T.vs[:, vo:vo + 128 + H], T.vr[:, vo:vo + 128 + H], [K("v", t, h), kum], t, h)
-        tt(hs("fi", h), a1, hs("u16", h, o), A.mult, H, [k1, ku16], [K("fi", h)])
-        ts(hs("fj", h), hs("fi", h), 5, 4095, A.arith_shift_right, A.bitwise_and, H, [K("fi", h)], [K("fj", h)])
-        ts(hs("fr", h), hs("fj", h), -2048.0, None, A.add, None, H, [K("fj", h)], [K("fr", h)])
-        grp(a2, [(M("SdI"), C), (M("R0a"), T.c1920[:, 0:H]), (M("R0a"), e)], [K("SdI"), K("R0a"), K("c1920"), kC, ke], [k2])
-        tt(a2, a2, hs("dm", h), A.mult, H, [k2, K("dm", h)], [k2])
-        tt(hs("Ct", h), a2, C, A.add, H, [k2, kC], [K("Ct", h)])
-        grp(a3, [(M("SuI"), C), (M("R15"), hs("fr", h))], [K("SuI"), K("R15"), kC, K("fr", h)], [k3])
-        tt(a3, a3, um, A.mult, H, [k3, kum], [k3])
-        tt(hs("C3", h), a3, hs("Ct", h), A.add, H, [k3, K("Ct", h)], [K("C3", h)])
+            grp(a0, [(M("Id"), C), (M("Idf"), zd, 4), (M("Idf"), zu, 4)], rd, [k0])
+            lin(N3, a0, H, [k0], [K("C3", h)], 0.0, 1.0)
+            grp(b2, [(N3, M("Id"))], [K("C3", h), K("Id")], [j2])
+            lin(L3, b2, H, [j2], [K("L3", h)], 0.0, 1.0)
 
-    def xoffs(t):
-        o = (t % 2) * 256
-        r, kr = slot(0, 5, 0, 16)
-        grp(r, [(OH(j), T.u16[:, o + j:o + 256:16]) for j in range(16)], [K("Zs")] + [K("u16", t % 2, h) for h in range(NS)], [kr], 16)
-        cp(T.xi[:], r, 16, [kr], [K("xi")])
-        ts(T.xj[:], T.xi[:], 4, 15, A.arith_shift_right, A.bitwise_and, 16, [K("xi")], [K("xj")])
-        tt(T.xk[:], T.xj[:], T.basex[:], A.add, 16, [K("xj"), K("basex")], [K("xk")])
-        cp(T.offx[:], T.xk[:], 16, [K("xk")], [K("offx")])
-        gather(T.Xo[:], T["X%d" % t][:, 0:4096], T.offx[:], 256, XK[t] + [K("offx")], [K("Xo")])
-
-    def xnew(h):
-        r, kr = slot(h, 6)
-        grp(r, [(M("I4"), hs("Xo", h)), (M("Id"), hs("yb", h))], [K("I4"), K("Id"), K("Xo"), K("yb", h)], [kr])
-        lin(hs("xn", h), r, H, [kr], [K("xn", h)], 167.5 + 1.0 / 16, 1.0 / 8)
-
-    def xscatter(t):
-        return vec(lambda: V.tensor_tensor(T["X%d" % (t + 1)][:, 0:4096].indirect(T.offx[:]), T.xn[:], T.cm192[:], A.add), 256,
-                   [K("xn", h) for h in range(NS)] + [K("cm192"), K("offx")], XK[t + 1], SC)
+    def renew(t):
+        kyb = [K("yb", h) for h in range(NS)]
+        p, kb, B = loan("pD")
+        grp(B(0, 256), [(M("I4"), T.Xo[:]), (M("Id"), T.yb[:])], [K("I4"), K("Id"), K("Xo")] + kyb, [kb], 256)
+        give(p, "pD", lin(T.xn[:], B(0, 256), 256, [kb], [K("xn")], 167.5 + 1.0 / 16, 1.0 / 8))
+        vec(lambda: V.tensor_tensor(T["X%d" % (t + 1)][:, 0:4096].indirect(T.offx[:]), T.xn[:], T.cm192[:], A.add), 256,
+            [K("xn"), K("cm192"), K("offx")], XK[t + 1], SC)
 
     def count():
-        r, kr = slot(NS - 1, 5, 0, 1)
-        grp(r, [(M("Rall"), T.acc[:, 4 * h:4 * h + 1], 4) for h in range(NS)], [K("Rall")] + [K("acc", h) for h in range(NS)], [kr], 1)
-        ts(col(CQ), r, 402653184.0, -402653184.0 - 8388608.0, A.add, A.add, 1, [kr], [K("col", CQ)])
+        p, kb, B = loan("pD")
+        grp(B(0, 128), [(T.du[:, 256 * h + H:256 * (h + 1)], M("R15")) for h in range(NS)], [K("R15")] + [K("um", h) for h in range(NS)], [kb])
+        give(p, "pD", lin(M("cnt"), B(0, 128), 128, [kb], [K("cnt")], 16.0, 1.0))
 
     def step4(t, h):
-        (a0, k0), (a1, k1), (a2, k2), (a3, k3) = [slot(h, s) for s in range(4)]
+        (a0, k0), (a1, k1), (a2, k2) = [slot("a", h, s) for s in range(3)]
+        (b0, j0), (b1, j1), (b2, j2) = [slot("b", h, s) for s in range(3)]
         e, ke = hs("er", NS * t + h), K("er", t, h)
-        C, kC = hs("C3", h), K("C3", h)
-        vo = (NS * t + h) * (128 + H)
-        kv = K("vr", t, h)
-        c19 = T.c1920[:, 0:H]
-        mm([(a0, M("BM"), c19, True, False, H), (a0, M("BM"), e, False, True, H),
-            (a1, M("B3232"), c19, True, False, H), (a1, M("B3232"), e, False, False, H), (a1, M("I2080"), C, False, True, H)],
-           [K("BM"), K("c1920"), K("I2080"), K("B3232"), kC, ke], [k0, k1])
-        tt(hs("pf", h), a0, C, A.mult, H, [k0, kC], [K("pf", h)])
-        tt(hs("pi", h), a1, hs("pf", h), A.add, H, [k1, K("pf", h)], [K("pi", h)])
-        point(h, "off2")
-        e, ke = hs("se", h), K("se", h)
-        cp(e, a0, H, [k0], [ke])
-        if not OPT["z16"]:
-            grp(a2, [(M("Id"), C), (M("nI"), e)], [K("Id"), K("nI"), kC, ke], [k2])
-        o = h * 16 * H
-        for j in range(NP):
-            gather(T.xb[:, o + j * 512:o + (j + 1) * 512], T["X%d" % t][:, 0:4096], T.off2[:, h * H + j * 32:h * H + (j + 1) * 32], 512,
-                   XK[t] + [K("off2", h)], [K("xb", h, j)])
-        def extra(a, b):
-            return [(T.EX8[0:8, :], T.ths[0:8, h * H + a:h * H + b]), (M("Mco"), T.vr[:, vo + 128 + a:vo + 128 + b])]
-
-        xrd = [K("EX8"), K("ths"), K("Mco"), kv]
-        if MAXP[t][h]:
-            v = T.vr[:, vo:vo + H]
-            for j in range(NP):
-                vec((lambda j: lambda: V.tensor_tensor(T.ad[:, o + j * 512:o + (j + 1) * 512], v.indirect(T.vl[:, j * 32:(j + 1) * 32]),
-                                                       T.xb[:, o + j * 512:o + (j + 1) * 512], A.max))(j), 512,
-                    [kv, K("vl"), K("xb", h, j)], [K("ad", h, j)], GA)
-            mm([(a0, v, M("nBM"), True, False, H)]
-               + [(slot(h, 0, k, H, 16)[0], T.xb[:, o + k:o + 16 * H:16], T.nBM[:, 0::16], False, False, 64) for k in range(16)],
-               [K("xb", h, j) for j in range(NP)] + [K("nBM"), kv, k2], [k0])
-            mm([(slot(h, 0, k, H, 16)[0], T.ad[:, o + k:o + 16 * H:16], T.B2[:, 0:8], False, k == 15, 64) for k in range(16)],
-               [K("ad", h, j) for j in range(NP)] + [K("B2")], [k0])
-            lin(hs("lk", h), a0, H, [k0], [K("lk", h)], 0.0, 1.0)
-            grp(a0, extra(0, H) + [(hs("lk", h), M("Id"))], xrd + [K("lk", h), K("Id")], [k0])
-        else:
-            for j in range(NP):
-                wide([(0, 512, T.vr[0:H, vo:vo + 128], T.Sel[0:H, j * 512:(j + 1) * 512], True, False),
-                      (0, 512, M("I8"), T.xb[:, o + j * 512:o + (j + 1) * 512], False, True)], [K("Sel"), K("I8"), kv, K("xb", h, j)],
-                     T.ad[:, o + j * 512:o + (j + 1) * 512], AF.Abs, 0.0, 0.125, [K("ad", h, j)])
-            reduce16(h, 0, "ad", OPT["lkd"], extra, xrd)
-        step(hs("hit", h), a0, H, [k0, K("col", CHT)], [K("hit", h)], col(CHT), -256.0)
-        grp(a3, [(M("Mst"), hs("hit", h))], [K("Mst"), K("hit", h)], [k3])
-        nn, kn = slot(h, 7)
-        if OPT["z16"]:
-            step(a2, a3, H, [k3], [k2], -128.0, 256.0)
-            tt(hs("Za", h), a2, C, A.mult, H, [k2, kC], [K("Za", h)])
-            tt(hs("Zb", h), a2, e, A.mult, H, [k2, ke], [K("Zb", h)])
-            grp(nn, [(M("Sd"), C), (M("R0"), e), (M("nSdI"), hs("Za", h)), (M("SdI"), hs("Zb", h))],
-                [K("Sd"), K("R0"), K("SdI"), K("nSdI"), kC, ke, K("Za", h), K("Zb", h)], [kn])
-        else:
-            step(hs("stay", h), a3, H, [k3], [K("stay", h)], -128.0, 256.0)
-            tt(hs("Z4", h), a2, hs("stay", h), A.mult, H, [k2, K("stay", h)], [K("Z4", h)])
-            grp(nn, [(M("Sd"), C), (M("R0"), e), (M("ImSd"), hs("Z4", h), 4)], [K("Sd"), K("R0"), K("ImSd"), kC, ke, K("Z4", h)], [kn])
+        N3, L3 = T.C3[:, 256 * h:256 * h + H], T.C3[:, 256 * h + H:256 * (h + 1)]
+        mm([(a0, T.one[0:31, :], T.cst[0:31, 0:128], H, (True, False)), (a0, e, M("BMe"), H, (False, True)),
+            (a1, T.one[0:1, :], T.cst[0:1, 128:256], H, (True, False)), (a1, e, M("B3232"), H, (False, True))],
+           [K("one"), K("cst", 0), K("cst", 1), K("BMe"), K("B3232"), ke], [k0, k1])
+        point(h, a0, L3, a1, [k0, K("L3", h)], [k1], "off2")
+        grp(b2, [(T.one[0:1, :], T.cst[0:1, 256:384]), (M("Id"), N3), (M("nBMe"), e)], [K("one"), K("cst", 2), K("Id"), K("nBMe"), K("C3", h), ke], [j2])
+        o, w = h * 2048, H * R
+        v, kv = hs("vr", NS * t + h, w), K("vr", t, h)
+        X, F = T["X%d" % t][:, 0:4096], 2048 - 512 * OPT["ua"]
+        for n in range(F // w):
+            vec((lambda n: lambda: V.tensor_tensor(T.dd[:, o + n * w:o + (n + 1) * w],
+                                                   X.indirect(T.off2[:, h * H + 8 * R * n:h * H + 8 * R * (n + 1)]), v, A.subtract))(n),
+                w, XK[t] + [K("off2", h), kv], [K("dd", h, n)], GA)
+        krl = []
+        for a in range(0, F, RL):
+            b = min(a + RL, F)
+            krl.append(K("rl", h, a))
+            i = ts(T.rl[:, o + a:o + b], T.dd[:, o + a:o + b], 0.0, None, A.max, None, b - a, [K("dd", h, n) for n in range(a // w, b // w)], krl[-1:], 0.5)
+            also(i, "A", (lambda a, b: lambda: S.activation(T.rl[:, a:b], T.dd[:, a:b], AF.Relu))(o + a, o + b), b - a)
+        for a in range(F, 2048, 512):
+            gather(T.dd[:, o + a:o + a + 512], X, T.off2[:, h * H + a // 16:h * H + a // 16 + 32], 512, XK[t] + [K("off2", h)], [K("xb", h, a)])
+            p, kb, B = loan("pD")
+            mm([(B(0, 512), M("Id"), T.dd[:, o + a:o + a + 512], 512)] + [(B(c, c + w), M("nI"), v, w) for c in range(0, 512, w)],
+               [], [kb], [[K("Id"), K("xb", h, a)]] + [[K("nI"), kv]] * (512 // w))
+            krl.append(K("rl", h, a))
+            give(p, "pD", act(T.rl[:, o + a:o + a + 512], B(0, 512), AF.Abs, 512, [kb], krl[-1:], 0.0, 0.5))
+        i = mm([(b0, T.RepN[0:16, h * H:(h + 1) * H], T.thT[0:16, :], H, (True, False)), (b0, M("Mco"), e, H, (False, False))]
+               + [(T[j0[0]][0:F // 16, i:H:16], T.dd[:, o + i:o + F:16], BOn, 64, (False, False)) for i in range(16)],
+               [K("dd", h, n) for n in range(F // w)] + [K("RepN"), K("thT"), K("Mco"), ke, K("b8", 2)], [j0])
+        i = mm([(slot("b", h, 0, i, H, 16)[0], T.rl[:, o + i:o + 2048:16], BO2, 64, (False, i == 15)) for i in range(16)],
+               krl + [K("b8", 1)], [j0])
+        step(hs("hit", h), b0, H, [j0, K("col", TH), K("col", BH)], [K("hit", h)], False, col(TH), col(BH))
+        grp(a0, [(M("Mst"), hs("hit", h))], [K("Mst"), K("hit", h)], [k0])
+        step(hs("mv", h), a0, H, [k0], [K("mv", h)], False, 0.5, 128.0)
+        tt(hs("Z4", h), b2, hs("mv", h), A.mult, H, [j2, K("mv", h)], [K("Z4", h)])
         if t < RO - 1:
-            cp(hs("Cc", h), nn, H, [kn], [K("Cc", h)])
+            grp(a2, [(N3, M("I1")), (hs("Z4", h), M("SdI1f"), 4)], [K("C3", h), K("I1"), K("SdI1f"), K("Z4", h)], [k2])
+        grp(b1, [(M("Id"), N3), (M("SdIf"), hs("Z4", h), 4)], [K("C3", h), K("Id"), K("SdIf"), K("Z4", h)], [j1])
+        if t < RO - 1:
+            lin(hs("Cc", h), b1, H, [j1], [K("Cc", h)], 0.0, 1.0)
         else:
-            lin(hs("yco", h), nn, H, [kn], [K("yco", h)], 2048.0, 1.0)
-            dma("S", "oyc%d" % h, T.yc[:, h * H:(h + 1) * H], hs("yco", h), 2500, [K("yco", h)], [])
+            lin(hs("yco", h), b1, H, [j1], [K("yco", h)], 2048.0, 1.0)
+            for j, q in enumerate("SA"):
+                dma(q, "oyc%d%d" % (h, j), [(T.yc[16 * u:16 * u + 16, h * H:(h + 1) * H], T.yco[:, h * H + 16 * u:h * H + 16 * u + 16]) for u in range(j, 8, 2)],
+                    3500, [K("yco", h)], [])
 
+    lin(T.yb[:], T.y0s[:], 256, [K("y0s")], [K("yb", h) for h in range(NS)], 192.0, 1.0, 0.5)
+    uphase(0)
     for h in range(NS):
-        ts(hs("yb", h), hs("y0s", h), 192.0, None, A.add, None, H, [K("y0s")], [K("yb", h)], 0.5)
-        ts(hs("Cc", h), hs("c0s", h), -2048.0, None, A.add, None, H, [K("c0s")], [K("Cc", h)])
-        nn, kn = slot(h, 7)
-        grp(nn, [(M("Id"), hs("Cc", h))], [K("Id"), K("Cc", h)], [kn])
-        uphase(0, h)
+        cur[0] = h
+        ts(hs("Cc", h), hs("c0s", h), -2048.0, None, A.add, None, H, [K("c0s", h)], [K("Cc", h)])
+        nn, kn = slot("a", h, 2)
+        grp(nn, [(hs("Cc", h), M("I1"))], [K("I1"), K("Cc", h)], [kn])
         qphase(h)
-    dma("S", "x1", T.X1[:], T.x0[:], 6000, [], XK[1], [last_w[k] for k in XK[0]])
+    cur[0] = 0
+    dma("S", "x1", [(T.X1[:], T.x0[:])], 6000, [], XK[1], [ix])
     stflip(0)
     for t in range(RO):
-        xoffs(t)
+        cur[1] = t
         for h in range(NS):
             cur[0] = h
             step12(t, h)
             step3(t, h)
-            xnew(h)
-            if t < RO - 1:
-                uphase(t + 1, h)
         cur[0] = 0
+        renew(t)
         if t < RO - 1:
             stflip(t + 1)
-        xscatter(t)
-        if t < RO - 1:
             count()
+            uphase(t + 1)
             for h in range(NS):
                 qphase(h)
+            dma("S", "x%d" % (t + 2), [(T["X%d" % (t + 2)][:], T["X%d" % (t + 1)][:])], 6000, XK[t + 1], XK[t + 2], [last_w[K("vr", t, NS - 1)]])
         else:
-            dma("S", "oyx", T.yx[:], T.X4[:], 6000, XK[4], [])
-            ts(T.yyo[:], T.yb[:], -192.0, None, A.add, None, 256, [K("yb", h) for h in range(NS)], [K("yyo")], 0.5)
-            dma("S", "oyy", T.yy[:], T.yyo[:], 2500, [K("yyo")], [])
-        if t < RO - 1:
-            dma("S", "x%d" % (t + 2), T["X%d" % (t + 2)][:], T["X%d" % (t + 1)][:], 6000, XK[t + 1], XK[t + 2], [last_w[K("vr", t, NS - 1)]])
+            dma("S", "oyx", [(T.yx[:], T.X4[:])], 6000, XK[4], [], [last_w[K("vr", t, NS - 1)]])
+            lin(T.yyo[:], T.yb[:], 256, [K("yb", h) for h in range(NS)], [K("yyo")], -192.0, 1.0, 0.5)
+            dma("S", "oyy", [(T.yy[:], T.yyo[:])], 2500, [K("yyo")], [])
         for h in range(NS):
             cur[0] = h
             step4(t, h)
         cur[0] = 0
-    for o in ops:
-        if "A" in o["alt"]:
-            o["alt"]["A"] = (o["alt"]["A"][0], o["alt"]["A"][1] + FA)
     return ops
-
-
-def tight(ops, plan, lat):
-    _, st = replay(ops, plan, lat)
-    eng, deps, prev, last = {}, {}, {}, {}
-    for i, e, d, _ in plan:
-        eng[i], deps[i], prev[i], last[e] = e, d, last.get(e), i
-    fin = {i: st[i] + ops[i]["alt"][eng[i]][1] for i in st}
-    i, out = max(fin, key=fin.get), []
-    while i is not None:
-        p = None
-        for d in deps[i]:
-            if abs(fin[d] + (0.0 if eng[i] == "P" == eng[d] else lat) - st[i]) < 1:
-                p = d
-        if p is None and st[i] > 1:
-            p = prev[i]
-            out.append((i, p))
-        elif p is not None and p not in ops[i]["deps"]:
-            out.append((i, p))
-        i = p
-    return out
-
-
-def nudge(ops, adj, seed, path):
-    r = [seed * 7919 % 2147483648]
-
-    def rnd():
-        r[0] = (r[0] * 1103515245 + 12345) % 2147483648
-        return r[0] / 2147483648.0
-
-    rnd()
-    n = len(ops)
-    pr, le, win = list(adj[0]), list(adj[1]), list(adj[2])
-    kind = int(rnd() * 8)
-    a = int(rnd() * n)
-    if kind >= 4:
-        a, b = path[int(rnd() * len(path))]
-        d = 200.0 + 2500.0 * rnd() ** 2
-        if rnd() < 0.35 and b is not None:
-            if rnd() < 0.5:
-                pr[b] -= d
-            else:
-                le[b] += d * (1 if rnd() < 0.5 else -1)
-            return pr, le, win
-        who, edge = {a}, [a]
-        for _ in range(int(rnd() * 5)):
-            edge = [j for i in edge for j in ops[i]["deps"] if j not in who]
-            who.update(edge)
-        for i in who:
-            pr[i] += d
-        if rnd() < 0.3:
-            win[a] += 300.0 * rnd()
-        return pr, le, win
-    if kind % 4 == 0:
-        who = range(a, min(n, a + 1 + int(rnd() * 40)))
-    elif kind % 4 == 1:
-        who = [i for i in range(n) if ops[i]["wr"][:1] == ops[a]["wr"][:1]]
-    elif kind % 4 == 2:
-        who = [i for i in range(n) if ops[i]["wr"] and ops[a]["wr"] and ops[i]["wr"][0][0] == ops[a]["wr"][0][0]]
-    else:
-        who = [i for i in range(max(0, a - 60), min(n, a + 60)) if rnd() < 0.15]
-    d = rnd() - 0.5
-    what = rnd()
-    for i in who:
-        if what < 0.55:
-            pr[i] += 5000.0 * d
-        elif what < 0.8:
-            le[i] += 2000.0 * d
-        else:
-            win[i] = max(0.0, win[i] + 800.0 * d)
-    return pr, le, win
 
 
 def schedule(ops, lat, adj):
@@ -640,7 +578,7 @@ def schedule(ops, lat, adj):
     fin, eng, plan = [0.0] * n, [None] * n, []
     bank = {b: {} for b in ("pa0", "pb0", "pa1", "pb1")}
     pool = {b: -1 for b in ("pT0", "pT1", "pD0", "pD1")}
-    held = {}
+    held, shut = {}, set()
 
     def enter(i):
         o = ops[i]
@@ -652,6 +590,8 @@ def schedule(ops, lat, adj):
         st, t0 = [], 1e18
         for x in ready:
             i, al, bs, take = x
+            if shut and "P" in ops[i]["alt"] and not ops[i]["in"] and shut.intersection(bs):
+                continue
             best = None
             for e, c, s in al:
                 if free[e] > s:
@@ -688,10 +628,12 @@ def schedule(ops, lat, adj):
             held[i] = got
         if "give" in o:
             pool[held[o["give"]]] = i
+        if e == "P":
+            (shut.update if o["open"] else shut.difference_update)(o["banks"])
         fin[i] = s + c
         eng[i] = e
         if e != "R":
-            free[e] = s + 60.0 if e == "S" else fin[i]
+            free[e] = s + (o["occ"] or c)
         plan.append((i, e, deps, got))
         ready.remove(x)
         for j in succ[i]:
@@ -701,33 +643,193 @@ def schedule(ops, lat, adj):
     return plan
 
 
+def ordered(ops, lat, key, engs):
+    n = len(ops)
+    succ = [[] for _ in range(n)]
+    left = [len(o["deps"]) for o in ops]
+    for i, o in enumerate(ops):
+        for d in o["deps"]:
+            succ[d].append(i)
+    free = {e: 0.0 for e in "PDAGSR"}
+    fin, plan = [0.0] * n, []
+    bank = {b: {} for b in ("pa0", "pb0", "pa1", "pb1")}
+    pool = {b: -1 for b in ("pT0", "pT1", "pD0", "pD1")}
+    held, shut = {}, set()
+    ready = sorted((key[i], i) for i in range(n) if left[i] == 0)
+    while ready:
+        for x in ready:
+            i = x[1]
+            o, e, got = ops[i], engs[i], None
+            if shut and e == "P" and not o["in"] and shut.intersection(o["banks"]):
+                continue
+            if "take" in o:
+                av = [(fin[pool[b]] if pool[b] >= 0 else 0.0, b) for b in o["take"] if pool[b] is not None]
+                if not av:
+                    continue
+                got = min(av)[1]
+            break
+        ready.remove(x)
+        deps = set(o["deps"])
+        for b in o["banks"]:
+            deps.update(j for e2, j in bank[b].items() if e2 != e)
+            bank[b][e] = i
+        if got:
+            if pool[got] >= 0:
+                deps.add(pool[got])
+            pool[got] = None
+            held[i] = got
+        if "give" in o:
+            pool[held[o["give"]]] = i
+        if e == "P":
+            (shut.update if o["open"] else shut.difference_update)(o["banks"])
+        s = max([free[e]] + [fin[d] + (0.0 if e == "P" == engs[d] else lat) for d in deps])
+        fin[i] = s + o["alt"][e][1]
+        if e != "R":
+            free[e] = s + (o["occ"] or o["alt"][e][1])
+        plan.append((i, e, deps, got))
+        for j in succ[i]:
+            left[j] -= 1
+            if left[j] == 0:
+                ready.append((key[j], j))
+        ready.sort()
+    return plan
+
+
+def packed(ops, lat, adj):
+    n = len(ops)
+    succ = [[] for _ in range(n)]
+    left = [len(o["deps"]) for o in ops]
+    for i, o in enumerate(ops):
+        for d in o["deps"]:
+            succ[d].append(i)
+    pri = [0.0] * n
+    for i in range(n - 1, -1, -1):
+        pri[i] = min(a[1] for a in ops[i]["alt"].values()) + max([pri[j] + lat for j in succ[i]] + [0.0])
+    key = [-p - q - (OPT["short"] if min(a[1] for a in o["alt"].values()) < 330 else 0.0) for p, q, o in zip(pri, adj[0], ops)]
+    lean = adj[1]
+    busy = {e: [] for e in "PDAGS"}
+    use = {b: [] for b in ("pa0", "pb0", "pa1", "pb1")}
+    pool = {b: 0.0 for b in ("pT0", "pT1", "pD0", "pD1")}
+    held, shut, began = {}, set(), {}
+    st, fin, eng = [0.0] * n, [0.0] * n, [None] * n
+    ready = sorted((key[i], i) for i in range(n) if left[i] == 0)
+
+    def fit(i, e, s):
+        o = ops[i]
+        c = o["alt"][e][1]
+        w = o["occ"] or c
+        while True:
+            s0 = s
+            if e != "R":
+                for a, b in busy[e]:
+                    if a >= s + w:
+                        break
+                    if b > s:
+                        s = b
+            for k in o["banks"]:
+                for a, b, e2 in use[k][-24:]:
+                    if e2 != e and b > s and a < s + c + lat and not (e2 == "L" and (e != "P" or o["in"])):
+                        s = b
+            if s == s0:
+                return s
+
+    while ready:
+        for x in ready:
+            i = x[1]
+            o, got = ops[i], None
+            if shut and "P" in o["alt"] and not o["in"] and shut.intersection(o["banks"]):
+                continue
+            if "take" in o:
+                av = [(pool[b], b) for b in o["take"] if pool[b] is not None]
+                if not av:
+                    continue
+                got = min(av)
+            break
+        ready.remove(x)
+        best = None
+        for e, a in o["alt"].items():
+            s = max([fin[d] + lat if e != "P" or eng[d] != "P" else st[d] + ops[d]["occ"] for d in o["deps"]] + [got[0] if got else 0.0])
+            if e == "P" and o["open"] and not o["in"]:
+                s = max([s] + [b - lat for k in o["banks"] for a2, b, e2 in use[k][-24:] if e2 == "P"])
+            s = fit(i, e, s)
+            v = s + a[1] + (lean[i] if e == "D" else 0.0)
+            if best is None or v < best[0]:
+                best = (v, s, e, a[1])
+        v, s, e, c = best
+        st[i], fin[i], eng[i] = s, s + c, e
+        if e != "R":
+            busy[e].append((s, s + (o["occ"] or c)))
+            busy[e].sort()
+            if len(busy[e]) > 60:
+                busy[e][0:2] = [(0.0, busy[e][1][1])]
+        for k in o["banks"]:
+            use[k].append((s, s + c + lat, e))
+            if e == "P" and o["open"] and not o["in"]:
+                began[k] = s
+            if e == "P" and o["in"] and not o["open"]:
+                use[k].append((began[k], s + o["occ"], "L"))
+        if got:
+            pool[got[1]] = None
+            held[i] = got[1]
+        if "give" in o:
+            pool[held[o["give"]]] = fin[i] + lat
+        if e == "P":
+            (shut.update if o["open"] else shut.difference_update)(o["banks"])
+        for j in succ[i]:
+            left[j] -= 1
+            if left[j] == 0:
+                ready.append((key[j], j))
+        ready.sort()
+    return ordered(ops, lat, st, eng)
+
+
+def keyed(ops):
+    lab = labels(ops)
+    return ([WHEN[k][0] + PERIOD * max(o["t"], 0) for k, o in zip(lab, ops)], [WHEN[k][1] for k in lab])
+
+
 def replay(ops, plan, lat):
     free, fin, eng, st = {}, {}, {}, {}
     for i, e, deps, _ in plan:
         s = max([free.get(e, 0.0)] + [fin[d] + (0.0 if e == "P" == eng[d] else lat) for d in deps])
         st[i], fin[i], eng[i] = s, s + ops[i]["alt"][e][1], e
         if e != "R":
-            free[e] = s + 60.0 if e == "S" else fin[i]
+            free[e] = s + (ops[i]["occ"] or ops[i]["alt"][e][1])
     return max(fin.values()), st
 
 
 def choose(g, T, topo, core):
-    sets = [build(g, T, topo, core, c) for c in COSTS]
+    ops = build(g, T, topo, core, COSTS[0])
     if "plan" not in MEMO:
-        ops = sets[0]
-        n = len(ops)
-        adj = ([-OPT["stag"] * o["half"] for o in ops], [OPT["lean"] + OPT["lam"] * o["alt"]["D"][1] if "D" in o["alt"] else 0.0 for o in ops], [OPT["win"]] * n)
-        best, kept, path = None, [], None
-        for s in [None] + NUDGES + list(OPT["seeds"]):
-            a = adj if s is None else nudge(ops, adj, s, path)
-            plan = schedule(ops, COSTS[0][5], a)
-            ts = [replay(o, plan, c[5])[0] for o, c in zip(sets, COSTS)]
-            v = sum(math.log(t) * w for t, w in zip(ts, WEIGH))
-            if best is None or v < best[0]:
-                best, adj, path = (v, plan, ts), a, tight(ops, plan, COSTS[0][5])
-                kept += [s] if s is not None else []
-        MEMO["plan"] = best + (kept,)
-    return sets[0], MEMO["plan"][1]
+        MEMO["plan"] = ordered(ops, COSTS[0][5], *keyed(ops)) if WHEN else schedule(ops, COSTS[0][5], adjust(ops))
+    return ops, MEMO["plan"]
+
+
+def labels(ops):
+    out, seen = [], {}
+    giver = {o["give"]: o for o in ops if "give" in o}
+    for i, o in enumerate(ops):
+        k = o["wr"][-1] if o["wr"] else ("send",) + ops[i + 1]["wr"][0] if o["sem"] == "sent" else (o["sem"],)
+        pre = "_" * (o["t"] < 0)
+        if k[0] == "loan":
+            k, pre = giver[k[1]]["wr"][-1], pre + "P"
+        if k[0] in ("es", "er", "v", "vr", "send", "stT"):
+            k = k[:-2] + k[-1:] if k[0] != "stT" else k[:1]
+        if k[0][0] == "X" and k[0] != "Xo":
+            k = ("X" + list(o["alt"])[0],)
+        if k[0] in ("pa0", "pa1", "pb0", "pb1"):
+            k = k + (o["tag"],)
+        k = pre + "".join(str(x) for x in k)
+        seen[o["t"], k] = seen.get((o["t"], k), 0) + 1
+        out.append(k + " bcdefghij"[seen[o["t"], k] - 1].strip())
+    return out
+
+
+def adjust(ops):
+    lab = labels(ops)
+    return ([AHEAD.get(k, 0.0) - OPT["stag"] * o["half"] for k, o in zip(lab, ops)],
+            [LEAN.get(k, 0.0) + OPT["lean"] + OPT["lam"] * o["alt"]["D"][1] if "D" in o["alt"] else 0.0 for k, o in zip(lab, ops)],
+            [OPT["win"] + WAIT.get(k, 0.0) for k in lab])
 
 
 def emit(g, T, ops, plan):
@@ -761,7 +863,7 @@ def emit(g, T, ops, plan):
         fns = o["alt"][e][0]
         for f in fns:
             ins = f()
-            if f is fns[-1] or OPT["each"]:
+            if f is fns[-1] or o["inc"] == 16:
                 if sem != "sent":
                     ins.then_inc(T.sem[sem], o["inc"])
                 total[sem] = total.get(sem, 0) + o["inc"]

import math
from concourse.mybir import AluOpType, ActivationFunctionType

NR, RO, NS, H = 4, 4, 2, 128
OPT = {"R": 2, "tg": 2, "rl": 512, "both": False, "stag": 3000.0, "lam": 0.1, "lean": 100.0, "win": 0.0, "x0q": "A", "ua": 1, "pmax": 9999, "gs": 512}
R = OPT["R"]
BF, F16, F32, I32, U16 = "bfloat16", "float16", "float32", "int32", "uint16"
MATS = ["val", "bq", "val1", "val2", "bq2", "dk", "B", "B2", "Id", "Ik1", "I1", "I4", "nI", "BMe", "nBMe", "B3232", "R0a", "Cm", "Mdl", "Md", "Mu", "Moh",
        "Mst", "SdI", "SuI", "Mco", "R15", "Wb", "tA", "tB", "tC", "tD", "one", "c32", "cnt", "offt", "thT", "K16", "c192"]
SCRATCH = {m: ("sbuf", [128, 128], BF) for m in MATS}
XW = 2048 + 16
SCRATCH.update({
    "Idf": ("sbuf", [128, 128], F32), "SdIf": ("sbuf", [128, 128], F32), "SdI1f": ("sbuf", [128, 128], F32),
    "Sel": ("sbuf", [128, 2048], BF), "Rep": ("sbuf", [128, 256], BF), "RepN": ("sbuf", [128, 256], BF), "cst": ("sbuf", [128, 512], BF),
    "RepP": ("sbuf", [128, 256], BF), "src": ("sbuf", [128, 1024], BF), "b8": ("sbuf", [128, 32], BF), "rows": ("sbuf", [128, 64], BF),
    "cm192": ("sbuf", [128, 256], BF), "col": ("sbuf", [128, 48], F32), "coli": ("sbuf", [128, 8], I32), "wcol": ("sbuf", [128, 8], BF),
    "c0s": ("sbuf", [128, 256], I32), "y0s": ("sbuf", [128, 256], BF), "sts": ("sbuf", [128, 1024], BF), "stT": ("sbuf", [128, 1024], BF),
    "X0": ("sbuf", [128, 4096], BF), "X1": ("sbuf", [128, 4096], BF), "X2": ("sbuf", [128, 4096], BF),
    "X3": ("sbuf", [128, 4096], BF), "X4": ("sbuf", [128, 4096], BF),
    "xa": ("sbuf", [128, 2 * XW], BF), "xT": ("sbuf", [128, 4096], BF), "ind": ("sbuf", [128, 4096], BF),
    "dd": ("sbuf", [128, 4096], BF), "rl": ("sbuf", [128, 4096], BF),
    "Cc": ("sbuf", [128, 256], F16), "C3": ("sbuf", [128, 512], F16), "fr": ("sbuf", [128, 256], F16),
    "yb": ("sbuf", [128, 256], BF), "mm": ("sbuf", [128, 256], F32), "ur": ("sbuf", [128, 128], F32), "rem": ("sbuf", [128, 128], F16),
    "uc": ("sbuf", [128, 16], F32), "pf": ("sbuf", [128, 256], F32), "pi": ("sbuf", [128, 256], I32), "pj": ("sbuf", [128, 256], I32),
    "fi": ("sbuf", [128, 16], I32), "fj": ("sbuf", [128, 16], I32),
    "off1": ("sbuf", [128, 256], U16), "off2": ("sbuf", [128, 256], U16), "offv": ("sbuf", [128, 64], U16), "offx": ("sbuf", [128, 16], U16),
    "Xo": ("sbuf", [128, 256], BF), "xn": ("sbuf", [128, 256], BF), "ww": ("sbuf", [128, 256], BF), "ss": ("sbuf", [128, 256], BF),
    "du": ("sbuf", [128, 512], BF), "Z3": ("sbuf", [128, 512], F32), "hit": ("sbuf", [128, 256], BF), "mv": ("sbuf", [128, 256], BF),
    "Z4": ("sbuf", [128, 256], F32), "es": ("sbuf", [128, 1024], F16), "er": ("sbuf", [128, 1024], F16),
    "vs": ("sbuf", [128, 1024 * R], BF), "vr": ("sbuf", [128, 1024 * R], BF),
    "yco": ("sbuf", [128, 256], F32), "yyo": ("sbuf", [128, 256], BF),
    "pT0": ("psum", [128, 1024], BF), "pT1": ("psum", [128, 1024], BF),
    "pD0": ("psum", [128, 512], F32), "pD1": ("psum", [128, 512], F32),
    "pa0": ("psum", [128, 512], F32), "pb0": ("psum", [128, 512], F32),
    "pa1": ("psum", [128, 512], F32), "pb1": ("psum", [128, 512], F32),
})
DMAS = ["w", "y0", "c00", "c01", "x0", "st0", "st1", "th", "x1", "x2", "x3", "x4", "oyx", "oyc00", "oyc01", "oyc10", "oyc11", "oyy"]
SEMAPHORES = (["qP", "qD", "qA", "qG", "sent"] + ["d" + n for n in DMAS]
              + ["a%s%d%d" % (k, t, h) for k in "ev" for t in range(RO) for h in range(NS)])

AHEAD = {'Pind01': 12000, 'Pind12': -7000, 'Prem': 9800, 'XD': 1000, 'Xo': 5300, 'cnt': -7300, 'col29': -5900, 'dd12': 6300, 'dd13': 3300, 'dd14': 6600, 'dm1': -300, 'fr0': 21000, 'ind00': 17000, 'ind02': 600, 'mm': -7700, 'off21': -5300, 'offv0': 1700, 'pa00BMe': 8700, 'pa00Z3': -23400, 'pa00hit': -13900, 'pa00ss': 300, 'pa01K16': 6000, 'pa02Z4': 3000, 'pa03Cm': -27700, 'pa10BMe': -5100, 'pa10ss': 9000, 'pb00ss': 1700, 'pb02er': -3700, 'pb03cnt': 1600, 'pb10ww': -26000, 'pb11Z4': -11700, 'pb11fr': 20600, 'pb13cnt': 16300, 'pf0': 3000, 'pf1': 9000, 'rem': 300, 'rl11536': 12400, 'sender1': -41300, 'tA': 15700, 'xT12': 7600, 'xa00': 9700, 'xa02': 9300, 'xa10': 9700, 'xa12': -6400, 'xb11536': 26300, 'xn': -9600}
LEAN = {'Cc1': 2600, 'Xo': -1700, 'cnt': -5000, 'dm0': 5300, 'dm1': -500, 'hit1': -200, 'ind01': 8400, 'ind10': 2200, 'mm': -600, 'mv1': -300, 'v0': 7600, 'xa01': -2100, 'xa02': 1200, 'xa10': 1500, 'yb1': -200}
WAIT = {'L31': 400, 'Pind00': 150, 'Prem': 150, 'PstT': 700, 'Z30': 700, 'Z40': 150, 'Z41': 150, 'es0': 250, 'ind01': 700, 'pa00b8': 400, 'pa10BMe': 1350, 'pa10Z3': 100, 'pa10b8': 150, 'pa12Z4': 950, 'pb13cnt': 550, 'rl01536': 150, 'ss0': 1000, 'ww0': 400, 'xa10': 150}
AHEAD = {'Pcnt': -4000, 'Pind01': 400, 'Pind02': 3600, 'Pind03': 4000, 'PstT': -6000, 'XD': -3700, 'Z31': -6900, '_SdI1f': -700, '_Wb': 1300, '_c32': -7000, '_cm192': -300, '_cnt': 4700, '_col0': 1000, '_col14': -700, '_col15': -4000, '_col17': -5000, '_col29': -1000, '_col31': -1000, '_col5': 1300, '_coli2': 1700, '_coli4': 2000, '_cst0': 4000, '_cst3': 2000, '_nI': -1000, '_offtb': -4000, '_rem': -5700, '_tB': -3000, '_tC': -2400, '_tD': 1000, '_val': 2000, 'dd00': 3600, 'dd02': -2700, 'dd03': -1300, 'dd04': -1400, 'dd10': 7600, 'dd11': 3600, 'dd12': 7200, 'dd14': 6700, 'dd15': 8700, 'dm0': -4300, 'fi0': -300, 'fi1': 7000, 'pa00BMe': -4700, 'pa13Cmb': 3600, 'pb10es': -7000, 'pb13cnt': 3900, 'pf0': 6000, 'rl11536': -3000, 'ww1': -700, 'xT12': 2000, 'xa01': 5000, 'xa10': -3000, 'xb11536': 4300}
LEAN = {'hit1': -500, 'ind00': -500, 'ind13': -3000, 'mv1': -500, 'rl01024': 500, 'rl10': -3000, 'uc': -500, 'xa03': 3000}
WAIT = {'Pind10': 300, 'Pind11': 150, 'Z40': 700, '_b80': 150, '_col22': 150, '_dk': 400, '_offtd': 150, '_tCc': 400, 'dd11': 1100, 'dd12': 750, 'dd14': 700, 'dm0': 300, 'fr0': 150, 'ind10': 300, 'pa00hit': 300, 'pa01K16': 300, 'pa10BMe': 600, 'pa10ss': 300, 'pb01ss': 600, 'pb10b8': 150, 'pb10ss': 300, 'pb11fr': 150, 'pf0': 150, 'pi1': 150, 'v0': 150, 'ww0': 600, 'ww1': 600}
WHEN, PERIOD = {}, 23500
PICK = {}
COSTS = [(.88, .42, 1.5, 3.8, 40., 140., 3300., 5., 40.), (.83, .40, 1.56, 3.8, 30., 200., 2500., 0., 40.),
         (.83, .40, 1.3, 3.8, 50., 50., 5000., 0., 130.), (1.04, .50, 1.3, 3.8, 50., 60., 2500., 0., 130.), (.83, .40, 1.3, 3.8, 0., 200., 2500., 28., 0.)]
MEMO = {}


def build(g, T, topo, core, costs):
    CY, PE, GA, SC, FIX, LAT, REM, MF, FA = costs
    TG, RL = OPT["tg"], OPT["rl"]
    rank = T.rank_of(core)
    A, AF = AluOpType, ActivationFunctionType
    V, S, PEq, SY = g.vector, g.scalar, g.tensor, g.sync
    ops, last_w, readers, cur = [], {}, {}, [0, -1]

    def add(eng, fns, cost, rd, wr, banks=(), sem=None, after=(), inc=1, occ=None):
        i = len(ops)
        deps = set(after)
        for k in rd:
            if k in last_w:
                deps.add(last_w[k])
        for k in wr:
            if k in last_w:
                deps.add(last_w[k])
            deps.update(readers.get(k, ()))
        for k in rd:
            readers.setdefault(k, []).append(i)
        for k in wr:
            last_w[k] = i
            readers[k] = []
        deps.discard(i)
        if eng == "A" and occ is None:
            cost += FA
        ops.append({"alt": {eng: (fns, cost)}, "deps": deps, "banks": tuple(banks), "sem": sem, "inc": inc, "wr": wr, "half": cur[0], "occ": occ,
                    "tag": rd[-1][0] if rd else "", "t": cur[1]})
        return i

    def also(i, eng, fn, n, rate=1.0):
        ops[i]["alt"][eng] = ([fn], FIX + max(64, n * rate) * CY + (FA if eng == "A" else 0.0))
        return i

    def at(x):
        return x[0]() if isinstance(x, list) else x

    def bk(keys):
        return sorted(set(k[0] for k in keys if k[0] in ("pa0", "pb0", "pa1", "pb1")))

    def vec(fn, n, rd, wr, rate=1.0):
        return add("D", [fn], FIX + max(64, n * rate) * CY, rd, wr, bk(rd + wr))

    def act(out, in_, func, n, rd, wr, bias=0.0, scale=1.0):
        return add("A", [lambda: S.activation(out, at(in_), func, bias=bias, scale=scale)], FIX + max(64, n) * CY, rd, wr, bk(rd + wr))

    def lin(out, in_, n, rd, wr, bias, scale, rate=1.0):
        i = act(out, in_, AF.Identity, n, rd, wr, bias, scale)
        return also(i, "D", lambda: V.tensor_scalar(out, at(in_), scale, bias, A.mult, A.add), n, rate)

    def step(out, in_, n, rd, wr, up, thr, bias):
        i = act(out, in_, AF.Sigmoid, n, rd, wr, bias, 256.0 if up else -256.0)
        return also(i, "D", lambda: V.tensor_scalar(out, at(in_), thr, None, A.is_gt if up else A.is_lt), n)

    def ts(out, in0, s1, s2, op0, op1, n, rd, wr, rate=1.0):
        if s2 is None:
            return vec(lambda: V.tensor_scalar(out, at(in0), s1, None, op0), n, rd, wr, rate)
        return vec(lambda: V.tensor_scalar(out, at(in0), s1, s2, op0, op1), n, rd, wr, rate)

    def tt(out, a, b, op, n, rd, wr, rate=1.0):
        return vec(lambda: V.tensor_tensor(out, at(a), b, op), n, rd, wr, rate)

    def cp(out, in_, n, rd, wr, rate=1.0):
        return vec(lambda: V.tensor_copy(out, in_), n, rd, wr, rate)

    def ms(ap, val, n, wr):
        return vec(lambda: V.memset(ap, val), n, [], wr, 0.5)

    def mm(items, rd, wr, rds=None):
        k = len(items)
        flags = [it[4] if len(it) > 4 else (j == 0, j == k - 1) for j, it in enumerate(items)]

        def one(j):
            it = items[j]
            if it[2] is None:
                return lambda: PEq.transpose(at(it[0]), it[1], M("Id"))
            return lambda: PEq.matmul(at(it[0]), it[1], it[2], *flags[j])
        parts, n = [[]], 0
        for j, it in enumerate(items):
            if parts[-1] and n + it[3] > OPT["pmax"]:
                parts.append([])
                n = 0
            parts[-1].append(j)
            n += it[3]
        for p in parts:
            c = sum(items[j][3] * PE + MF for j in p)
            i = add("P", [one(j) for j in p], c + 40, sum((rds[j] for j in p), []) + rd if rds else rd, wr, bk(wr), occ=c)
            ops[i]["in"], ops[i]["open"] = not flags[p[0]][0], not flags[p[-1]][1]
        return i

    def grp(out, pairs, rd, wr, n=H):
        return mm([(out, p[0], p[1], n * (p[2] if len(p) > 2 else 1)) for p in pairs], rd, wr)

    def dma(q, name, pairs, cost, rd, wr, after=()):
        qq = SY if q == "S" else S
        return add(q, [(lambda p: lambda: qq.dma_start(p[0], p[1]))(p) for p in pairs], cost, rd, wr, (), "d" + name, after, 16, 60.0 * len(pairs))

    def gp(fn, n, rd, wr):
        return add("G", [fn], 170 + 2 * n * CY, rd, wr)

    def K(name, *a):
        return (name,) + a

    def M(name):
        return T[name][:]

    def col(j):
        return T.col[:, j:j + 1]

    def loan(kind):
        p = len(ops)
        return p, K("loan", p), lambda a, b, r=128, s=1, r0=0: [lambda: T[PICK[p]][r0:r, a:b:s]]

    def give(p, kind, i):
        ops[p]["take"], ops[i]["give"] = (kind + "0", kind + "1"), p

    XK = [[K("X%d" % t)] for t in range(5)]
    for h in range(NS):
        i = dma("S", "c0%d" % h, [(T.c0s[:, h * H + 16 * q:h * H + 16 * q + 16], T.c0[16 * q:16 * q + 16, h * H:(h + 1) * H]) for q in range(8)],
                3000, [], [K("c0s", h)])
        if h == 0:
            dma("S", "y0", [(T.y0s[:], T.y0[:])], 2400, [], [K("y0s")])
            dma("S", "w", [(T.wcol[:, 0:1], T.w[:])], 2400, [], [K("wcol")])
            ix = dma(OPT["x0q"], "x0", [(T.X0[:], T.x0[:])], 6500, [], XK[0])
    dma("S", "st0", [(T.sts[:, 0:256], T.st[:, 0:256])], 6000, [], [K("sts", 0)])
    dma("S", "th", [(T.thT[0:16, 16 * q:16 * q + 16], T.th[q:q + 1, :]) for q in range(8)], 3000, [], [K("thT")], [ix])
    dma("S", "st1", [(T.sts[:, 256:1024], T.st[:, 256:1024])], 3000, [], [K("sts", 1)], [ix])

    def iota(name, pattern, cm, n=128, base=0, ap=None):
        gp(lambda: g.iota(ap or M(name), pattern, base, cm, allow_small_or_imprecise_dtypes=True), n, [], [K(name)])

    gp(lambda: g.iota(T.coli[:, 0:1], [[0, 1]], 0, 1), 1, [], [K("coli", 0)])
    iota("val1", [[1, 4], [4, 2], [8, 16]], -1)
    iota("bq2", [[1, 8], [0, 16]], 0)
    iota("val", [[1, 128]], -1)
    iota("bq", [[0, 16], [1, 8]], 0)
    iota("val2", [[1, 8], [8, 16]], -1)
    iota("rowx", [[256, 16]], 0, 16, 0, T.rows[:, 0:16])
    iota("rowv", [[0, R], [256, 2], [512, 4]], 0, 8 * R, 256, T.rows[:, 16:16 + 8 * R])
    ms(T.src[:, 0:128], 4096.0, 128, [K("src", 0)])
    ms(T.src[:, 256:512], -8.0, 256, [K("src", 1)])
    ms(T.src[0:32, 512:768], -1.0, 256, [K("src", 2)])
    ms(T.src[0:80, 768:1024], -32.0, 256, [K("src", 3)])

    def sel(out, in_, pattern, base, n, rd, wr):
        gp(lambda: g.affine_select(out, in_, pattern, A.is_equal, 0.0, base, -1), n, rd, wr)

    for h in range(NS):
        sel(T.Rep[0:16, h * H:(h + 1) * H], T.src[0:16, 0:128], [[1, 4], [4, 2], [0, 16]], 8 * h, 128, [K("src", 0)], [K("Rep", h)])
    for c in range(4):
        for r in range(2):
            o = 512 * c + 256 * r
            sel(T.Sel[:, o:o + 256], T.src[:, 256:512], [[2, 8], [0, 16], [64, 2]], 16 * c + r, 256, [K("src", 1)], [K("Sel", c, r)])
    sel(T.RepP[0:80, :], T.src[0:80, 768:1024], [[8, 2], [0, 16], [1, 8]], 64, 256, [K("src", 3)], [K("RepP")])
    sel(T.RepN[0:16, :], T.src[0:16, 512:768], [[8, 2], [0, 16], [1, 8]], 0, 256, [K("src", 2)], [K("RepN")])
    ms(M("one"), 1.0, 128, [K("one")])
    ms(M("c32"), 32.0, 128, [K("c32")])
    ms(M("cnt"), 16.0, 128, [K("cnt")])
    ms(T.c192[:, 0:80], -192.0, 80, [K("c192")])
    ms(T.offt[0:23, 0:80], 0.0, 80, [K("offt")])
    for rows, a, b, v in ((23, 0, 32, -44.5), (1, 32, 64, -7.5), (1, 64, 80, -0.5)):
        ms(T.offt[0:rows, a:b], v, 32, [K("offt")])
    ms(T.cst[0:32, 0:128], 992.0, 128, [K("cst", 0)])
    ms(T.cst[0:32, 128:256], 87.0 * 2 ** 20, 128, [K("cst", 1)])
    ms(T.cst[0:32, 256:384], -28672.0, 128, [K("cst", 2)])
    ms(T.cst[0:32, 384:512], 0.0, 128, [K("cst", 3)])
    ms(T.cst[0:32, 384:392], 28672.0, 8, [K("cst", 3)])
    ms(T.cm192[:], -192.0, 256, [K("cm192")])
    for h in range(NS):
        ms(T.xa[:, h * XW + 2048:(h + 1) * XW], 0.0, 16, [K("xa", h, "pad")])
    ts(T.fr[:], T.cm192[:], 0.0, None, A.mult, None, 256, [K("cm192")], [K("fr", h) for h in range(NS)], 0.5)

    (KP, BP, IP, GP, E0, E15, TM, C16, CD0, NG1, PG1, CT1, CT2, CV1, CV2, CM4, CM8, CMF, COH, CSG, TD, BD, TU, BU, TH, BH,
     C32, CCO, CX, MAG, T1, T2) = range(32)
    for j, (c, s, op) in enumerate(((BP, 7, A.bitwise_and), (GP, 4, A.arith_shift_right), (KP, 3, A.arith_shift_right), (IP, 15, A.bitwise_and))):
        ts(T.coli[:, 2 + j:3 + j], T.coli[:, 0:1], s, None, op, None, 1, [K("coli", 0)], [K("coli", 2 + j)])
        lin(col(c), T.coli[:, 2 + j:3 + j], 1, [K("coli", 2 + j)], [K("col", c)], 0.0, 1.0)
        ops[-1]["alt"].pop("A")

    def c1(j, src, s1, s2, o0, o1, extra=()):
        ts(col(j), col(src), s1, s2, o0, o1, 1, [K("col", src)] + [K("col", e) for e in extra], [K("col", j)])

    def ca(j, src, scale, bias, extra=()):
        lin(col(j), col(src), 1, [K("col", src)] + [K("col", e) for e in extra], [K("col", j)], bias, scale)

    CE = math.log(32.0)
    for j, (a, v) in enumerate(((0, 34), (32, 27), (64, 24))):
        ms(T.col[a:a + 32, MAG:MAG + 1], 1.5 * 2 ** v, 1, [K("col", MAG)])
    c1(E0, KP, 0.0, None, A.is_equal, None)
    c1(E15, KP, 15.0, None, A.is_equal, None)
    c1(TM, E0, col(E15), None, A.add, None, [E15])
    ca(C16, KP, -1.0, 16.0)
    ca(CD0, E0, -21.0, 1.0)
    ca(NG1, E0, 1.0, -1.0)
    ca(PG1, E0, -1.0, 1.0)
    ca(CT1, TM, -50.0, 100.0)
    ca(CT2, TM, -50.0, 99.5)
    ca(CM4, TM, -4096.0, 4096.0)
    ca(CM8, TM, -8192.0, 8192.0)
    ca(CMF, TM, -1024.0, 0.0)
    ca(CV2, TM, -33.0, 1.0)
    ca(CV1, E15, 64.0, col(CV2), [CV2])
    ca(CSG, E15, -math.exp(CE * (8.5 - 16) - 10), 0.0)
    c1(T1, KP, 14.0, -4096.0, A.min, A.mult)
    ca(COH, E0, -3072.0, col(T1), [T1])
    c1(T2, KP, 1.0, 46.0, A.max, A.add)
    ca(TD, T2, -1.0, 0.0)
    ca(BD, T2, -256.0, 0.0)
    c1(TU, C16, 49.0, col(E15), A.add, A.subtract, [E15])
    ca(BU, TU, -256.0, 0.0)
    ca(TH, E15, -1024.0, 512.5)
    ca(BH, TH, 256.0, 0.0)
    ca(C32, E0, -3232.0, 3232.0)
    ca(CCO, E0, -0.5, 0.0)
    ca(CX, IP, 16.0, 7.5)

    def mat(name, src, s1, o0, s2=1.0, cols=(), o1=None, a=0, b=128, out=None):
        ts(out or M(name), T[src][:, a:b], s1, s2, o0, o1 or A.mult, b - a, [K(src)] + [K("col", c) for c in cols], [K(name)], 0.5)

    def mat2(name, a, b, op):
        tt(M(name), M(a), M(b), op, 128, [K(a), K(b)], [K(name)], 2.0)

    mat("I1", "val1", 0.0, A.is_equal)
    mat("tC", "bq2", col(GP), A.is_equal, 1.0, [GP])
    ts(M("Wb"), M("tC"), T.wcol[:, 0:1], None, A.mult, None, 128, [K("tC"), K("wcol")], [K("Wb")], 0.5)
    for j, v in enumerate((1.0, 2.0, -1.0)):
        ts(T.b8[:, 8 * j:8 * j + 8], T.bq2[:, 0::16], col(GP), v, A.is_equal, A.mult, 8, [K("bq2"), K("col", GP)], [K("b8", j)])
    BO8, BO2, BOn = T.b8[:, 0:8], T.b8[:, 8:16], T.b8[:, 16:24]
    mat("Id", "val", 0.0, A.is_equal)
    mat("I4", "val", 0.0, A.is_equal, 4.0)
    mat("nI", "val", 0.0, A.is_equal, -1.0)
    mat("Idf", "val", 0.0, A.is_equal)
    mat("Ik1", "val", 0.0, A.is_equal, col(PG1), [PG1])
    mat("B2", "bq2", col(BP), A.is_equal, 1.0, [BP])
    mat("tA", "val2", 0.0, A.is_gt, col(C16), [C16], A.subtract)
    mat2("tA", "tA", "B2", A.mult)
    mat("tB", "val2", 0.0, A.is_equal, col(KP), [KP])
    mat2("Cm", "tB", "tA", A.subtract)
    mat("B", "bq", col(BP), A.is_equal, 1.0, [BP])
    mat("dk", "val", 0.125, A.mult, 100.0, (), A.add)
    mat2("dk", "dk", "B", A.mult)
    mat("nBMe", "bq", col(BP), A.is_equal, col(NG1), [BP, NG1])
    mat("BMe", "bq", col(BP), A.is_equal, col(PG1), [BP, PG1])
    mat("B3232", "bq", col(BP), A.is_equal, col(C32), [BP, C32])
    mat("K16", "bq", col(BP), A.is_equal, -16.0, [BP])
    mat("tD", "val", 0.0, A.is_equal, 16.0)
    mat2("Mdl", "nBMe", "tD", A.add)
    mat("Mdl", "bq", col(BP), A.is_equal, col(CD0), [BP, CD0], None, 0, 8, T.Mdl[:, 0:8])
    mat("Mdl", "bq", col(BP), A.is_equal, col(E0), [BP, E0], None, 0, 8, T.Mdl[:, 120:128])
    mat("Md", "dk", col(CT1), A.is_gt, col(CV1), [CT1, CV1])
    mat("Mu", "dk", col(CT2), A.is_gt, col(CV2), [CT2, CV2])
    mat("tC", "dk", 99.5, A.is_gt, col(CM4), [CM4])
    mat("tD", "dk", 100.0, A.is_gt, col(CM8), [CM8])
    mat2("Moh", "tC", "tD", A.subtract)
    mat("Moh", "bq", col(BP), A.is_equal, col(CMF), [BP, CMF], None, 0, 8, T.Moh[:, 0:8])
    ms(M("R0a"), 0.0, 128, [K("R0a")])
    mat("R0a", "bq", col(BP), A.is_equal, col(PG1), [BP, PG1], None, 0, 8, T.R0a[:, 0:8])
    mat("tA", "val", 8.0, A.is_equal)
    mat2("SdI", "tA", "Id", A.subtract)
    mat2("SdIf", "tA", "Id", A.subtract)
    mat("tB", "val", -8.0, A.is_equal)
    mat2("SuI", "tB", "Id", A.subtract)
    mat("tC", "val1", 8.0, A.is_equal)
    mat2("SdI1f", "tC", "I1", A.subtract)
    mat("tD", "dk", 100.0, A.is_gt, -17.0)
    mat2("Mst", "tD", "B", A.add)
    mat("R15", "bq", -1.0, A.is_gt, col(E15), [E15])
    mat("Mco", "bq", col(BP), A.is_equal, col(CCO), [BP, CCO])
    mat("Mco", "Mco", -1.0, A.mult, 1.0, (), None, 120, 128, T.Mco[:, 120:128])

    def flip(srcs, dst, rd, wr):
        n = 128 * len(srcs)
        p, kb, B = loan("pT")
        mm([(B(c * 128, (c + 1) * 128), s, None, 128, (True, True)) for c, s in enumerate(srcs)], [K("Id")], [kb], rd)
        i = vec(lambda: V.tensor_copy(dst, at(B(0, n))), n, [kb], wr, 0.5)
        also(i, "A", lambda: S.activation(dst, at(B(0, n)), AF.Copy), n)
        give(p, "pT", i)

    def stflip(t):
        flip([T.sts[:, t * 256 + h * H:t * 256 + (h + 1) * H] for h in range(NS)], T.stT[:, t * 256:(t + 1) * 256], [[K("sts", min(t, 1))]] * NS, [K("stT", t)])

    def hs(name, h, w=H):
        return T[name][:, h * w:(h + 1) * w]

    def slot(b, h, s, a=0, e=H, st=1):
        nm = "p%s%d" % (b, h)
        return T[nm][:, s * H + a:s * H + e:st], K(nm, s)

    def gather(out, win, offs, n, rd, wr):
        i = vec(lambda: V.tensor_copy(out, win.indirect(offs)), n, rd, wr, GA)
        return also(i, "A", lambda: S.activation(out, win.indirect(offs), AF.Copy), n, GA)

    def uphase(t):
        kyb = [K("yb", h) for h in range(NS)]
        p, kb, B = loan("pD")
        mm([(B(0, 128, 80), T.c192[:, 0:80], M("Wb"), 128)]
           + [(B(i, 128, 32 * a + 16, 16, 32 * a), T.yb[:, i::16], T.Wb[:, 0::16], 16) for a in range(3) for i in range(16)]
           + [(B(0, 128, 80), T.offt[0:23, 0:80], T.one[0:23, :], 128)],
           kyb + [K("c192"), K("Wb"), K("offt"), K("one")], [kb])
        mg = T.col[0:80, MAG:MAG + 1]
        ts(T.ur[0:80, :], B(0, 128, 80), mg, mg, A.add, A.subtract, 128, [K("col", MAG)], [kb, K("ur")])
        give(p, "pD", tt(T.rem[0:80, :], B(0, 128, 80), T.ur[0:80, :], A.subtract, 128, [K("ur")], [kb, K("rem")]))
        p, kb, B = loan("pD")
        mm([(B(0, 256), T.rem[0:16, :], T.Rep[0:16, :], 256, (True, True)), (B(256, 272), T.rem[0:16, :], T.Id[0:16, 0:16], 64, (True, True)),
            (B(272, 288), T.one[0:1, :], T.rows[0:1, 0:16], 64, (True, False)), (B(272, 288), T.rem[0:48, :], T.Id[0:48, 32:48], 64, (False, True))],
           [K("rem"), K("Rep", 0), K("Rep", 1), K("Id"), K("one"), K("rowx")], [kb])
        lin(T.mm[:], B(0, 256), 256, [], [kb, K("mm")], 2080.0, 1.0 / 2048)
        ts(T.offx[:], B(272, 288), col(CX), None, A.add, None, 16, [K("col", CX)], [kb, K("offx")])
        give(p, "pD", lin(T.uc[:], B(256, 272), 16, [], [kb, K("uc")], 1023.5, 1.0))
        gather(T.Xo[:], T["X%d" % t][:, 0:4096], T.offx[:], 256, XK[t] + [K("offx")], [K("Xo")])

    def qphase(h):
        q, kq = slot("b", h, 3)
        grp(q, [(T.rem[0:16, :], T.Rep[0:16, h * H:(h + 1) * H]), (M("c32"), M("cnt"))], [K("rem"), K("Rep", h), K("c32"), K("cnt")], [kq])

    def point(h, a, b, c, rd1, rd2, off):
        tt(hs("pf", h), a, b, A.mult, H, rd1, [K("pf", h)])
        tt(hs("pi", h), c, hs("pf", h), A.add, H, rd2 + [K("pf", h)], [K("pi", h)])
        ts(hs("pj", h), hs("pi", h), 5, 4095, A.arith_shift_right, A.bitwise_and, H, [K("pi", h)], [K("pj", h)])
        cp(hs(off, h), hs("pj", h), H, [K("pj", h)], [K(off, h)])

    def fold(out, name, h, lo, rhs, a, b):
        return [(out(i), lo(i), rhs, 64, (a, b(i))) for i in range(16)]

    def step12(t, h):
        nn, kn = slot("a", h, 2)
        q, kq = slot("b", h, 3)
        point(h, nn, hs("mm", h), q, [kn, K("mm")], [kq], "off1")
        xo, o = h * XW, h * 2048
        GS = OPT["gs"]
        for c in range(2048 // GS):
            gather(T.xa[:, xo + c * GS:xo + (c + 1) * GS], T["X%d" % t][:, 0:4096], T.off1[:, h * H + c * GS // 16:h * H + (c + 1) * GS // 16], GS,
                   XK[t] + [K("off1", h)], [K("xa", h, c)])
        so = t * 256 + h * H
        kE = K("pa%d" % h, 3)
        for c0 in range(0, 4, TG):
            cs = range(c0, c0 + TG)
            blocks = [(c, bh, r) for c in cs for bh in range(2) for r in range(2)]
            flip([T.xa[:, xo + 512 * c + 256 * bh + r:xo + 512 * c + 256 * (bh + 1):2] for c, bh, r in blocks],
                 T.xT[:, o + c0 * 512:o + (c0 + TG) * 512], [[K("xa", h, (512 * c + 256 * bh) // GS)] for c, bh, r in blocks], [K("xT", h, c0)])

            def xT(c, bh, r):
                a = o + 512 * c + 256 * bh + 128 * r
                return T.xT[:, a:a + 128]
            for c in cs:
                p, kb, B = loan("pD")
                mm([(B(0, 512), T.stT[:, so:so + 128], T.Sel[:, 512 * c:512 * (c + 1)], 512)]
                   + [(B(256 * r + bh, 256 * (r + 1), 128, 2), xT(c, bh, r), M("Cm"), 128) for bh in range(2) for r in range(2)],
                   [], [kb], [[K("stT", t), K("Sel", c, 0), K("Sel", c, 1), K("xa", h, 512 * c0 // GS)]] + [[K("xT", h, c0), K("Cm")]] * 4)
                give(p, "pD", step(T.ind[:, o + c:o + 2048:4], B(0, 512), 512, [kb], [K("ind", h, c)], True, -0.5, 128.0))
            mm([(slot("a", h, 3, 16 * (c + 4 * bh) + r, 16 * (c + 4 * bh) + 16, 2)[0], xT(c, bh, r), T.Cm[:, 0::16], 64, (True, True))
                for c, bh, r in blocks], [K("xT", h, c0), K("Cm")], [kE])
        mm([(slot("a", h, 0, i, H, 16)[0], T.ind[:, o + 128 * (8 * (i & 1) + i // 2):o + 128 * (8 * (i & 1) + i // 2 + 1)], BO8, 64, (True, True))
            for i in range(16)], [K("ind", h, c) for c in range(4)] + [K("b8", 0)], [K("pa%d" % h, 0)])
        lin(hs("yb", h), slot("a", h, 3)[0], H, [kE], [K("yb", h)], 191.5 + 1.0 / 64, 1.0 / 32)

    def send(name, src, dst, ksrc, t, h):
        to = T.cores[(rank + 1 + t % 3) % NR]
        rid, pid = topo.addr(to)[:2]
        mk = topo.mask(core, to)
        n = len(topo.engines(core, to))
        sem = "a%s%d%d" % (name, t, h)
        i = add("G", [lambda: g.remote_dma(dst, src, T.sem[sem], T.sem.sent, pid, rid, mk)], 300, ksrc, [], (), "sent", (), n)
        add("R", [], REM, [], [K(name + "r", t, h)], (), sem, [i], n)

    def step3(t, h):
        (a0, k0), (a1, k1) = slot("a", h, 0), slot("a", h, 1)
        (b0, j0), (b1, j1), (b2, j2) = [slot("b", h, s) for s in range(3)]
        C, kC = hs("Cc", h), K("Cc", h)
        act(hs("ww", h), a0, AF.Sigmoid, H, [k0], [K("ww", h)], -16 * CE - 10, CE)
        grp(b0, [(M("Mdl"), hs("ww", h))], [K("Mdl"), K("ww", h)], [j0])
        act(hs("ss", h), b0, AF.Sign, H, [j0, K("col", CSG)], [K("ss", h)], col(CSG))
        s, ks = hs("ss", h), K("ss", h)
        grp(a0, [(M("Ik1"), C), (M("Moh"), s)], [K("Ik1"), kC, K("Moh"), ks], [k0])
        e, ke = hs("es", NS * t + h), K("es", t, h)
        ts(e, a0, col(COH), -2048.0, A.add, A.max, H, [k0, K("col", COH)], [ke])
        send("e", e, hs("er", NS * t + h), [ke], t, h)
        dm, um = T.du[:, 256 * h:256 * h + H], T.du[:, 256 * h + H:256 * (h + 1)]
        grp(b0, [(M("Mu"), s)], [K("Mu"), ks], [j0])
        step(um, b0, H, [j0, K("col", TU), K("col", BU)], [K("um", h)], True, col(TU), col(BU))
        grp(b1, [(T.RepP[0:80, h * H:(h + 1) * H], T.rem[0:80, :]), (M("Md"), s)], [K("RepP"), K("rem"), K("Md"), ks], [j1])
        step(dm, b1, H, [j1, K("col", TD), K("col", BD)], [K("dm", h)], False, col(TD), col(BD))
        n = 8 * R
        kv = slot("a", h, 1, 0, n)[0]
        grp(kv, [(T.one[0:1, :], T.rows[0:1, 16:16 + n]), (um, T.K16[:, 0:n])], [K("one"), K("rowv"), K("um", h), K("K16")], [k1], 64)
        ts(hs("offv", h, n), kv, col(IP), None, A.add, None, n, [k1, K("col", IP)], [K("offv", h)])
        v = hs("vs", NS * t + h, H * R)
        gather(v, T.xa[:, h * XW:(h + 1) * XW], hs("offv", h, n), H * R,
               [K("xa", h, c) for c in list(range(2048 // OPT["gs"])) + ["pad"]] + [K("offv", h)], [K("v", t, h)])
        send("v", v, hs("vr", NS * t + h, H * R), [K("v", t, h)], t, h)
        ec = slot("a", h, 0, 0, 8)[0]
        grp(ec, [(T.one[0:31, :], T.cst[0:31, 0:8]), (e, T.BMe[:, 0:8])], [K("one"), K("cst", 0), ke, K("BMe")], [k0], 64)
        tt(hs("fi", h, 8), ec, hs("uc", h, 8), A.mult, 8, [k0, K("uc")], [K("fi", h)])
        ts(hs("fj", h, 8), hs("fi", h, 8), 5, 4095, A.arith_shift_right, A.bitwise_and, 8, [K("fi", h)], [K("fj", h)])
        ts(T.fr[:, h * H + 120:(h + 1) * H], hs("fj", h, 8), -2048.0, None, A.add, None, 8, [K("fj", h)], [K("fr", h)])
        grp(b0, [(T.cst[0:1, 384:512], T.one[0:1, :]), (M("SdI"), C), (M("R0a"), e)], [K("cst", 3), K("one"), K("SdI"), K("R0a"), kC, ke], [j0])
        grp(b1, [(M("SuI"), C), (hs("fr", h), M("Id"))], [K("SuI"), K("Id"), kC, K("fr", h)], [j1])
        tt(hs("Z3", h, 256), slot("b", h, 0, 0, 256)[0], hs("du", h, 256), A.mult, 256, [j0, j1, K("dm", h), K("um", h)], [K("Z3", h)])
        zd, zu = T.Z3[:, 256 * h:256 * h + H], T.Z3[:, 256 * h + H:256 * (h + 1)]
        N3, L3 = T.C3[:, 256 * h:256 * h + H], T.C3[:, 256 * h + H:256 * (h + 1)]
        rd = [K("Id"), K("Idf"), kC, K("Z3", h)]
        if OPT["both"]:
            grp(a1, [(C, M("Id")), (zd, M("Idf"), 4), (zu, M("Idf"), 4)], rd, [k1])
            grp(a0, [(M("Id"), C), (M("Idf"), zd, 4), (M("Idf"), zu, 4)], rd, [k0])
            lin(hs("C3", h, 256), slot("a", h, 0, 0, 256)[0], 256, [k0, k1], [K("C3", h), K("L3", h)], 0.0, 1.0)
        else:
            grp(a0, [(M("Id"), C), (M("Idf"), zd, 4), (M("Idf"), zu, 4)], rd, [k0])
            lin(N3, a0, H, [k0], [K("C3", h)], 0.0, 1.0)
            grp(b2, [(N3, M("Id"))], [K("C3", h), K("Id")], [j2])
            lin(L3, b2, H, [j2], [K("L3", h)], 0.0, 1.0)

    def renew(t):
        kyb = [K("yb", h) for h in range(NS)]
        p, kb, B = loan("pD")
        grp(B(0, 256), [(M("I4"), T.Xo[:]), (M("Id"), T.yb[:])], [K("I4"), K("Id"), K("Xo")] + kyb, [kb], 256)
        give(p, "pD", lin(T.xn[:], B(0, 256), 256, [kb], [K("xn")], 167.5 + 1.0 / 16, 1.0 / 8))
        vec(lambda: V.tensor_tensor(T["X%d" % (t + 1)][:, 0:4096].indirect(T.offx[:]), T.xn[:], T.cm192[:], A.add), 256,
            [K("xn"), K("cm192"), K("offx")], XK[t + 1], SC)

    def count():
        p, kb, B = loan("pD")
        grp(B(0, 128), [(T.du[:, 256 * h + H:256 * (h + 1)], M("R15")) for h in range(NS)], [K("R15")] + [K("um", h) for h in range(NS)], [kb])
        give(p, "pD", lin(M("cnt"), B(0, 128), 128, [kb], [K("cnt")], 16.0, 1.0))

    def step4(t, h):
        (a0, k0), (a1, k1), (a2, k2) = [slot("a", h, s) for s in range(3)]
        (b0, j0), (b1, j1), (b2, j2) = [slot("b", h, s) for s in range(3)]
        e, ke = hs("er", NS * t + h), K("er", t, h)
        N3, L3 = T.C3[:, 256 * h:256 * h + H], T.C3[:, 256 * h + H:256 * (h + 1)]
        mm([(a0, T.one[0:31, :], T.cst[0:31, 0:128], H, (True, False)), (a0, e, M("BMe"), H, (False, True)),
            (a1, T.one[0:1, :], T.cst[0:1, 128:256], H, (True, False)), (a1, e, M("B3232"), H, (False, True))],
           [K("one"), K("cst", 0), K("cst", 1), K("BMe"), K("B3232"), ke], [k0, k1])
        point(h, a0, L3, a1, [k0, K("L3", h)], [k1], "off2")
        grp(b2, [(T.one[0:1, :], T.cst[0:1, 256:384]), (M("Id"), N3), (M("nBMe"), e)], [K("one"), K("cst", 2), K("Id"), K("nBMe"), K("C3", h), ke], [j2])
        o, w = h * 2048, H * R
        v, kv = hs("vr", NS * t + h, w), K("vr", t, h)
        X, F = T["X%d" % t][:, 0:4096], 2048 - 512 * OPT["ua"]
        for n in range(F // w):
            vec((lambda n: lambda: V.tensor_tensor(T.dd[:, o + n * w:o + (n + 1) * w],
                                                   X.indirect(T.off2[:, h * H + 8 * R * n:h * H + 8 * R * (n + 1)]), v, A.subtract))(n),
                w, XK[t] + [K("off2", h), kv], [K("dd", h, n)], GA)
        krl = []
        for a in range(0, F, RL):
            b = min(a + RL, F)
            krl.append(K("rl", h, a))
            i = ts(T.rl[:, o + a:o + b], T.dd[:, o + a:o + b], 0.0, None, A.max, None, b - a, [K("dd", h, n) for n in range(a // w, b // w)], krl[-1:], 0.5)
            also(i, "A", (lambda a, b: lambda: S.activation(T.rl[:, a:b], T.dd[:, a:b], AF.Relu))(o + a, o + b), b - a)
        for a in range(F, 2048, 512):
            gather(T.dd[:, o + a:o + a + 512], X, T.off2[:, h * H + a // 16:h * H + a // 16 + 32], 512, XK[t] + [K("off2", h)], [K("xb", h, a)])
            p, kb, B = loan("pD")
            mm([(B(0, 512), M("Id"), T.dd[:, o + a:o + a + 512], 512)] + [(B(c, c + w), M("nI"), v, w) for c in range(0, 512, w)],
               [], [kb], [[K("Id"), K("xb", h, a)]] + [[K("nI"), kv]] * (512 // w))
            krl.append(K("rl", h, a))
            give(p, "pD", act(T.rl[:, o + a:o + a + 512], B(0, 512), AF.Abs, 512, [kb], krl[-1:], 0.0, 0.5))
        i = mm([(b0, T.RepN[0:16, h * H:(h + 1) * H], T.thT[0:16, :], H, (True, False)), (b0, M("Mco"), e, H, (False, False))]
               + [(T[j0[0]][0:F // 16, i:H:16], T.dd[:, o + i:o + F:16], BOn, 64, (False, False)) for i in range(16)],
               [K("dd", h, n) for n in range(F // w)] + [K("RepN"), K("thT"), K("Mco"), ke, K("b8", 2)], [j0])
        i = mm([(slot("b", h, 0, i, H, 16)[0], T.rl[:, o + i:o + 2048:16], BO2, 64, (False, i == 15)) for i in range(16)],
               krl + [K("b8", 1)], [j0])
        step(hs("hit", h), b0, H, [j0, K("col", TH), K("col", BH)], [K("hit", h)], False, col(TH), col(BH))
        grp(a0, [(M("Mst"), hs("hit", h))], [K("Mst"), K("hit", h)], [k0])
        step(hs("mv", h), a0, H, [k0], [K("mv", h)], False, 0.5, 128.0)
        tt(hs("Z4", h), b2, hs("mv", h), A.mult, H, [j2, K("mv", h)], [K("Z4", h)])
        if t < RO - 1:
            grp(a2, [(N3, M("I1")), (hs("Z4", h), M("SdI1f"), 4)], [K("C3", h), K("I1"), K("SdI1f"), K("Z4", h)], [k2])
        grp(b1, [(M("Id"), N3), (M("SdIf"), hs("Z4", h), 4)], [K("C3", h), K("Id"), K("SdIf"), K("Z4", h)], [j1])
        if t < RO - 1:
            lin(hs("Cc", h), b1, H, [j1], [K("Cc", h)], 0.0, 1.0)
        else:
            lin(hs("yco", h), b1, H, [j1], [K("yco", h)], 2048.0, 1.0)
            for j, q in enumerate("SA"):
                dma(q, "oyc%d%d" % (h, j), [(T.yc[16 * u:16 * u + 16, h * H:(h + 1) * H], T.yco[:, h * H + 16 * u:h * H + 16 * u + 16]) for u in range(j, 8, 2)],
                    3500, [K("yco", h)], [])

    lin(T.yb[:], T.y0s[:], 256, [K("y0s")], [K("yb", h) for h in range(NS)], 192.0, 1.0, 0.5)
    uphase(0)
    for h in range(NS):
        cur[0] = h
        ts(hs("Cc", h), hs("c0s", h), -2048.0, None, A.add, None, H, [K("c0s", h)], [K("Cc", h)])
        nn, kn = slot("a", h, 2)
        grp(nn, [(hs("Cc", h), M("I1"))], [K("I1"), K("Cc", h)], [kn])
        qphase(h)
    cur[0] = 0
    dma("S", "x1", [(T.X1[:], T.x0[:])], 6000, [], XK[1], [ix])
    stflip(0)
    for t in range(RO):
        cur[1] = t
        for h in range(NS):
            cur[0] = h
            step12(t, h)
            step3(t, h)
        cur[0] = 0
        renew(t)
        if t < RO - 1:
            stflip(t + 1)
            count()
            uphase(t + 1)
            for h in range(NS):
                qphase(h)
            dma("S", "x%d" % (t + 2), [(T["X%d" % (t + 2)][:], T["X%d" % (t + 1)][:])], 6000, XK[t + 1], XK[t + 2], [last_w[K("vr", t, NS - 1)]])
        else:
            dma("S", "oyx", [(T.yx[:], T.X4[:])], 6000, XK[4], [], [last_w[K("vr", t, NS - 1)]])
            lin(T.yyo[:], T.yb[:], 256, [K("yb", h) for h in range(NS)], [K("yyo")], -192.0, 1.0, 0.5)
            dma("S", "oyy", [(T.yy[:], T.yyo[:])], 2500, [K("yyo")], [])
        for h in range(NS):
            cur[0] = h
            step4(t, h)
        cur[0] = 0
    return ops


def schedule(ops, lat, adj):
    n = len(ops)
    succ = [[] for _ in range(n)]
    for i, o in enumerate(ops):
        for d in o["deps"]:
            succ[d].append(i)
    pri = [0.0] * n
    for i in range(n - 1, -1, -1):
        pri[i] = min(a[1] for a in ops[i]["alt"].values()) + max([pri[j] + lat for j in succ[i]] + [0.0])
    pri = [p + q for p, q in zip(pri, adj[0])]
    lean, win = adj[1], adj[2]
    left = [len(o["deps"]) for o in ops]
    free = {e: 0.0 for e in "PDAGSR"}
    fin, eng, plan = [0.0] * n, [None] * n, []
    bank = {b: {} for b in ("pa0", "pb0", "pa1", "pb1")}
    pool = {b: -1 for b in ("pT0", "pT1", "pD0", "pD1")}
    held, shut = {}, set()

    def enter(i):
        o = ops[i]
        return (i, [(e, a[1], max([fin[d] + (0.0 if e == "P" == eng[d] else lat) for d in o["deps"]] + [0.0])) for e, a in o["alt"].items()],
                o["banks"], o.get("take"))

    ready = [enter(i) for i in range(n) if left[i] == 0]
    while ready:
        st, t0 = [], 1e18
        for x in ready:
            i, al, bs, take = x
            if shut and "P" in ops[i]["alt"] and not ops[i]["in"] and shut.intersection(bs):
                continue
            best = None
            for e, c, s in al:
                if free[e] > s:
                    s = free[e]
                for b in bs:
                    for e2, f in bank[b].items():
                        if e2 != e and fin[f] + lat > s:
                            s = fin[f] + lat
                v = s + c + (lean[i] if e == "D" else 0.0)
                if best is None or v < best[0]:
                    best = (v, s, e, c)
            v, s, e, c = best
            got = None
            if take:
                av = [(fin[pool[b]] + lat if pool[b] >= 0 else 0.0, b) for b in take if pool[b] is not None]
                if not av:
                    continue
                f, got = min(av)
                s = max(s, f)
            st.append((s, x, e, c, got))
            if s < t0:
                t0 = s
        s, x, e, c, got = max([y for y in st if y[0] <= t0 + win[y[1][0]]], key=lambda y: pri[y[1][0]])
        i = x[0]
        o = ops[i]
        deps = set(o["deps"])
        for b in x[2]:
            deps.update(j for e2, j in bank[b].items() if e2 != e)
            bank[b][e] = i
        if got:
            if pool[got] >= 0:
                deps.add(pool[got])
            pool[got] = None
            held[i] = got
        if "give" in o:
            pool[held[o["give"]]] = i
        if e == "P":
            (shut.update if o["open"] else shut.difference_update)(o["banks"])
        fin[i] = s + c
        eng[i] = e
        if e != "R":
            free[e] = s + (o["occ"] or c)
        plan.append((i, e, deps, got))
        ready.remove(x)
        for j in succ[i]:
            left[j] -= 1
            if left[j] == 0:
                ready.append(enter(j))
    return plan


def ordered(ops, lat, key, engs):
    n = len(ops)
    succ = [[] for _ in range(n)]
    left = [len(o["deps"]) for o in ops]
    for i, o in enumerate(ops):
        for d in o["deps"]:
            succ[d].append(i)
    free = {e: 0.0 for e in "PDAGSR"}
    fin, plan = [0.0] * n, []
    bank = {b: {} for b in ("pa0", "pb0", "pa1", "pb1")}
    pool = {b: -1 for b in ("pT0", "pT1", "pD0", "pD1")}
    held, shut = {}, set()
    ready = sorted((key[i], i) for i in range(n) if left[i] == 0)
    while ready:
        for x in ready:
            i = x[1]
            o, e, got = ops[i], engs[i], None
            if shut and e == "P" and not o["in"] and shut.intersection(o["banks"]):
                continue
            if "take" in o:
                av = [(fin[pool[b]] if pool[b] >= 0 else 0.0, b) for b in o["take"] if pool[b] is not None]
                if not av:
                    continue
                got = min(av)[1]
            break
        ready.remove(x)
        deps = set(o["deps"])
        for b in o["banks"]:
            deps.update(j for e2, j in bank[b].items() if e2 != e)
            bank[b][e] = i
        if got:
            if pool[got] >= 0:
                deps.add(pool[got])
            pool[got] = None
            held[i] = got
        if "give" in o:
            pool[held[o["give"]]] = i
        if e == "P":
            (shut.update if o["open"] else shut.difference_update)(o["banks"])
        s = max([free[e]] + [fin[d] + (0.0 if e == "P" == engs[d] else lat) for d in deps])
        fin[i] = s + o["alt"][e][1]
        if e != "R":
            free[e] = s + (o["occ"] or o["alt"][e][1])
        plan.append((i, e, deps, got))
        for j in succ[i]:
            left[j] -= 1
            if left[j] == 0:
                ready.append((key[j], j))
        ready.sort()
    return plan


def packed(ops, lat, adj):
    n = len(ops)
    succ = [[] for _ in range(n)]
    left = [len(o["deps"]) for o in ops]
    for i, o in enumerate(ops):
        for d in o["deps"]:
            succ[d].append(i)
    pri = [0.0] * n
    for i in range(n - 1, -1, -1):
        pri[i] = min(a[1] for a in ops[i]["alt"].values()) + max([pri[j] + lat for j in succ[i]] + [0.0])
    key = [-p - q - (OPT["short"] if min(a[1] for a in o["alt"].values()) < 330 else 0.0) for p, q, o in zip(pri, adj[0], ops)]
    lean = adj[1]
    busy = {e: [] for e in "PDAGS"}
    use = {b: [] for b in ("pa0", "pb0", "pa1", "pb1")}
    pool = {b: 0.0 for b in ("pT0", "pT1", "pD0", "pD1")}
    held, shut, began = {}, set(), {}
    st, fin, eng = [0.0] * n, [0.0] * n, [None] * n
    ready = sorted((key[i], i) for i in range(n) if left[i] == 0)

    def fit(i, e, s):
        o = ops[i]
        c = o["alt"][e][1]
        w = o["occ"] or c
        while True:
            s0 = s
            if e != "R":
                for a, b in busy[e]:
                    if a >= s + w:
                        break
                    if b > s:
                        s = b
            for k in o["banks"]:
                for a, b, e2 in use[k][-24:]:
                    if e2 != e and b > s and a < s + c + lat and not (e2 == "L" and (e != "P" or o["in"])):
                        s = b
            if s == s0:
                return s

    while ready:
        for x in ready:
            i = x[1]
            o, got = ops[i], None
            if shut and "P" in o["alt"] and not o["in"] and shut.intersection(o["banks"]):
                continue
            if "take" in o:
                av = [(pool[b], b) for b in o["take"] if pool[b] is not None]
                if not av:
                    continue
                got = min(av)
            break
        ready.remove(x)
        best = None
        for e, a in o["alt"].items():
            s = max([fin[d] + lat if e != "P" or eng[d] != "P" else st[d] + ops[d]["occ"] for d in o["deps"]] + [got[0] if got else 0.0])
            if e == "P" and o["open"] and not o["in"]:
                s = max([s] + [b - lat for k in o["banks"] for a2, b, e2 in use[k][-24:] if e2 == "P"])
            s = fit(i, e, s)
            v = s + a[1] + (lean[i] if e == "D" else 0.0)
            if best is None or v < best[0]:
                best = (v, s, e, a[1])
        v, s, e, c = best
        st[i], fin[i], eng[i] = s, s + c, e
        if e != "R":
            busy[e].append((s, s + (o["occ"] or c)))
            busy[e].sort()
            if len(busy[e]) > 60:
                busy[e][0:2] = [(0.0, busy[e][1][1])]
        for k in o["banks"]:
            use[k].append((s, s + c + lat, e))
            if e == "P" and o["open"] and not o["in"]:
                began[k] = s
            if e == "P" and o["in"] and not o["open"]:
                use[k].append((began[k], s + o["occ"], "L"))
        if got:
            pool[got[1]] = None
            held[i] = got[1]
        if "give" in o:
            pool[held[o["give"]]] = fin[i] + lat
        if e == "P":
            (shut.update if o["open"] else shut.difference_update)(o["banks"])
        for j in succ[i]:
            left[j] -= 1
            if left[j] == 0:
                ready.append((key[j], j))
        ready.sort()
    return ordered(ops, lat, st, eng)


def keyed(ops):
    lab = labels(ops)
    return ([WHEN[k][0] + PERIOD * max(o["t"], 0) for k, o in zip(lab, ops)], [WHEN[k][1] for k in lab])


def replay(ops, plan, lat):
    free, fin, eng, st = {}, {}, {}, {}
    for i, e, deps, _ in plan:
        s = max([free.get(e, 0.0)] + [fin[d] + (0.0 if e == "P" == eng[d] else lat) for d in deps])
        st[i], fin[i], eng[i] = s, s + ops[i]["alt"][e][1], e
        if e != "R":
            free[e] = s + (ops[i]["occ"] or ops[i]["alt"][e][1])
    return max(fin.values()), st


def choose(g, T, topo, core):
    ops = build(g, T, topo, core, COSTS[0])
    if "plan" not in MEMO:
        MEMO["plan"] = ordered(ops, COSTS[0][5], *keyed(ops)) if WHEN else schedule(ops, COSTS[0][5], adjust(ops))
    return ops, MEMO["plan"]


def labels(ops):
    out, seen = [], {}
    giver = {o["give"]: o for o in ops if "give" in o}
    for i, o in enumerate(ops):
        k = o["wr"][-1] if o["wr"] else ("send",) + ops[i + 1]["wr"][0] if o["sem"] == "sent" else (o["sem"],)
        pre = "_" * (o["t"] < 0)
        if k[0] == "loan":
            k, pre = giver[k[1]]["wr"][-1], pre + "P"
        if k[0] in ("es", "er", "v", "vr", "send", "stT"):
            k = k[:-2] + k[-1:] if k[0] != "stT" else k[:1]
        if k[0][0] == "X" and k[0] != "Xo":
            k = ("X" + list(o["alt"])[0],)
        if k[0] in ("pa0", "pa1", "pb0", "pb1"):
            k = k + (o["tag"],)
        k = pre + "".join(str(x) for x in k)
        seen[o["t"], k] = seen.get((o["t"], k), 0) + 1
        out.append(k + " bcdefghij"[seen[o["t"], k] - 1].strip())
    return out


def adjust(ops):
    lab = labels(ops)
    return ([AHEAD.get(k, 0.0) - OPT["stag"] * o["half"] for k, o in zip(lab, ops)],
            [LEAN.get(k, 0.0) + OPT["lean"] + OPT["lam"] * o["alt"]["D"][1] if "D" in o["alt"] else 0.0 for k, o in zip(lab, ops)],
            [OPT["win"] + WAIT.get(k, 0.0) for k in lab])


def emit(g, T, ops, plan):
    q = {"P": g.tensor, "D": g.vector, "A": g.scalar, "G": g, "S": g.sync}
    total, known, mark, eng, pos = {}, {e: {} for e in q}, {}, {}, {}
    for i, e, deps, got in plan:
        o = ops[i]
        PICK[i] = got
        eng[i] = e
        pos[i] = len(pos)
        sem = o["sem"] or "q" + e
        if e == "R":
            total[sem] = o["inc"]
            mark[i] = (sem, o["inc"], {})
            continue
        kn = known[e]
        need = {}
        for d in deps:
            if e == "P" and eng[d] == "P":
                continue
            s, v, _ = mark[d]
            if s != "sent" and kn.get(s, 0) < v and need.get(s, (0, 0))[0] < v:
                need[s] = (v, d)
        for s, (v, d) in sorted(need.items(), key=lambda x: -pos[x[1][1]]):
            if kn.get(s, 0) < v:
                q[e].wait_ge(T.sem[s], v)
                kn[s] = v
                for s2, v2 in mark[d][2].items():
                    if kn.get(s2, 0) < v2:
                        kn[s2] = v2
        fns = o["alt"][e][0]
        for f in fns:
            ins = f()
            if f is fns[-1] or o["inc"] == 16:
                if sem != "sent":
                    ins.then_inc(T.sem[sem], o["inc"])
                total[sem] = total.get(sem, 0) + o["inc"]
        mark[i] = (sem, total[sem], dict(kn))
    for s in sorted(total):
        if known["S"].get(s, 0) < total[s]:
            g.sync.wait_ge(T.sem[s], total[s])


def rank_program(g, core, T, topo):
    if T.rank_of(core) is None:
        return
    ops, plan = choose(g, T, topo, core)
    emit(g, T, ops, plan)
